import numpy as np, ml_dtypes
CORES = [40,41,42,43,44,45,46,47]
N = 8
BF = ml_dtypes.bfloat16
def gentries(a):
    return np.ascontiguousarray(a.reshape(8, 16, -1).transpose(0, 2, 1)).reshape(8, -1)
def gtable(e):
    e = np.asarray(e); return np.ascontiguousarray(e.reshape(8, -1, 16).transpose(0, 2, 1)).reshape(128, -1).astype(np.int32)
V, M, KK, RO, S, TH = 1024, 256, 1024, 6, 3, 12
W = V + M * RO
def parts(rng):
    c = rng.integers(-60, 61, (N, 8, 8, V)); s = rng.integers(5, 36, (N, 8, 8, V))
    x = np.stack([c + s, s - c], axis=3).reshape(N, 8, 16, V)
    nb = rng.integers(0, V, (N, 8, 16, V))
    sh = (N, 8, 8, KK // 2); cut = rng.random(sh) < 0.25; h = rng.integers(-60, 61, sh); big = rng.integers(60, 128, (4,) + sh)
    k0 = np.stack([np.where(cut, h, big[0]), big[1]], axis=3).reshape(N, 8, 16, KK // 2)
    k1 = np.stack([big[2], np.where(cut, -h, big[3])], axis=3).reshape(N, 8, 16, KK // 2)
    k = np.stack([k0, k1], axis=-1).reshape(N, 8, 16, KK)
    z = rng.integers(-127, 128, (N, 8, 16, M)); p = rng.integers(0, V, (N, 8, M))
    p = np.where(rng.random(p.shape) < 0.15, p[..., ::-1], p)
    return x, nb, k, z, p, rng.integers(-127, 128, (N, 8, 16))
def distinct(rng):
    return np.argsort(rng.random((8, V)), axis=1)[:, :M]
def pack(x, nb, k, z, p, w):
    b = lambda a: np.ascontiguousarray(a.reshape(N, 128, -1)).astype(np.float32).astype(BF)
    return {"xc": b(x), "nb": np.ascontiguousarray(nb.reshape(N, 128, V)).astype(np.int32), "kc": b(k), "zi": b(z),
            "ps": np.stack([gtable(a) for a in p]), "wt": np.ascontiguousarray(w.reshape(N, 128, 1)).astype(np.int32)}
def setup_inputs(rng):
    return pack(*parts(rng))
def setup_inputs_spread(rng):
    x, nb, k, z, p, w = parts(rng)
    x = 127 - np.floor(255 * rng.random(x.shape) * rng.random((N, 8, 1, V)) ** rng.integers(0, 3, (N, 8, 1, V))).astype(np.int64)
    k = 127 - np.floor(255 * rng.random(k.shape) * rng.random((N, 8, 1, KK)) ** rng.integers(1, 4, (N, 8, 1, KK))).astype(np.int64)
    z = np.rint(z * rng.random((N, 8, 1, M)) ** 2).astype(np.int64); w = np.rint(w * rng.random((N, 8, 16)) ** 2).astype(np.int64)
    p[:, ::2] = np.floor(V * rng.random((N, 4, M)) ** 3).astype(np.int64)
    return pack(x, nb, k, z, np.minimum(p, V - 1), w)
def setup_inputs_ends(rng):
    x, nb, k, z, p, w = parts(rng)
    sg = lambda sh: np.where(rng.random(sh) < 0.5, 127, -127)
    def recs(n, a, b):
        h = rng.random((N, 8, 1, n)); return np.where(h < a, 127, np.where(h < b, -127, sg((N, 8, 16, n))))
    x = recs(V, 0.35, 0.5); k = recs(KK, 0.5, 0.6); w = sg((N, 8, 16)); z = sg((N, 8, 16, M))
    x[..., V - 1] = 127; x[..., V - 2] = 127; x[:, ::2, :, 0] = 127; x[:, 1::2, :, 0] = -127
    for i in (1, M - 1): z[..., i] = w
    for i in (0, M - 2): z[..., i] = -w
    for u in ((16 * 127 * 127) & (KK - 1), (-16 * 127 * 127) & (KK - 1)): k[..., u] = 127; k[..., u ^ 1] = -127
    e = np.where(rng.random(nb.shape) < 0.5, 0, V - 1); nb = np.where(rng.random((N, 8, 1, V)) < 0.72, e, nb)
    nb[..., 0] = np.where(np.arange(16) % 3 == 0, 0, V - 1); nb[..., V - 1] = np.where(np.arange(16) % 4 == 3, V - 1, 0); nb[..., V - 2] = np.where(np.arange(16) % 2 == 0, 0, V - 1)
    p = np.where(rng.random(p.shape) < 0.93, np.where(rng.random(p.shape) < 0.5, 0, V - 1), p); p[..., M - 1] = V - 2
    d = np.argsort(rng.random((8, V - 2)), axis=1)[:, :M] + 1; d[::2, 0] = V - 1; d[::2, M - 1] = 0; d[1::2, 0] = 0; d[1::2, M - 1] = V - 1
    p[N - 1] = d
    return pack(x, nb, k, z, p, w)
def setup_inputs_corners(rng):
    x, nb, k, z, p, w = parts(rng); v = np.arange(V); i = np.arange(M)
    for r in range(N):
        for g in range(8):
            m = (g + r) % 8; o = (3 * g + r) % 8
            if m == 0: nb[r, g] = v
            elif m == 1: nb[r, g] = (v + 1) & (V - 1)
            elif m == 2: nb[r, g] = 0
            elif m == 3: nb[r, g] = V - 1
            elif m == 4: nb[r, g, ::2] = v; nb[r, g, 1::4] = 0; nb[r, g, 3::4] = V - 1
            elif m == 5: nb[r, g] = (v - 1) & (V - 1)
            elif m == 6: nb[r, g] = int(rng.integers(0, V))
            if o < 7: p[r, g] = ((V - 1 + i // 2) & (V - 1), 0 * i + V - 1, 0 * i, i, V - M + i, i // 16, V - 1 - i)[o]
    h = rng.random((N, 8, 1, V)); x = np.where(h < 0.05, -127, np.where(h < 0.1, 127, np.where(h < 0.15, 0, x)))
    h = rng.random((N, 8, 1, KK)); k = np.where(h < 0.1, -127, np.where(h < 0.3, 127, k))
    z[:, 0] = 0; z[:, 3] = 0; z[:, 5] = np.where(rng.random((N, 16, M)) < 0.5, 127, -127); w[:, 2] = 0; w[:, 6] = 127
    return pack(x, nb, k, z, p, w)
def setup_inputs_crowd(rng):
    x, nb, k, z, p, w = parts(rng)
    for r in range(N):
        d = distinct(rng)
        for g in range(8):
            one = (0, V - 1, int(rng.integers(0, V)))[int(rng.integers(0, 3))]
            m = 0 if r == 0 else 3 if r in (1, 3) else (g + r) % 4
            if m == 3: p[r, g] = d[g]
            elif m == 2: p[r, g] = rng.choice(np.array([one, (one + 1) & (V - 1), (one + 7) & (V - 1)]), M)
            else:
                p[r, g] = one
                if m == 1: p[r, g, (0, M - 1)[int(rng.integers(0, 2))]] = (one + 1) & (V - 1)
    p[3, 0, M - 1] = p[3, 0, 0]
    few = rng.integers(0, V, (N, 4)); few[:, 0] = 0; few[:, 1] = V - 1
    for r in range(N):
        for g in (1, 5): nb[r, g] = few[r][rng.integers(0, 4, (16, V))]
    x[:, 6] = np.where(rng.random((N, 16, V)) < 0.02, -127, 127); k[:, 6] = np.where(rng.random((N, 16, KK)) < 0.02, -127, 127)
    return pack(x, nb, k, z, p, w)
def setup_inputs_ties(rng):
    x, nb, k, z, p, w = parts(rng)
    h = rng.random(x.shape); x = np.where(h < 0.2, -1, np.where(h < 0.5, 0, 1))
    h = rng.random(k.shape); k = np.where(h < 0.1, -1, np.where(h < 0.25, 0, np.where(h < 0.4, 1, 127)))
    nb[:, ::2, 8:] = nb[:, ::2, :8]
    return pack(x, nb, k, rng.integers(-3, 4, z.shape), p, rng.integers(-2, 3, w.shape))
def check_inputs(d):
    bad = []
    for key, lo, hi in (("xc", -127, 127), ("nb", 0, V - 1), ("kc", -127, 127), ("zi", -127, 127), ("ps", 0, V - 1), ("wt", -127, 127)):
        a = np.asarray(d[key]).astype(np.float64)
        if not (np.min(a) >= lo and np.max(a) <= hi): bad.append("range of " + key)
        elif np.any(a != np.floor(a)): bad.append("whole numbers in " + key)
    return bad
def relist(child, xa, xb, a, b, other):
    c = child[:, np.arange(16) ^ 1][:, :, None, :]
    oa = np.add.reduce(xa + c >= 0, axis=1, dtype=np.int32); ob = np.add.reduce(xb + c >= 0, axis=1, dtype=np.int32)
    s = np.maximum(oa, ob)
    return np.where(s < TH, other[:, None, :], np.where(ob > oa, b, a)), s
def reference(xc, nb, kc, zi, ps, wt):
    whole = lambda a: a.astype(np.float32).astype(np.int32).reshape(N, 8, 16, -1)
    X = np.zeros((N, 8, 16, W), np.int32); X[..., :V] = whole(xc)
    L = np.zeros((N, 8, 16, W), np.int64); L[..., :V] = nb.reshape(N, 8, 16, V)
    sib = np.tile(np.arange(W), (N, 8, 1)); K = whole(kc); w = wt.astype(np.int64).reshape(N, 8, 16, 1)
    z = whole(zi); p = np.stack([gentries(a) for a in ps]).astype(np.int64); A = np.zeros(N, np.int64)
    before = np.arange(M)[:, None] > np.arange(M)[None, :]
    for t in range(RO):
        n = V + M * t + np.arange(M)
        for r in range(N):
            q = (r + S * t) % N; pp = p[r]; zz = z[r]
            act = ~np.any((pp[:, :, None] == pp[:, None, :]) & before, axis=2)
            u = (np.add.reduce(w[q] * zz, axis=1) + A[q]) & (KK - 1)
            xp = np.take_along_axis(X[q], pp[:, None, :], 2)
            C = np.minimum(xp, np.take_along_axis(K[q], u[:, None, :], 2)); E = np.minimum(xp, np.take_along_axis(K[q], (u ^ 1)[:, None, :], 2))
            a = np.take_along_axis(L[q], pp[:, None, :], 2)
            for g in range(8):
                m = act[g]; X[q, g][:, pp[g, m]] = C[g][:, m]; X[q, g][:, n[m]] = E[g][:, m]; sib[q, g][pp[g, m]] = n[m]
            b = np.take_along_axis(sib[q], a.reshape(8, 16 * M), 1).reshape(8, 16, M)
            xa = np.take_along_axis(X[q], a.reshape(8, 1, 16 * M), 2).reshape(8, 16, 16, M)
            xb = np.take_along_axis(X[q], b.reshape(8, 1, 16 * M), 2).reshape(8, 16, 16, M)
            lc, sc = relist(C, xa, xb, a, b, np.tile(n, (8, 1))); le, se = relist(E, xa, xb, a, b, pp)
            for g in range(8):
                m = act[g]; L[q, g][:, pp[g, m]] = lc[g][:, m]; L[q, g][:, n[m]] = le[g][:, m]
            A[q] = np.sum(act)
            top = np.argmax(sc, axis=1)
            p[r] = np.where(act, np.take_along_axis(lc, top[:, None, :], 1)[:, 0], (pp + 1) & (V - 1))
            z[r] = np.where(act[:, None, :], (zz + C) >> 1, zz)
    return {"yx": X.reshape(N, 128, W).astype(np.float32).astype(BF), "yn": L.reshape(N, 128, W).astype(np.float32)}

@@ -1,0 +1,837 @@
+from concourse.mybir import AluOpType, AxisListType, ActivationFunctionType
+
+ALU = AluOpType
+AF = ActivationFunctionType
+V0, M, RO, STEP, NR = 1024, 256, 6, 3, 8
+W = V0 + M * RO
+WD = W + M
+UNIT = float(2 ** 19)
+BIG = float(2 ** 22)
+M23, M24, M35, M36 = 1.5 * 2 ** 23, 1.5 * 2 ** 24, 1.5 * 2 ** 35, 1.5 * 2 ** 36
+NV, NA = 28, 16
+F32, BF, I32, U16 = "float32", "bfloat16", "int32", "uint16"
+
+CFG = {
+    "scalar": [{(1, 1, h, q) for h in range(2) for q in range(4)} | {(1, 0, 1, q) for q in range(4)},
+               {(1, 0, h, q) for h in range(2) for q in range(4)} | {(1, 1, 0, q) for q in range(4)}],
+    "gather": [(0, 0, 64, "a"), (0, 64, 128, "v"), (0, 128, 192, "a"), (0, 192, 256, "a"),
+               (1, 0, 64, "a"), (1, 64, 128, "a"), (1, 128, 192, "a"), (1, 192, 256, "a")],
+    "RE": "a", "RU": "a", "entC": "v", "boost": {}, "xa": 0, "passes": 6, "tries": 1300, "seed": 7, "look": 300.0,
+    "lvl": {"in": 10, "a": 20, "key": 24, "z": 22, "x": 60, "g": 20, "sib": 21, "c": 25, "u": 23, "out": 26, "lc": 29, "e": 30, "ev": 28, "le": 111},
+    "frac": 0.5, "eorder": [(0, 0), (0, 1), (1, 0), (1, 1)],
+}
+PB = False
+C = {"cyc": 0.83, "pcyc": 0.42, "g": 1.56, "s": 3.8, "v": 55.0, "a": 120.0, "p": 12.0, "hop": 90.0, "flight": 2200.0, "dma": 2200.0}
+
+SB = {
+    "nbs": (1024, I32), "KK": (2048, BF), "zis": (256, BF), "pss": (16, I32), "wts": (4, I32),
+    "P": (WD, BF), "L": (WD, F32), "Xo": (W, BF), "xs": (1024, BF), "x2": (1024, BF), "vr": (1024, F32), "R0": (1024, F32), "R00": (1024, F32),
+    "b0": (1024, BF), "Tri": (128, BF), "Tr1": (128, F32), "Tr2": (128, F32), "D11": (128, F32), "Ip": (128, BF), "pw3": (32, F32),
+    "Ru": (512, F32), "bit": (512, BF), "xh": (256, F32),
+    "pci": (4, I32), "tmi": (4, I32), "cols": (16, F32), "ci": (16, I32), "cidx": (16, U16), "rr16": (16, U16),
+    "jrow": (256, F32), "grow": (128, F32), "mrow": (256, F32), "maskM": (256, F32),
+    "If": (128, F32), "NIf": (128, F32), "Ib": (128, BF), "Ih": (128, BF), "NP": (128, BF), "Pm": (128, BF),
+    "blk8": (8, F32), "W19": (8, BF), "W18": (8, BF), "pickw": (8, BF), "pickb": (8, BF),
+    "Boff": (128, BF), "Bdia": (128, BF), "pw2": (16, F32), "hf16": (16, F32), "zr16": (16, F32), "pt16": (16, F32), "thrc": (256, F32),
+    "Sel": (2048, BF), "Wm": (2048, BF), "onb": (128, BF), "onf": (128, F32), "zb": (128, BF), "mh": (256, BF),
+    "ki": (2048, BF), "rst": (512, BF), "ncol": (16, F32), "dmw": (16, F32),
+    "Z0": (256, BF), "pT0": (16, F32),
+    "bm": (256, F32), "bc0": (256, F32), "bc1": (256, F32), "pwf": (16, F32), "pw16": (16, U16), "pr16": (256, U16),
+    "act0": (256, BF), "act1": (256, BF), "xg": (256, F32), "xp": (256, BF), "KU": (512, BF),
+    "CE0": (512, BF), "CE1": (512, BF), "Em": (256, BF),
+    "so1": (16, F32), "so0": (16, U16), "soo": (16, U16),
+    "a16": (256, U16), "aF": (256, F32), "b16": (256, U16), "Rb": (256, F32), "bT": (256, F32),
+    "wsc": (512, F32), "px1": (16, F32), "px2": (16, F32), "px3": (16, F32), "R1": (256, F32), "ia": (512 * NA, BF),
+    "al1": (16, I32), "al2": (16, I32), "t3": (16, F32), "kyo": (16, F32),
+    "ui": (16, I32), "um": (16, I32), "u16": (32, U16), "dm": (256, BF),
+    "m1C": (256, F32), "m2C": (256, F32), "RC": (256, I32), "entC": (256, I32), "jb": (256, BF), "D11b": (128, BF), "Dt": (128 * RO, BF), "on2": (256, BF),
+    "m1E": (256, F32), "m2E": (256, F32), "RE": (256, F32),
+    "sp": (16 * (RO - 1), F32), "sz": (256 * (RO - 1), BF), "lp": (16 * (RO - 1), F32), "lz": (256 * (RO - 1), BF),
+}
+SHAPES = {n: [128, c] for n, (c, d) in SB.items()}
+SCRATCH = {n: ("sbuf", [128, c], d) for n, (c, d) in SB.items()}
+for _n, _s, _d in [("Ga", [128, 4096], BF), ("Gb", [128, 4096], BF), ("NT", [128, 512], BF), ("iv", [128, 128 * NV, 4], BF),
+                   ("eq", [128, 16, 272], BF)]:
+    SHAPES[_n] = _s
+    SCRATCH[_n] = ("sbuf", _s, _d)
+PS = {"TC0": [128, 128, 4], "TC1": [128, 128, 4], "KA": [128, 512], "KC": [128, 512], "KE": [128, 512], "S0": [128, 512], "S1": [128, 512]}
+PS.update({"TB": [128, 256, 4]} if PB else {"S2": [128, 512]})
+for _n, _s in PS.items():
+    SHAPES[_n] = _s
+    SCRATCH[_n] = ("psum", _s, BF if _n == "TB" else F32)
+DT = {n: v[2] for n, v in SCRATCH.items()}
+LOADS = ["ps", "zi", "wt", "kc", "nb", "xc"]
+STORES = ["x0", "x1", "n0", "n1", "n2"]
+SEMAPHORES = ["sv", "sa", "st", "sg"] + ["ld" + n for n in LOADS] + ["st" + n for n in STORES] \
+    + ["ap%d" % t for t in range(RO - 1)] + ["az%d" % t for t in range(RO - 1)] + ["lo%d" % t for t in range(2 * RO - 2)]
+ESEM = {"v": "sv", "a": "sa", "p": "st", "g": "sg"}
+
+
+def R(name, a=None, b=None, step=1, p=None):
+    n = SHAPES[name][1] * (SHAPES[name][2] if len(SHAPES[name]) == 3 else 1)
+    a = 0 if a is None else a
+    b = n if b is None else b
+    ps = slice(None) if p is None else slice(p[0], p[1])
+    if len(SHAPES[name]) == 3:
+        q = SHAPES[name][2]
+        return (name, (ps, slice(a // q, b // q), slice(None)), a, b, b - a, None)
+    return (name, (ps, slice(a, b, step)), a, b, len(range(a, b, step)), None)
+
+
+def R3(name, i0, i1, k0, k1=None):
+    q = SHAPES[name][2]
+    kk = k0 if k1 is None else slice(k0, k1)
+    return (name, (slice(None), slice(i0, i1), kk), i0 * q, i1 * q, (i1 - i0) * (1 if k1 is None else k1 - k0), None)
+
+
+def EQ(c, a, b):
+    return ("eq", (slice(None), c, slice(a, b)), 272 * c + a, 272 * c + b, b - a, None)
+
+
+def IND(win, off):
+    return (win[0], win[1], win[2], win[3], 16 * off[4], off)
+
+
+def ap(T, r):
+    if not isinstance(r, tuple):
+        return r
+    x = T[r[0]][r[1]]
+    return x if r[5] is None else x.indirect(ap(T, r[5]))
+
+
+def build():
+    ops = []
+    cyc = C["cyc"]
+    lvl = [0]
+
+    def at(t, name):
+        lvl[0] = 100 * t + CFG["lvl"][name]
+
+    def add(eng, kind, args, outs, ins, cost, **kw):
+        rd = []
+        for r in ins:
+            if isinstance(r, tuple):
+                rd.append(r)
+                if r[5] is not None:
+                    rd.append(r[5])
+        for r in outs:
+            if r[5] is not None:
+                rd.append(r[5])
+        o = dict(eng=eng, kind=kind, args=args, w=list(outs), r=rd, cost=cost, n=len(ops), lvl=lvl[0], **kw)
+        ops.append(o)
+        return o
+
+    def two(*rs):
+        return all(DT[r[0]] in (BF, U16) for r in rs)
+
+    def vcost(out, ins, tt=False):
+        n = ins[0][4]
+        if out[5] is not None:
+            return 50 + n * C["s"] * cyc
+        if ins[0][5] is not None:
+            return 50 + n * C["g"] * cyc
+        c = 0.5 if two(out, *ins) else 1.0
+        if tt and not any(r[0] in PS for r in ins):
+            c *= 2
+        return C["v"] + n * c * cyc
+
+    def cp(out, a):
+        return add("v", "cp", (out, a), [out], [a], vcost(out, [a]))
+
+    def tt(out, a, b, op):
+        return add("v", "tt", (out, a, b, op), [out], [a, b], vcost(out, [a, b], True))
+
+    def ts(out, a, s1, s2, o0, o1=None):
+        return add("v", "ts", (out, a, s1, s2, o0, o1), [out], [a, s1, s2], vcost(out, [a]))
+
+    def ms(out, val):
+        return add("v", "ms", (out, val), [out], [], C["v"] + out[4] * cyc * (0.5 if two(out) else 1))
+
+    def scan(out, a, b, init, o0, o1):
+        return add("v", "scan", (out, a, b, init, o0, o1), [out], [a, b], C["v"] + a[4] * cyc)
+
+    def red(out, a):
+        return add("v", "red", (out, a), [out], [a], C["v"] + a[4] * cyc)
+
+    def act(out, a, f, bias=0.0, scale=1.0):
+        c = 65 + a[4] * C["g"] * cyc if a[5] is not None else C["a"] + a[4] * cyc
+        return add("a", "act", (out, a, f, bias, scale), [out], [a, bias, scale], c)
+
+    def mm(out, l, r, start=True, stop=True, grp=None):
+        c = max(min(64, l[4]), r[4]) * C["pcyc"] * (4 if DT[l[0]] == F32 else 1) + C["p"]
+        return add("p", "mm", (out, l, r, start, stop), [out], [l, r], c, grp=grp)
+
+    def iota(out, pat, base, cm):
+        return add("g", "iota", (out, pat, base, cm), [out], [], 130 + 2 * out[4] * cyc)
+
+    def dma(q, sem, out, src, nbytes, **kw):
+        outs = [out] if out[0] in SHAPES else []
+        ins = [src] if src[0] in SHAPES else []
+        return add(q, "dma", (out, src, kw), outs, ins + (outs if kw else []), 100.0 if q != "g" else 1000.0,
+                   sem=sem, lat=C["dma"] + nbytes / 200.0)
+
+    def ext(name, a, b):
+        return (name, (slice(None), slice(a, b)), a, b, b - a, None)
+
+    def send(kind, t, src, dst, li):
+        s = add("g", "send", (kind, t, src, dst), [], [src], 300.0, sem="lo%d" % li, lat=C["flight"])
+        return add("x", "arr", (), [dst], [], 0.0, sem=("ap%d" if kind == "p" else "az%d") % t, lat=0.0, after=s)
+
+    col = lambda name, j: R(name, j, j + 1)
+    HB = lambda nm, h, o=0: R(nm, o + 128 * h, o + 128 * h + 128)
+    dma("s", "ldps", R("pss"), ext("ps", 0, 16), 8192)
+    dma("s", "ldzi", R("zis"), ext("zi", 0, 256), 65536)
+    dma("a", "ldwt", R("wts", 0, 1), ("wt", (slice(None), slice(None)), 0, 1, 1, None), 4096)
+    dma("a", "ldkc", R("KK", 0, 1024), ext("kc", 0, 1024), 262144)
+    dma("s", "ldnb", R("nbs"), ext("nb", 0, 1024), 524288)
+    iota(R("jrow"), [[1, 256]], 0, 0)
+    iota(R("pci", 0, 1), [[0, 1]], 0, 1)
+    iota(R("ci"), [[1, 16]], 0, 0)
+    for q in range(4):
+        act(R("vr", 256 * q, 256 * q + 256), R("jrow"), AF.Identity, 256.0 * q - V0)
+    iota(R("mrow"), [[0, 16], [1, 16]], 0, 0)
+    iota(R("grow"), [[1, 8], [0, 16]], 0, 0)
+    dma("s", "ldxc", R("xs"), ext("xc", 0, 1024), 262144)
+    PF, RC_, GC_, PX, WH, P2 = [col("cols", j) for j in range(6)]
+    S2 = "S1" if PB else "S2"
+    cp(PF, col("pci", 0))
+    ts(col("tmi", 0), col("pci", 0), 15, None, ALU.bitwise_and)
+    ts(col("tmi", 1), col("pci", 0), 4, None, ALU.arith_shift_right)
+    ts(col("tmi", 2), col("pci", 0), 1, None, ALU.bitwise_and)
+    cp(RC_, col("tmi", 0))
+    cp(GC_, col("tmi", 1))
+    ts(col("cols", 6), col("tmi", 2), -2.0, 1.0, ALU.mult, ALU.add)
+    tt(PX, col("cols", 6), PF, ALU.add)
+    cp(R("cidx"), R("ci"))
+    j128 = R("jrow", 0, 128)
+    ts(R("maskM"), R("mrow"), RC_, None, ALU.is_equal)
+    ts(R("blk8"), R("jrow", 0, 8), GC_, None, ALU.is_equal)
+    ts(R("If"), j128, PF, None, ALU.is_equal)
+    ms(R("Sel"), 0.0)
+    ms(R("onb"), 1.0)
+    iota(R("onf"), [[0, 128]], 1, 0)
+    ms(R("zb"), 0.0)
+    ms(R("mh"), -0.5)
+    ms(R("rst", 0, 256), 0.0)
+    ms(R("rst", 0, 256, 16), -float(2 ** 25))
+    ms(R("hf16"), 0.5)
+    ms(R("zr16"), 0.0)
+    act(R("NIf"), R("If"), AF.Identity, 0.0, -1.0)
+    act(R("Ib"), R("If"), AF.Copy)
+    act(R("Ih"), R("If"), AF.Identity, 0.0, -0.5)
+    ts(R("NP"), j128, PX, -1.0, ALU.is_equal, ALU.mult)
+    act(R("Pm"), R("NP"), AF.Identity, 0.0, -1.0)
+    ts(R("W19"), R("blk8"), UNIT, None, ALU.mult)
+    ts(R("W18"), R("blk8"), UNIT / 2, None, ALU.mult)
+    act(R("Ip"), R("If"), AF.Identity, 0.0, 0.5)
+    ts(R("pickb"), R("jrow", 0, 128, 16), PF, -2 * BIG, ALU.is_equal, ALU.mult)
+    scan(R("pw2"), R("hf16"), R("zr16"), float(2 ** 17), ALU.mult, ALU.add)
+    tt(R("pt16"), R("pw2"), R("maskM", 0, 16), ALU.mult)
+    red(col("cols", 7), R("pt16"))
+    ts(P2, col("cols", 7), 0.5, None, ALU.mult)
+    ts(R("Boff"), R("grow"), GC_, 65536.0, ALU.is_equal, ALU.mult)
+    ts(R("Bdia"), R("grow"), GC_, P2, ALU.is_equal, ALU.mult)
+    ts(R("rr16"), R("zr16"), RC_, None, ALU.add)
+    cp(R("thrc"), IND(R("pw2"), R("rr16")))
+    ms(R("pw3", 16, 32), 2.0)
+    scan(R("pw3", 0, 16), R("pw3", 16, 32), R("zr16"), 0.5, ALU.mult, ALU.add)
+    tt(R("pw3", 0, 16), R("pw3", 0, 16), R("maskM", 0, 16), ALU.mult)
+    red(col("cols", 8), R("pw3", 0, 16))
+    ts(col("cols", 9), RC_, 12.0, col("cols", 8), ALU.is_lt, ALU.mult)
+    ts(R("pickw"), R("blk8"), col("cols", 9), None, ALU.mult)
+    ts(col("cols", 10), RC_, 12.0, P2, ALU.is_lt, ALU.mult)
+    ts(R("D11"), R("If"), col("cols", 10), 1.0 / 16, ALU.mult, ALU.mult)
+    act(R("D11b"), R("D11"), AF.Copy)
+    iota(R("jb"), [[1, 256]], 0, 0)
+    iota(R("on2"), [[0, 256]], 1, 0)
+    for t in range(1, RO):
+        act(HB("Dt", t), R("D11"), AF.Identity, 0.0, 256.0 * t)
+    ts(R("Tr1"), R("mrow", 0, 128), RC_, col("cols", 8), ALU.is_gt, ALU.mult)
+    ts(R("Tr2"), R("mrow", 0, 128), 12.0, -1.0 / 32 / 65536, ALU.is_lt, ALU.mult)
+    tt(R("Tr1"), R("Tr1"), R("Tr2"), ALU.mult)
+    tt(R("Tr2"), R("thrc", 0, 128), R("Boff"), ALU.mult)
+    tt(R("Tri"), R("Tr1"), R("Tr2"), ALU.mult)
+
+    def code(bank, a, x, num):
+        n = x[4]
+        if isinstance(num, tuple):
+            mm(R(bank, a, a + n), R("D11"), num, True, False)
+        else:
+            mm(R(bank, a, a + n), R("D11b"), R("jb"), True, False)
+            if num:
+                mm(R(bank, a, a + n), HB("Dt", num), R("on2"), False, False)
+        for j in range(0, n, 256):
+            mm(R(bank, a + j, a + j + 256), R("NP"), R("mh"), False, False)
+        mm(R(bank, a, a + n), R("Tri"), x, False, True)
+
+    act(R("x2"), R("xs"), AF.Identity, 0.0, 2.0)
+    for q in range(2):
+        bk, H = ("S0", "KA")[q], lambda nm: R(nm, 512 * q, 512 * q + 512)
+        code(bk, 0, H("x2"), H("vr"))
+        act(H("R00"), R(bk), AF.Identity, M35)
+        act(H("R0"), H("R00"), AF.Identity, -M35)
+        tt(H("b0"), R(bk), H("R0"), ALU.is_lt)
+        mm(R(bk), R("Ib"), H("x2"), True, False)
+        mm(R(bk), R("Ib"), H("b0"), False, True)
+        act(H("P"), R(bk), AF.Copy)
+    ts(WH, col("wts", 0), -0.5 / 256, None, ALU.mult)
+    for gg in range(8):
+        ts(R("Sel", 16 * gg, 2048, 129), R("onb", 0, 16), col("blk8", gg), -256.0, ALU.mult, ALU.mult)
+    ts(R("Wm"), R("Sel"), WH, None, ALU.mult)
+    ts(R("pt16"), R("jrow", 0, 16), 128.0, float(V0), ALU.mult, ALU.add)
+    ts(R("ncol"), R("pt16"), PF, None, ALU.add)
+    ts(R("pt16"), R("jrow", 0, 16), 16.0, float(W), ALU.mult, ALU.add)
+    ts(R("dmw"), R("pt16"), RC_, None, ALU.add)
+    for v in range(4):
+        iota(R("ki", 512 * v, 512 * v + 512, p=(0, 64)), [[-112, 2], [0, 16], [-256, 16]], 31 * 128, 0)
+    for v in range(2):
+        for ch in range(2):
+            for s in range(2):
+                for h in range(2):
+                    b = 1024 * v + 512 * ch + 256 * s + 128 * h
+                    on = [(ch, s, h, kq) in CFG["scalar"][v] for kq in range(4)]
+                    if all(on) or not any(on):
+                        iota(R("ki", b, b + 128, p=(64, 128)), [[0, 128]], (-7 if on[0] else -23) * 4096, 0)
+                    else:
+                        for kq in range(4):
+                            iota(R("ki", b + kq, b + 128, 4, p=(64, 128)), [[0, 32]], (-7 if on[kq] else -23) * 4096, 0)
+    act(R("Z0"), R("zis"), AF.Identity, 0.0, 2.0)
+    act(R("KK", 1024, 2048, 2), R("KK", 1, 1024, 2), AF.Copy)
+    act(R("KK", 1025, 2048, 2), R("KK", 0, 1024, 2), AF.Copy)
+    cp(R("L", 0, 1024), R("nbs"))
+
+    def wrap(src):
+        tt(R("bm"), IND(src, R("cidx")), R("maskM"), ALU.mult)
+        for h in range(2):
+            mm(R("TC0", 256 + 8 * h, 264 + 8 * h), HB("bm", h), R("blk8"))
+
+    def cut_numbers(t, Z):
+        for r in range(16):
+            mm(R("S1", 384, 400), HB("Wm", r), R(Z[0], Z[2] + r, Z[3], 16), r == 0, r == 15)
+        if t == 0:
+            cp(R("ui"), R("S1", 384, 400))
+        else:
+            ts(R("ui"), R("S1", 384, 400), col("cols", 12), None, ALU.add)
+        ts(R("um"), R("ui"), V0 - 1, None, ALU.bitwise_and)
+        cp(R("u16", 0, 16), R("um"))
+        for j in range(2):
+            act(R("KU", 256 * j, 256 * j + 256), IND(R("KK", 1024 * j, 1024 * j + 1024), R("u16", 0, 16)), AF.Identity, 0.0, 2.0)
+
+    wrap(R("pss"))
+    cp(R("pT0"), R("TC0", 256, 272))
+    cut_numbers(0, R("Z0"))
+    slot = {"v": 0, "a": 0, "s": 0}
+
+    for t in range(RO):
+        last = t == RO - 1
+        SC = CFG["scalar"][1 if last else 0]
+        pT = R("pT0") if t == 0 else R("lp", 16 * (t - 1), 16 * t)
+        Z = R("Z0") if t == 0 else R("lz", 256 * (t - 1), 256 * t)
+        bc, ac, CE, so, nf = "bc%d" % (t % 2), "act%d" % (t % 2), "CE%d" % (t % 2), ("so0", "soo")[t % 2], "nfr%d" % (t % 2)
+        n0 = V0 + M * t
+        at(t, "in")
+        wrap(pT)
+        act(R(bc), IND(pT, R("cidx")), AF.Copy)
+        for h in range(2):
+            mm(HB("TC0", h), HB(bc, h), R("If"))
+        cp(R("pw16"), R("TC0", 256, 272))
+        cp(R("pwf"), R("TC0", 256, 272))
+        cp(R("pr16"), R("TC0", 0, 256))
+        mm(R("TC1", 0, 256), R("zb"), R("mh"), True, False, grp=("d", t))
+        for c in range(16):
+            ts(EQ(c, 0, 256 - 16 * c), R("pr16", 16 * c, 256), col("pwf", c), None, ALU.is_equal)
+            if c < 15:
+                mm(R("TC1", 16 * c + 16, 256), R("Boff"), EQ(c, 16, 256 - 16 * c), False, False, grp=("d", t))
+        mm(R("TC1", 0, 256), R("Bdia"), R3("eq", 0, 16, 0, 16), False, False, grp=("d", t))
+        tt(R(ac), R("TC1", 0, 256), R("thrc"), ALU.is_lt)
+        act(R("xg"), IND(R("P", 0, n0), R("pw16")), AF.Identity, -0.5)
+        act(R("xh"), R("xg"), AF.Identity, M24)
+        act(R("xp"), R("xh"), AF.Identity, -M24)
+        tt(R(CE, 0, 256), R("xp"), R("KU", 0, 256), ALU.min)
+        tt(R(CE, 256, 512), R("xp"), R("KU", 256, 512), ALU.min)
+        code("S1", 0, R(CE, 0, 256), t)
+        if CFG["RU"] == "a":
+            act(R("xh"), R("S1", 0, 256), AF.Identity, M35)
+            act(R("Ru", 0, 256), R("xh"), AF.Identity, -M35)
+        else:
+            ts(R("Ru", 0, 256), R("S1", 0, 256), M35, -M35, ALU.add, ALU.add)
+        tt(R("bit", 0, 256), R("S1", 0, 256), R("Ru", 0, 256), ALU.is_lt)
+        aw = R3("TC0", 0, 16, 0)
+        mm(aw, R("If"), R("dmw"), True, False)
+        for r in range(16):
+            mm(aw, HB("Sel", r), R(ac, r, 256, 16), False, r == 15)
+        if not last:
+            for h in range(2):
+                mm(R3("TC0", 8 * h, 8 * h + 8, 1), HB(ac, h), R("pickb"))
+        tt(R("Em"), R(CE, 256, 512), R(ac), ALU.mult)
+        code("TC1", 256, R("Em"), t)
+        ts(R("Ru", 256, 512), R("TC1", 256, 512), M35, -M35, ALU.add, ALU.add)
+        tt(R("bit", 256, 512), R("TC1", 256, 512), R("Ru", 256, 512), ALU.is_lt)
+        tt(R("so1"), aw, R("pwf"), ALU.max)
+        cp(R(so), R("so1"))
+        tt(IND(R("P"), R(so)), R(CE, 0, 256), R("bit", 0, 256), ALU.add)
+        tt(R("P", n0, n0 + M), R("Em"), R("bit", 256, 512), ALU.add)
+        at(t, "a")
+        cp(R("a16"), IND(R("L", 0, n0) if t else R("nbs"), R("pw16")))
+        act(R("aF"), IND(R("L", 0, n0), R("pw16")), AF.Copy)
+        at(t, "key")
+        if not last:
+            red(col("cols", 11), aw)
+            ts(R("al1"), pT, 1.0 + BIG, None, ALU.add)
+            ts(R("al2"), R("al1"), int(BIG) + V0 - 1, None, ALU.bitwise_and)
+            tt(R("kyo"), R3("TC0", 0, 16, 1), R("al2"), ALU.add)
+        KB = (("KA", "KC"), ("KE", "KE"))
+        held = {}
+
+        def thresholds(ch, s, h):
+            if PB:
+                if held.get(("TB", h)) != ch:
+                    held[("TB", h)] = ch
+                    for kk in range(4):
+                        o, x = R3("TB", 128 * h, 128 * h + 128, kk), HB("NT", h, 256 * ch)
+                        add("p", "tr", (o, x, R("Ib")), [o], [x, R("Ib")], 128 * C["pcyc"] + C["p"], grp=None)
+                return R3("TB", 128 * h, 128 * h + 128, 0, 4)
+            bk = "TC1" if ch and not last else ("TC0", "TC1")[h]
+            if held.get(bk) != (ch, h):
+                held[bk] = (ch, h)
+                for kk in range(4):
+                    mm(R3(bk, 0, 128, kk), R("NP"), HB(CE, h, 256 * ch))
+            return R(bk)
+
+        if PB:
+            for j in range(4):
+                mm(HB("S1", j), HB(CE, j), R("NP"))
+            act(R("NT"), R("S1"), AF.Copy)
+            thresholds(0, 1, 0)
+            thresholds(0, 1, 1)
+        for ch in range(2):
+            b = 1024 * last + 512 * ch
+            if ch:
+                mm(R("KE"), R("onb"), R("ki", b, b + 512), True, False, grp=("KE", t))
+            else:
+                mm(R("KA", 0, 256), R("onb"), R("ki", b, b + 256), True, False, grp=("KA", t))
+                mm(R("KC", 256, 512), R("onb"), R("ki", b + 256, b + 512), True, False, grp=("KC", t))
+            for h in range(2):
+                mm(HB(KB[ch][0], h), HB("aF", h), R("If"), False, False, grp=(KB[ch][0], t))
+        at(t, "x" if last else "z")
+        if not last:
+            mm(col("S1", 400), R("onf"), col("cols", 11))
+            ts(col("cols", 12), col("S1", 400), -1.0 / 4096, 8 * (M * W + M * (M - 1) // 2) / 4096.0, ALU.mult, ALU.add)
+            mm(R("S1", 0, 256), R("Ip"), R(CE, 0, 256), True, False)
+            mm(R("S1", 0, 256), R("Ih"), Z, False, True)
+            tt(R("dm"), R("S1", 0, 256), R(ac), ALU.mult)
+            mm(R("S1", 0, 256), R("Ib"), Z, True, False)
+            mm(R("S1", 0, 256), R("Ib"), R("mh"), False, False)
+            mm(R("S1", 0, 256), R("Ib"), R("dm"), False, True)
+            ts(R("sz", 256 * t, 256 * t + 256), R("S1", 0, 256), M24, -M24, ALU.add, ALU.add)
+            send("z", t, R("sz", 256 * t, 256 * t + 256), R("lz", 256 * t, 256 * t + 256), 2 * t)
+        else:
+            for q, (a, b) in enumerate(((0, 1024), (1024, W))):
+                for a1 in range(a, b, 512):
+                    mm(R("S1"), R("Ip"), R("P", a1, a1 + 512), True, False)
+                    for j in range(2):
+                        mm(R("S1", 256 * j, 256 * j + 256), R("Ip"), R("mh"), False, j == 1)
+                    if a1 // 512 < CFG["xa"]:
+                        act(R("R00", 0, 512), R("S1"), AF.Identity, M23)
+                        act(R("Xo", a1, a1 + 512), R("R00", 0, 512), AF.Identity, -M23)
+                    else:
+                        ts(R("Xo", a1, a1 + 512), R("S1"), M23, -M23, ALU.add, ALU.add)
+                dma("s", "stx%d" % q, ext("yx", a, b), R("Xo", a, b), 128 * 2 * (b - a))
+
+        def gather(s, h):
+            at(t, "g")
+            for s1, i0, i1, q in CFG["gather"]:
+                if s1 == s and i0 // 128 == h:
+                    o = R(("Ga", "Gb")[s], 16 * i0, 16 * i1)
+                    src = IND(R("P", 0, n0 + M), R(("a16", "b16")[s], i0, i1))
+                    if q == "v":
+                        cp(o, src)
+                    else:
+                        act(o, src, AF.Copy)
+
+        def siblings(h):
+            at(t, "sib")
+            S = ("S0", "S0" if PB else "S2")[h]
+            for k in range(16):
+                mm(R(S, k, 128, 16), R("Ga", 2048 * h + k, 2048 * h + 2048, 16), R("pickw"))
+            ts(HB("Rb", h), HB(S, 0), M35, -M35, ALU.add, ALU.add)
+            tt(HB("bT", h), HB(S, 0), HB("Rb", h), ALU.subtract)
+            mm(HB(S, 1), HB("bT", h), R("If"))
+            ts(HB("b16", h), HB(S, 1), float(V0), None, ALU.add)
+            for ch in range(2):
+                mm(HB(KB[ch][1], h, 256), R("If"), HB("bT", h), False, False, grp=(KB[ch][1], t))
+
+        def tiles(ch, s, h):
+            G = ("Ga", "Gb")[s]
+            for kq in range(4):
+                at(t, ("c", "e" if (ch, s, h, kq) in SC else "ev")[ch])
+                b = 256 * s + 128 * h
+                x4 = R(G, 2048 * h + kq, 2048 * h + 2048, 4)
+                key = lambda kk: R(KB[ch][s], b + kq + 4 * kk, b + 128, 16)
+                grp = (KB[ch][s], t)
+                if (ch, s, h, kq) in SC:
+                    S = (S2, "S0", "KA")[slot["s"] % 3] if ch else (S2, "S0")[slot["s"] % 2]
+                    slot["s"] += 1
+                    j = 512 * (slot["a"] % NA)
+                    slot["a"] += 1
+                    mm(R(S), R("Ib"), x4, True, False)
+                    for kk in range(4):
+                        mm(R(S, kk, 512, 4), R("Pm"), HB(CE, h, 256 * ch), False, kk == 3)
+                    act(R("ia", j, j + 512), R(S), AF.Sign, 0.5)
+                    for kk in range(4):
+                        mm(key(kk), R("ia", j + kk, j + 512, 4), R("W18"), False, False, grp=grp)
+                else:
+                    j = 128 * (slot["v"] % NV)
+                    slot["v"] += 1
+                    tt(R3("iv", j, j + 128, 0, 4), x4, thresholds(ch, s, h), ALU.is_ge)
+                    for kk in range(4):
+                        mm(key(kk), R3("iv", j, j + 128, kk), R("W19"), False, False, grp=grp)
+
+        def lists(ch):
+            c = "CE"[ch]
+            if ch == 1:
+                tt(R("m1E"), R("KE", 0, 256), R(bc), ALU.max)
+            tt(R("m2" + c), R(KB[ch][1], 256, 512), R("m1" + c), ALU.max)
+            if ch == 0:
+                for h in range(2):
+                    mm(HB("KC", h), HB("m2C", h), R("If"))
+                cp(R("RC"), R("KC", 0, 256))
+                ts(R("entC"), R("RC"), 8191, None, ALU.bitwise_and)
+                return
+            if ch == 1 and CFG["RE"] == "a":
+                act(R("R1"), R("m2E"), AF.Identity, M36)
+                act(R("RE"), R("R1"), AF.Identity, -M36)
+            else:
+                ts(R("R" + c), R("m2" + c), M36, -M36, ALU.add, ALU.add)
+            for h in range(2):
+                mm(HB(KB[ch][1], h), HB("m2" + c, h), R("If"), True, False)
+                mm(HB(KB[ch][1], h), HB("R" + c, h), R("NIf"), False, True)
+
+        gather(0, 0)
+        gather(0, 1)
+        siblings(0)
+        tiles(0, 0, 0)
+        siblings(1)
+        tiles(0, 0, 1)
+        gather(1, 0)
+        gather(1, 1)
+        at(t, "c")
+        for h in range(2):
+            ts(HB("m1C", h), HB("KA", h), col("ncol", 2 * t + h), None, ALU.max)
+        if not last:
+            scan(R("wsc", 0, 256), R("rst", 0, 256), R("m1C"), 0.0, ALU.add, ALU.max)
+            tt(R("px1"), R("wsc", 15, 256, 16), R("kyo"), ALU.max)
+        at(t, "u")
+        if not last:
+            cut_numbers(t + 1, R("lz", 256 * t, 256 * t + 256))
+        tiles(0, 1, 0)
+        tiles(0, 1, 1)
+        at(t, "out")
+        if not last:
+            scan(R("wsc", 256, 512), R("rst", 0, 256), R("KC", 256, 512), 0.0, ALU.add, ALU.max)
+            tt(R("px2"), R("px1"), R("wsc", 271, 512, 16), ALU.max)
+            ts(R("px3"), R("px2"), M36, -M36, ALU.add, ALU.add)
+            tt(R("sp", 16 * t, 16 * t + 16), R("px2"), R("px3"), ALU.subtract)
+            send("p", t, R("sp", 16 * t, 16 * t + 16), R("lp", 16 * t, 16 * t + 16), 2 * t + 1)
+        at(t, "lc")
+        lists(0)
+        cp(IND(R("L"), R(so)), R("entC"))
+        if last:
+            dma("s", "stn0", ext("yn", 0, 1152), R("L", 0, 1152), 128 * 4 * 1152)
+            dma("s", "stn1", ext("yn", 1152, n0), R("L", 1152, n0), 128 * 4 * 1152)
+        for s, h in CFG["eorder"]:
+            tiles(1, s, h)
+        at(t, "le")
+        lists(1)
+        tt(R("L", n0, n0 + M), R("KE", 0, 256), R(ac), ALU.mult)
+        if last:
+            dma("s", "stn2", ext("yn", n0, W), R("L", n0, W), 128 * 4 * M)
+    return ops
+
+
+def depend(ops):
+    acc = {}
+    bank = {}
+    for o in ops:
+        dep, follow = set(), set()
+        if "after" in o:
+            follow.add(o["after"]["n"])
+        for rs, wr in ((o["r"], False), (o["w"], True)):
+            for r in rs:
+                if r[0] in PS:
+                    b = bank.setdefault(r[0], {"eng": None, "cur": [], "prev": []})
+                    if b["eng"] != o["eng"]:
+                        b["eng"], b["prev"], b["cur"] = o["eng"], b["cur"], []
+                    dep.update(b["prev"])
+                    if o["eng"] == "p":
+                        for m in b["cur"]:
+                            q = ops[m]
+                            if o["grp"] is None or q["grp"] != o["grp"] or q["args"][3]:
+                                follow.add(m)
+                    if o["n"] not in b["cur"]:
+                        b["cur"].append(o["n"])
+                    continue
+                keep = []
+                full = wr and r[5] is None and r[4] == r[3] - r[2] and r[1][0] == slice(None)
+                for (lo, hi, w, m) in acc.get(r[0], []):
+                    if lo < r[3] and r[2] < hi and (w or wr) and m != o["n"]:
+                        dep.add(m)
+                    if not (full and r[2] <= lo and hi <= r[3]):
+                        keep.append((lo, hi, w, m))
+                keep.append((r[2], r[3], wr, o["n"]))
+                acc[r[0]] = keep
+        dep.discard(o["n"])
+        follow.discard(o["n"])
+        o["dep"], o["follow"] = dep, follow - dep
+
+
+def schedule(ops):
+    n = len(ops)
+    hop = C["hop"]
+    succ = [[] for _ in ops]
+    for o in ops:
+        for m in o["dep"] | o["follow"]:
+            succ[m].append(o["n"])
+    rank = [0.0] * n
+    for o in reversed(ops):
+        i = o["n"]
+        rank[i] = o["cost"] + o.get("lat", 0.0) + max([rank[m] + hop for m in succ[i]] + [0.0]) \
+            + CFG["boost"].get(o["w"][0][0] if o["w"] else "", 0.0)
+    left = [len(o["dep"] | o["follow"]) for o in ops]
+    ready_at = [0.0] * n
+    free = {e: 0.0 for e in "vapgsx"}
+    pool = {e: [] for e in "vapgsx"}
+    for o in ops:
+        if left[o["n"]] == 0:
+            pool[o["eng"]].append(o["n"])
+    order = []
+    end = 0.0
+    while len(order) < n:
+        best = None
+        for e, pl in pool.items():
+            if pl:
+                t0 = max(free[e], min(ready_at[i] for i in pl))
+                if best is None or t0 < best[0]:
+                    best = (t0, e)
+        t0, e = best
+        i = max((i for i in pool[e] if ready_at[i] <= t0 + 1e-6), key=lambda i: (rank[i], -i))
+        j = max((j for j in pool[e] if ready_at[j] <= t0 + CFG["look"]), key=lambda j: (rank[j], -j))
+        if j != i and ready_at[j] - t0 < CFG["frac"] * ops[i]["cost"]:
+            i, t0 = j, ready_at[j]
+        pool[e].remove(i)
+        o = ops[i]
+        o["t0"] = t0
+        if e != "x":
+            free[e] = t0 + o["cost"]
+        done = t0 + o["cost"] + o.get("lat", 0.0)
+        end = max(end, done)
+        order.append(i)
+        for m in succ[i]:
+            same = i in ops[m]["follow"] and ops[m]["eng"] == e
+            ready_at[m] = max(ready_at[m], t0 if same else done + hop)
+            left[m] -= 1
+            if left[m] == 0:
+                pool[ops[m]["eng"]].append(m)
+    return order, end
+
+
+def place(ops, seq, before):
+    start = [0.0] * len(ops)
+    line = {e: ([], []) for e in "vapgs"}
+    for i in seq:
+        o = ops[i]
+        t = max([start[m] + d for m, d in before[i]] + [0.0])
+        if o["eng"] != "x":
+            a, b = line[o["eng"]]
+            lo, hi = 0, len(b)
+            while lo < hi:
+                mid = (lo + hi) // 2
+                if b[mid] <= t:
+                    lo = mid + 1
+                else:
+                    hi = mid
+            while lo < len(a) and a[lo] < t + o["cost"] - 1e-6:
+                t = max(t, b[lo])
+                lo += 1
+            a.insert(lo, t)
+            b.insert(lo, t + o["cost"])
+        start[i] = t
+    return start
+
+
+def improve(ops):
+    n = len(ops)
+    fwd = [[] for _ in ops]
+    bwd = [[] for _ in ops]
+    for o in ops:
+        i = o["n"]
+        for m in o["dep"] | o["follow"]:
+            q = ops[m]
+            d = q["cost"] + (0.0 if m in o["follow"] and q["eng"] == o["eng"] else q.get("lat", 0.0) + C["hop"])
+            fwd[i].append((m, d))
+            bwd[m].append((i, o["cost"] - q["cost"] + d))
+    tail = n
+    left = [len(f) for f in fwd]
+    pool = [i for i in range(n) if not left[i]]
+    seq = []
+    while pool:
+        i = min(pool, key=lambda i: (ops[i]["lvl"], i))
+        pool.remove(i)
+        seq.append(i)
+        for m, d in bwd[i]:
+            left[m] -= 1
+            if not left[m]:
+                pool.append(m)
+    start = place(ops, seq, fwd)
+    best = (max(start[i] + ops[i]["cost"] + ops[i].get("lat", 0.0) for i in range(n)), start)
+    for o in ops:
+        bwd[o["n"]].append((tail, o.get("lat", 0.0)))
+    ext = ops + [dict(eng="x", cost=0.0)]
+    finish = lambda st: max(st[i] + ops[i]["cost"] + ops[i].get("lat", 0.0) for i in range(n))
+
+    def there_and_back(st):
+        rev = place(ext, [tail] + sorted(range(n), key=lambda i: (-(st[i] + ops[i]["cost"]), -i)), bwd + [[]])
+        return place(ops, sorted(range(n), key=lambda i: (-(rev[i] + ops[i]["cost"]), i)), fwd)
+
+    for _ in range(CFG["passes"]):
+        start = there_and_back(start)
+        if finish(start) < best[0]:
+            best = (finish(start), start)
+    kinds = {}
+    for o in ops:
+        kinds.setdefault((o["lvl"] % 100, o["eng"], o["w"][0][0][:2] if o["w"] else ""), []).append(o["n"])
+    names = sorted(kinds)
+    x = CFG["seed"]
+    for it in range(CFG["tries"]):
+        x = (x * 1103515245 + 12345) % 2 ** 31
+        key = list(best[1])
+        shift = (-4000.0, -2000.0, -900.0, -400.0, 400.0, 900.0, 2000.0, 4000.0)[(x >> 8) % 8]
+        members = kinds[names[(x >> 12) % len(names)]]
+        for i in members[(x >> 24) % 2::1 + (x >> 25) % 2]:
+            key[i] += shift
+        for i in range(n):
+            for m, d in fwd[i]:
+                if key[m] >= key[i]:
+                    key[i] = key[m] + 1e-3
+        start = place(ops, sorted(range(n), key=lambda i: key[i]), fwd)
+        if (x >> 20) % 4 == 0:
+            start = there_and_back(start)
+        if finish(start) < best[0]:
+            best = (finish(start), start)
+    end, start = best
+    for o in ops:
+        o["t0"] = start[o["n"]]
+    return sorted(range(n), key=lambda i: (start[i], i)), end
+
+
+def plan():
+    ops = build()
+    depend(ops)
+    order, end = improve(ops)
+    lastg = {}
+    for i in order:
+        if ops[i].get("grp") is not None:
+            lastg[ops[i]["grp"]] = i
+    for i in lastg.values():
+        ops[i]["args"] = ops[i]["args"][:4] + (True,)
+    pos, cnt, known = {}, {}, {e: {} for e in "vapgsx"}
+    for i in order:
+        o = ops[i]
+        e = o["eng"]
+        kn = known[e]
+        need = {}
+        if o["kind"] == "iota":
+            if lastg.get("g") is not None:
+                o["dep"].add(lastg["g"])
+            lastg["g"] = i
+        for m in o["dep"]:
+            src, p = pos[m]
+            if kn.get(src, 0) < p and need.get(src, (0, 0))[0] < p:
+                need[src] = (p, m)
+        waits = []
+        for src, (p, m) in sorted(need.items(), key=lambda kv: -ops[kv[1][1]]["t0"]):
+            if kn.get(src, 0) >= p:
+                continue
+            waits.append(m)
+            ops[m]["mark"] = True
+            for s2, p2 in ops[m]["clock"].items():
+                if kn.get(s2, 0) < p2:
+                    kn[s2] = p2
+        o["waits"] = waits[::-1]
+        src = o.get("sem") or ESEM[e]
+        cnt[src] = cnt.get(src, 0) + 1
+        pos[i] = (src, cnt[src])
+        o["src"] = src
+        o["clock"] = dict(kn) if e != "x" else {}
+        o["clock"][src] = cnt[src]
+    val = {}
+    for i in order:
+        o = ops[i]
+        if "sem" not in o and o.get("mark"):
+            val[o["src"]] = val.get(o["src"], 0) + 1
+            o["val"] = val[o["src"]]
+    return ops, order, val, end
+
+
+PLAN = []
+
+
+def rank_program(g, core, T, topo):
+    rank = T.rank_of(core)
+    if rank is None:
+        return
+    if not PLAN:
+        PLAN.append(plan())
+    ops, order, val, _ = PLAN[0]
+    nxt = T.cores[(rank + STEP) % NR]
+    prv = T.cores[(rank - STEP) % NR]
+    rid, pid, _ = topo.addr(nxt)
+    n_out, n_in = len(topo.engines(core, nxt)), len(topo.engines(prv, core))
+    Q = {"v": g.vector, "a": g.scalar, "p": g.tensor, "g": g, "s": g.sync}
+    count = lambda o: {"dma": 16, "send": n_out, "arr": n_in}.get(o["kind"]) or o["val"]
+    for i in order:
+        o = ops[i]
+        k = o["kind"]
+        if k == "arr":
+            continue
+        q = Q[o["eng"]]
+        for m in o["waits"]:
+            q.wait_ge(T.sem[ops[m]["src"]], count(ops[m]))
+        a = [ap(T, x) for x in o["args"]]
+        if k == "cp":
+            ins = q.tensor_copy(a[0], a[1])
+        elif k == "tt":
+            ins = q.tensor_tensor(a[0], a[1], a[2], a[3])
+        elif k == "ts":
+            ins = q.tensor_scalar(a[0], a[1], a[2], None, a[4]) if a[5] is None else q.tensor_scalar(*a)
+        elif k == "ms":
+            ins = q.memset(a[0], a[1])
+        elif k == "scan":
+            ins = q.tensor_tensor_scan(*a)
+        elif k == "red":
+            ins = q.tensor_reduce(a[0], a[1], AxisListType.X, ALU.add)
+        elif k == "act":
+            ins = q.activation(a[0], a[1], a[2], bias=a[3], scale=a[4])
+        elif k == "mm":
+            ins = q.matmul(*a)
+        elif k == "tr":
+            ins = q.transpose(*a)
+        elif k == "iota":
+            if DT[o["args"][0][0]] == I32:
+                ins = q.iota(*a)
+            else:
+                ins = q.iota(a[0], a[1], a[2], a[3], allow_small_or_imprecise_dtypes=True)
+        elif k == "dma":
+            q.dma_start(a[0], a[1], **a[2]).then_inc(T.sem[o["sem"]], 16)
+            continue
+        else:
+            q.remote_dma(a[3], a[2], T.sem[("ap%d" if a[0] == "p" else "az%d") % a[1]], T.sem[o["sem"]], pid, rid, topo.mask(core, nxt))
+            continue
+        if o.get("mark"):
+            ins.then_inc(T.sem[o["src"]], 1)
+    for i in order:
+        o = ops[i]
+        if o["kind"] in ("dma", "send", "arr"):
+            g.wait_ge(T.sem[o["sem"]], count(o))
+    for s, c in val.items():
+        g.wait_ge(T.sem[s], c)

@@ -1,3 +1,4 @@
+from concourse.bass import DstId, RemoteDMATransfer
 from concourse.mybir import AluOpType, AxisListType, ActivationFunctionType
 
 ALU = AluOpType
@@ -8,57 +9,87 @@ WD = W + M
 UNIT = float(2 ** 19)
 BIG = float(2 ** 22)
 M23, M24, M35, M36 = 1.5 * 2 ** 23, 1.5 * 2 ** 24, 1.5 * 2 ** 35, 1.5 * 2 ** 36
-NV, NA = 28, 16
-F32, BF, I32, U16 = "float32", "bfloat16", "int32", "uint16"
+OFF = 1536.0
+EPS = 2.0 ** -12
+NV, NA = 24, 8
+F32, BF, F16, I32, U16 = "float32", "bfloat16", "float16", "int32", "uint16"
 
 CFG = {
-    "scalar": [{(1, 1, h, q) for h in range(2) for q in range(4)} | {(1, 0, 1, q) for q in range(4)},
-               {(1, 0, h, q) for h in range(2) for q in range(4)} | {(1, 1, 0, q) for q in range(4)}],
-    "gather": [(0, 0, 64, "a"), (0, 64, 128, "v"), (0, 128, 192, "a"), (0, 192, 256, "a"),
-               (1, 0, 64, "a"), (1, 64, 128, "a"), (1, 128, 192, "a"), (1, 192, 256, "a")],
-    "RE": "a", "RU": "a", "entC": "v", "boost": {}, "xa": 0, "passes": 6, "tries": 1300, "seed": 7, "look": 300.0,
-    "lvl": {"in": 10, "a": 20, "key": 24, "z": 22, "x": 60, "g": 20, "sib": 21, "c": 25, "u": 23, "out": 26, "lc": 29, "e": 30, "ev": 28, "le": 111},
-    "frac": 0.5, "eorder": [(0, 0), (0, 1), (1, 0), (1, 1)],
+    "scalar": [{(0, h, q) for h in range(2) for q in range(2)}, {(0, h, q) for h in range(2) for q in range(2)}],
+    "split": {(0, 1, 3)},
+    "gather": [[(0, 0, 64, "a"), (0, 64, 128, "v"), (0, 128, 192, "a"), (0, 192, 256, "a"),
+                (1, 0, 64, "a"), (1, 64, 128, "a"), (1, 128, 192, "a"), (1, 192, 224, "a"), (1, 224, 256, "a")]] * 2,
+    "TB": "aavv", "acut": (0, 3), "o16": "av", "Lw": "a", "sibs": [(0,), (1,), (2, 3)], "fuse": 0, "pr": "a", "Cb": "a", "Eb": "p", "Q": "aa", "xo": "vv", "run": 330.0, "passes": 4, "tries": 5000, "seed": 7,
+    "relu": 1,
+    "slack": 300.0, "span": 19500.0, "lead": 12000.0,
+    "when": {
+        ('pre', 'a', 'nrow'): (-3000, 0), ('pre', 'p', 'X'): (-1500, 100),
+        ('in', 'v', 'bm'): (0, 0), ('in', 'a', 'bc'): (0, 0), ('in', 'p', 'X'): (450, 300), ('in', 'p', 'X2'): (500, 0), ('in', 'v', 'pw16'): (600, 0),
+        ('in', 'v', 'pwf'): (650, 0), ('in', 'a', 'pr'): (640, 0),
+        ('eq', 'v', 'eq'): (1050, 120), ('eq', 'p', 'X'): (1900, 90), ('eq', 'v', 'sc'): (3450, 0), ('eq', 'v', 'so'): (3800, 0), ('eq', 'a', 'idle'): (4900, 0),
+        ('cd', 'a', 'xp'): (960, 0), ('cd', 'v', 'CE'): (1000, 2200), ('cd', 'p', 'X2'): (1800, 250), ('cd', 'a', 'Cb'): (3400, 0), ('cd', 'v', 'P'): (3950, 0),
+        ('ce', 'p', 'X2'): (4300, 240), ('ce', 'a', 'act'): (6300, 0), ('ce', 'v', 'P'): (6900, 0),
+        ('tb', 'p', 'K'): (3900, 0), ('tb', 'a', 'thr'): (4250, 0), ('tb', 'v', 'TBC'): (6300, 270),
+        ('te', 'p', 'KE'): (5500, 0), ('te', 'a', 'thr'): (9400, 0), ('te', 'v', 'TBE'): (12500, 270),
+        ('a', 'a', 'aF'): (1400, 0), ('a', 'v', 'aF'): (1400, 0), ('a', 'p', 'K'): (3350, 200), ('a', 'a', 'a16'): (3800, 300),
+        ('key', 'v', 'al'): (7200, 0), ('key', 'v', 'al2'): (7300, 0), ('key', 'p', 'X2'): (7000, 0), ('key', 'v', 'kyo'): (7400, 0),
+        ('key', 'v', 'cols'): (7500, 0), ('key', 'p', 'K'): (6000, 100), ('key', 'v', 'L'): (12000, 500),
+        ('ke', 'p', 'KE'): (10000, 200), ('z', 'p', 'X2'): (7600, 240), ('z', 'v', 'dm'): (8200, 0), ('z', 'g', 'send'): (8500, 0), ('z', 'x', 'lz'): (8800, 0),
+        ('g', 'a', 'Ga'): (4900, 1400), ('g', 'v', 'Ga'): (4900, 1400), ('g', 'a', 'Gb'): (9500, 1400), ('g', 'v', 'Gb'): (9000, 1400),
+        ('sib', 'p', 'X'): (6400, 350), ('sib', 'v', 'Rb'): (6800, 1400), ('sib', 'v', 'Zb'): (6900, 1400), ('sib', 'v', 'b16'): (7300, 1400),
+        ('c', 'p', 'K'): (7500, 330), ('c', 'v', 'iv'): (7600, 900),
+        ('out', 'v', 'm1C'): (14000, 500), ('out', 'v', 'm2C'): (14200, 500), ('out', 'v', 'wsc'): (14400, 500), ('out', 'v', 'px'): (15200, 0),
+        ('out', 'v', 'pq'): (15300, 0), ('out', 'v', 'sp'): (15400, 0), ('out', 'g', 'send'): (15500, 0), ('out', 'x', 'lp'): (15800, 0),
+        ('u', 'p', 'X2'): (12000, 320), ('u', 'v', 'ui'): (12800, 0), ('u', 'v', 'um'): (12900, 0), ('u', 'v', 'u16'): (13000, 0), ('u', 'a', 'KU'): (16500, 400),
+        ('lc', 'a', 'QC'): (15500, 300), ('lc', 'p', 'K'): (15800, 300), ('lc', 'a', 'entC'): (16100, 300), ('lc', 'v', 'L'): (17500, 0),
+        ('ev', 'v', 'iv'): (15600, 480), ('ev', 'p', 'KE'): (16000, 480), ('e', 'p', 'X'): (14500, 500), ('e', 'p', 'X2'): (14800, 500),
+        ('e', 'a', 'ia'): (15000, 550), ('e', 'p', 'KE'): (15600, 550),
+        ('le', 'a', 'm1E'): (18800, 0), ('le', 'v', 'm2E'): (19200, 0), ('le', 'a', 'QE'): (19500, 0), ('le', 'p', 'KE'): (19800, 250), ('le', 'a', 'L'): (20800, 0),
+    },
+    "lvl": {"pre": -60, "in": 8, "eq": 10, "cd": 9, "ce": 12, "tb": 14, "a": 13, "key": 24, "z": 22, "x": 60, "g": 20, "sib": 21, "c": 25, "u": 40,
+            "out": 26, "lc": 110, "te": 14, "ke": 28, "e": 111, "ev": 111, "le": 112},
 }
-PB = False
 C = {"cyc": 0.83, "pcyc": 0.42, "g": 1.56, "s": 3.8, "v": 55.0, "a": 120.0, "p": 12.0, "hop": 90.0, "flight": 2200.0, "dma": 2200.0}
+CW = ["p24", "m24", "p36", "m36", "p23", "m23", "q", "mk", "pk", "m2o", "pq"]
 
 SB = {
-    "nbs": (1024, I32), "KK": (2048, BF), "zis": (256, BF), "pss": (16, I32), "wts": (4, I32),
-    "P": (WD, BF), "L": (WD, F32), "Xo": (W, BF), "xs": (1024, BF), "x2": (1024, BF), "vr": (1024, F32), "R0": (1024, F32), "R00": (1024, F32),
-    "b0": (1024, BF), "Tri": (128, BF), "Tr1": (128, F32), "Tr2": (128, F32), "D11": (128, F32), "Ip": (128, BF), "pw3": (32, F32),
-    "Ru": (512, F32), "bit": (512, BF), "xh": (256, F32),
-    "pci": (4, I32), "tmi": (4, I32), "cols": (16, F32), "ci": (16, I32), "cidx": (16, U16), "rr16": (16, U16),
-    "jrow": (256, F32), "grow": (128, F32), "mrow": (256, F32), "maskM": (256, F32),
-    "If": (128, F32), "NIf": (128, F32), "Ib": (128, BF), "Ih": (128, BF), "NP": (128, BF), "Pm": (128, BF),
-    "blk8": (8, F32), "W19": (8, BF), "W18": (8, BF), "pickw": (8, BF), "pickb": (8, BF),
-    "Boff": (128, BF), "Bdia": (128, BF), "pw2": (16, F32), "hf16": (16, F32), "zr16": (16, F32), "pt16": (16, F32), "thrc": (256, F32),
-    "Sel": (2048, BF), "Wm": (2048, BF), "onb": (128, BF), "onf": (128, F32), "zb": (128, BF), "mh": (256, BF),
-    "ki": (2048, BF), "rst": (512, BF), "ncol": (16, F32), "dmw": (16, F32),
-    "Z0": (256, BF), "pT0": (16, F32),
-    "bm": (256, F32), "bc0": (256, F32), "bc1": (256, F32), "pwf": (16, F32), "pw16": (16, U16), "pr16": (256, U16),
-    "act0": (256, BF), "act1": (256, BF), "xg": (256, F32), "xp": (256, BF), "KU": (512, BF),
-    "CE0": (512, BF), "CE1": (512, BF), "Em": (256, BF),
-    "so1": (16, F32), "so0": (16, U16), "soo": (16, U16),
-    "a16": (256, U16), "aF": (256, F32), "b16": (256, U16), "Rb": (256, F32), "bT": (256, F32),
-    "wsc": (512, F32), "px1": (16, F32), "px2": (16, F32), "px3": (16, F32), "R1": (256, F32), "ia": (512 * NA, BF),
-    "al1": (16, I32), "al2": (16, I32), "t3": (16, F32), "kyo": (16, F32),
-    "ui": (16, I32), "um": (16, I32), "u16": (32, U16), "dm": (256, BF),
-    "m1C": (256, F32), "m2C": (256, F32), "RC": (256, I32), "entC": (256, I32), "jb": (256, BF), "D11b": (128, BF), "Dt": (128 * RO, BF), "on2": (256, BF),
-    "m1E": (256, F32), "m2E": (256, F32), "RE": (256, F32),
-    "sp": (16 * (RO - 1), F32), "sz": (256 * (RO - 1), BF), "lp": (16 * (RO - 1), F32), "lz": (256 * (RO - 1), BF),
+    "nbs": (1024, I32), "KK": (2048, BF), "zis": (256, BF), "pss": (16, I32), "wts": (4, I32), "xs": (1024, BF),
+    "P": (WD, BF), "L": (WD, F32), "Xo": (W, BF), "X16": (W, F16),
+    "pci": (4, I32), "tmi": (4, I32), "cols": (32, F32), "ci": (16, I32), "cidx": (16, U16),
+    "jrow": (256, BF), "grow": (128, BF), "mrow": (256, BF), "maskM": (256, BF), "nrow": (M * RO, F16),
+    "rown": (256, BF), "first": (256, BF), "half": (256, BF), "pw2": (48, F32), "I2": (128, BF), "t4": (128, BF),
+    "If": (128, F32), "NIf": (128, F32), "Ib": (128, BF), "NIb": (128, BF), "Ih": (128, BF), "NIh": (128, BF),
+    "NP2": (128, BF), "PM2": (128, BF), "blkM": (128, BF), "t1": (128, BF), "t2": (128, BF), "t3": (128, BF),
+    "tu": (128, BF), "N3": (128, BF), "N8": (128, BF), "nbias": (8, F32), "K32": (2048, F32), "QC": (256, F16), "QE": (256, F16), "N13": (128, BF), "P13": (128, BF),
+    "TriN": (128, BF), "TriP": (128, BF), "D": (128, BF), "ND": (128, BF), "C3": (128, BF), "C8": (128, BF), "C30": (128, BF), "C80": (128, BF),
+    "blk8": (8, BF), "W19": (8, BF), "pickw": (8, BF), "pickb": (8, BF), "Boff": (128, BF), "Bdia": (128, BF),
+    "Wz": (144, BF), "on5": (512, BF), "onf": (128, F32), "cw": (128 * len(CW), BF),
+    "rst": (128, BF), "ncol": (16, F32), "d0": (272, F32), "sc": (272, F32), "pT0": (16, F32),
+    "bm": (256, F16), "bc0": (256, F16), "bc1": (256, F16), "pwf": (16, F32), "pw16": (16, U16),
+    "xp": (256, F16), "KU": (512, F16), "CE0": (512, F16), "CE1": (512, F16), "Cb": (512, BF),
+    "so0": (16, U16), "so1": (16, U16), "thr": (1024, BF), "act0": (256, BF), "act1": (256, BF), "NblkM": (128, BF),
+    "a16": (256, U16), "aF": (256, F16), "b16": (256, U16), "Rb": (256, F32), "Zq": (4 * 144, BF), "Ga": (4096, BF), "Gb": (4096, BF),
+    "wsc": (256, F32), "px": (16, F32), "pq": (16, F32), "ia": (512 * NA, BF), "al1": (16, I32), "al2": (16, I32), "kyo": (16, F32),
+    "ui": (16, I32), "um": (16, I32), "u16": (16, U16),
+    "m1C": (256, F32), "m2C": (256, F32), "entC": (256, F32), "m1E": (256, F32), "m2E": (256, F32),
+    "sp": (16 * (RO - 1), F32), "dm": (256 * (RO - 1), BF), "lp": (16 * (RO - 1), F32), "lz": (256 * (RO - 1), BF),
 }
+MATS = [n for n, x in SB.items() if x == (128, BF)]
+for _n in MATS:
+    del SB[_n]
+SB["mat"] = (128 * len(MATS), BF)
 SHAPES = {n: [128, c] for n, (c, d) in SB.items()}
 SCRATCH = {n: ("sbuf", [128, c], d) for n, (c, d) in SB.items()}
-for _n, _s, _d in [("Ga", [128, 4096], BF), ("Gb", [128, 4096], BF), ("NT", [128, 512], BF), ("iv", [128, 128 * NV, 4], BF),
-                   ("eq", [128, 16, 272], BF)]:
+for _n, _s in [("iv", [128, 128 * NV, 4]), ("eq", [128, 16, 272]), ("mk", [128, 16, 17]), ("th2", [128, 16, 17]), ("ki", [128, 2, 256]),
+               ("idle", [128, 16, 17]), ("pr0", [128, 16, 17]), ("pr1", [128, 16, 17]),
+               ("Zb", [128, 260, 4]), ("I4", [128, 32, 4])]:
     SHAPES[_n] = _s
-    SCRATCH[_n] = ("sbuf", _s, _d)
-PS = {"TC0": [128, 128, 4], "TC1": [128, 128, 4], "KA": [128, 512], "KC": [128, 512], "KE": [128, 512], "S0": [128, 512], "S1": [128, 512]}
-PS.update({"TB": [128, 256, 4]} if PB else {"S2": [128, 512]})
+    SCRATCH[_n] = ("sbuf", _s, F16 if _n[:2] in ("pr", "Zb") else BF)
+PS = {"TBC": [128, 256, 4], "TBE": [128, 256, 4], "K0": [128, 128, 4], "K1": [128, 128, 4], "KE": [128, 128, 4],
+      "X0": [128, 512], "X1": [128, 512], "X2": [128, 512]}
 for _n, _s in PS.items():
     SHAPES[_n] = _s
-    SCRATCH[_n] = ("psum", _s, BF if _n == "TB" else F32)
+    SCRATCH[_n] = ("psum", _s, BF if _n[:2] == "TB" else F32)
 DT = {n: v[2] for n, v in SCRATCH.items()}
 LOADS = ["ps", "zi", "wt", "kc", "nb", "xc"]
 STORES = ["x0", "x1", "n0", "n1", "n2"]
@@ -68,6 +99,9 @@ ESEM = {"v": "sv", "a": "sa", "p": "st", "g": "sg"}
 
 
 def R(name, a=None, b=None, step=1, p=None):
+    if name in MATS:
+        j = 128 * MATS.index(name)
+        return R("mat", j + (a or 0), j + (b or 128), step, p)
     n = SHAPES[name][1] * (SHAPES[name][2] if len(SHAPES[name]) == 3 else 1)
     a = 0 if a is None else a
     b = n if b is None else b
@@ -78,10 +112,18 @@ def R(name, a=None, b=None, step=1, p=None):
     return (name, (ps, slice(a, b, step)), a, b, len(range(a, b, step)), None)
 
 
-def R3(name, i0, i1, k0, k1=None):
+def R3(name, i0, i1, k0, k1=None, p=None):
     q = SHAPES[name][2]
     kk = k0 if k1 is None else slice(k0, k1)
-    return (name, (slice(None), slice(i0, i1), kk), i0 * q, i1 * q, (i1 - i0) * (1 if k1 is None else k1 - k0), None)
+    ps = slice(None) if p is None else slice(p[0], p[1])
+    return (name, (ps, slice(i0, i1), kk), i0 * q, i1 * q, (i1 - i0) * (1 if k1 is None else k1 - k0), None)
+
+
+def RS(name, i0, i1, step, k0, k1=None, kstep=1):
+    q = SHAPES[name][2]
+    kk = k0 if k1 is None else slice(k0, k1, kstep)
+    n = len(range(i0, i1, step)) * (1 if k1 is None else len(range(k0, k1, kstep)))
+    return (name, (slice(None), slice(i0, i1, step), kk), i0 * q, i1 * q, n, None)
 
 
 def EQ(c, a, b):
@@ -102,10 +144,11 @@ def ap(T, r):
 def build():
     ops = []
     cyc = C["cyc"]
-    lvl = [0]
+    lvl = [0, (0, "start")]
 
     def at(t, name):
         lvl[0] = 100 * t + CFG["lvl"][name]
+        lvl[1] = (t, name)
 
     def add(eng, kind, args, outs, ins, cost, **kw):
         rd = []
@@ -117,12 +160,12 @@ def build():
         for r in outs:
             if r[5] is not None:
                 rd.append(r[5])
-        o = dict(eng=eng, kind=kind, args=args, w=list(outs), r=rd, cost=cost, n=len(ops), lvl=lvl[0], **kw)
+        o = dict(eng=eng, kind=kind, args=args, w=list(outs), r=rd, cost=cost, n=len(ops), lvl=lvl[0], at=lvl[1], **kw)
         ops.append(o)
         return o
 
     def two(*rs):
-        return all(DT[r[0]] in (BF, U16) for r in rs)
+        return all(DT[r[0]] in (BF, F16, U16) for r in rs)
 
     def vcost(out, ins, tt=False):
         n = ins[0][4]
@@ -148,402 +191,477 @@ def build():
         return add("v", "ms", (out, val), [out], [], C["v"] + out[4] * cyc * (0.5 if two(out) else 1))
 
     def scan(out, a, b, init, o0, o1):
-        return add("v", "scan", (out, a, b, init, o0, o1), [out], [a, b], C["v"] + a[4] * cyc)
+        return add("v", "scan", (out, a, b, init, o0, o1), [out], [a, b], vcost(out, [a, b]))
 
     def red(out, a):
         return add("v", "red", (out, a), [out], [a], C["v"] + a[4] * cyc)
 
-    def act(out, a, f, bias=0.0, scale=1.0):
+    def act(out, a, f, bias=0.0, scale=1.0, acc=None, more=0.0):
         c = 65 + a[4] * C["g"] * cyc if a[5] is not None else C["a"] + a[4] * cyc
-        return add("a", "act", (out, a, f, bias, scale), [out], [a, bias, scale], c)
+        return add("a", "act", (out, a, f, bias, scale, acc), [out] + ([acc] if acc else []), [a, bias, scale], c + more + (20 if acc else 0))
 
-    def mm(out, l, r, start=True, stop=True, grp=None):
+    def shift(q, out, a, bias, scale=1.0):
+        if q == "a":
+            return act(out, a, AF.Identity, bias, scale)
+        return ts(out, a, bias, None, ALU.add) if scale == 1.0 else ts(out, a, scale, bias, ALU.mult, ALU.add)
+
+    def mm(out, l, r, start=False, stop=False, grp=None):
         c = max(min(64, l[4]), r[4]) * C["pcyc"] * (4 if DT[l[0]] == F32 else 1) + C["p"]
-        return add("p", "mm", (out, l, r, start, stop), [out], [l, r], c, grp=grp)
+        o = ops[-1]
+        if o["kind"] == "mm" and o["w"][0][0] == out[0] and o["grp"] == grp and o["at"] == lvl[1] and o["cost"] + c < CFG["run"] \
+                and not (grp and o["start"]):
+            o["args"].append((out, l, r, start, stop))
+            o["w"].append(out)
+            o["r"] += [l, r]
+            o["cost"] += c
+            return o
+        return add("p", "mm", [(out, l, r, start, stop)], [out], [l, r], c, grp=grp, start=start)
+
+    def const(out, name, start=False, stop=False, grp=None):
+        j = 128 * CW.index(name)
+        return mm(out, R("cw", j, j + 128), R("on5", 0, out[4]), start, stop, grp)
 
     def iota(out, pat, base, cm):
         return add("g", "iota", (out, pat, base, cm), [out], [], 130 + 2 * out[4] * cyc)
 
-    def dma(q, sem, out, src, nbytes, **kw):
+    def dma(q, sem, out, src, nbytes):
         outs = [out] if out[0] in SHAPES else []
         ins = [src] if src[0] in SHAPES else []
-        return add(q, "dma", (out, src, kw), outs, ins + (outs if kw else []), 100.0 if q != "g" else 1000.0,
-                   sem=sem, lat=C["dma"] + nbytes / 200.0)
+        return add(q, "dma", (out, src), outs, ins, 100.0, sem=sem, lat=C["dma"] + nbytes / 200.0)
 
     def ext(name, a, b):
         return (name, (slice(None), slice(a, b)), a, b, b - a, None)
 
-    def send(kind, t, src, dst, li):
-        s = add("g", "send", (kind, t, src, dst), [], [src], 300.0, sem="lo%d" % li, lat=C["flight"])
-        return add("x", "arr", (), [dst], [], 0.0, sem=("ap%d" if kind == "p" else "az%d") % t, lat=0.0, after=s)
+    def send(kind, t, srcs, dst, li):
+        s = add("g", "send", (kind, t, dst) + tuple(srcs), [], srcs, 300.0, sem="lo%d" % li, lat=C["flight"])
+        return add("x", "arr", (dst,) + tuple(srcs), [dst], [], 0.0, sem=("ap%d" if kind == "p" else "az%d") % t, lat=0.0, after=s)
 
     col = lambda name, j: R(name, j, j + 1)
+    ONB = R("on5", 0, 128)
     HB = lambda nm, h, o=0: R(nm, o + 128 * h, o + 128 * h + 128)
-    dma("s", "ldps", R("pss"), ext("ps", 0, 16), 8192)
+    dma("s", "ldxc", R("xs"), ext("xc", 0, 1024), 262144)
+    dma("a", "ldps", R("pss"), ext("ps", 0, 16), 8192)
     dma("s", "ldzi", R("zis"), ext("zi", 0, 256), 65536)
     dma("a", "ldwt", R("wts", 0, 1), ("wt", (slice(None), slice(None)), 0, 1, 1, None), 4096)
     dma("a", "ldkc", R("KK", 0, 1024), ext("kc", 0, 1024), 262144)
     dma("s", "ldnb", R("nbs"), ext("nb", 0, 1024), 524288)
-    iota(R("jrow"), [[1, 256]], 0, 0)
     iota(R("pci", 0, 1), [[0, 1]], 0, 1)
-    iota(R("ci"), [[1, 16]], 0, 0)
-    for q in range(4):
-        act(R("vr", 256 * q, 256 * q + 256), R("jrow"), AF.Identity, 256.0 * q - V0)
+    iota(R("jrow"), [[1, 256]], 0, 0)
     iota(R("mrow"), [[0, 16], [1, 16]], 0, 0)
     iota(R("grow"), [[1, 8], [0, 16]], 0, 0)
-    dma("s", "ldxc", R("xs"), ext("xc", 0, 1024), 262144)
-    PF, RC_, GC_, PX, WH, P2 = [col("cols", j) for j in range(6)]
-    S2 = "S1" if PB else "S2"
+    iota(R("ci"), [[1, 16]], 0, 0)
+    PF, RC, GC, PX, CN, CNM, CP2, CPM, CA, G15, WF, U12, AC, AT, WS = [col("cols", j) for j in range(15)]
+    tmp = lambda j: col("cols", 16 + j)
+    j128, m128 = R("jrow", 0, 128), R("mrow", 0, 128)
+    ms(R("on5"), 1.0)
+    for name, val in (("p24", M24), ("m24", -M24), ("q", -0.25)) + (("p36", M36), ("m36", -M36), ("pk", 1024.0)) * (CFG["Q"] != "aa"):
+        ms(HB("cw", CW.index(name)), val / 128)
+    for name, a, b in (("p23", M23 / 2, M23 / 2), ("mk", -512, -512), ("m2o", -M23, -2 * OFF), ("m23", -M23, -OFF / 2), ("pq", 2.0 ** 23, 1024.0)):
+        j = 128 * CW.index(name)
+        if a == b:
+            iota(R("cw", j, j + 128), [[0, 128]], int(a / 64), 0)
+        else:
+            iota(R("cw", j, j + 128, p=(0, 64)), [[0, 128]], int(a / 64), 0)
+            iota(R("cw", j, j + 128, p=(64, 128)), [[0, 128]], int(b / 64), 0)
+    act(R("onf"), R("on5", 0, 128), AF.Identity, 0.0, 1.0 / 16)
+    ms(R("rst"), 0.0)
+    ms(R("rst", 0, 128, 16), -float(2 ** 25))
+    ms(R("half"), 0.5)
+    ms(R("first"), 0.0)
+    ms(R("first", 0, 256, 16), 1.0)
+    scan(R("rown"), R("half"), R("first"), 0.0, ALU.mult, ALU.max)
+    ms(R("pw2", 16, 32), 2.0)
+    scan(R("pw2", 0, 16), R("pw2", 16, 32), R("first", 0, 16), 0.0, ALU.mult, ALU.max)
     cp(PF, col("pci", 0))
     ts(col("tmi", 0), col("pci", 0), 15, None, ALU.bitwise_and)
     ts(col("tmi", 1), col("pci", 0), 4, None, ALU.arith_shift_right)
     ts(col("tmi", 2), col("pci", 0), 1, None, ALU.bitwise_and)
-    cp(RC_, col("tmi", 0))
-    cp(GC_, col("tmi", 1))
-    ts(col("cols", 6), col("tmi", 2), -2.0, 1.0, ALU.mult, ALU.add)
-    tt(PX, col("cols", 6), PF, ALU.add)
+    cp(RC, col("tmi", 0))
+    cp(GC, col("tmi", 1))
+    ts(tmp(0), col("tmi", 2), -2.0, 1.0, ALU.mult, ALU.add)
+    tt(PX, tmp(0), PF, ALU.add)
     cp(R("cidx"), R("ci"))
-    j128 = R("jrow", 0, 128)
-    ts(R("maskM"), R("mrow"), RC_, None, ALU.is_equal)
-    ts(R("blk8"), R("jrow", 0, 8), GC_, None, ALU.is_equal)
-    ts(R("If"), j128, PF, None, ALU.is_equal)
-    ms(R("Sel"), 0.0)
-    ms(R("onb"), 1.0)
-    iota(R("onf"), [[0, 128]], 1, 0)
-    ms(R("zb"), 0.0)
-    ms(R("mh"), -0.5)
-    ms(R("rst", 0, 256), 0.0)
-    ms(R("rst", 0, 256, 16), -float(2 ** 25))
-    ms(R("hf16"), 0.5)
-    ms(R("zr16"), 0.0)
-    act(R("NIf"), R("If"), AF.Identity, 0.0, -1.0)
-    act(R("Ib"), R("If"), AF.Copy)
-    act(R("Ih"), R("If"), AF.Identity, 0.0, -0.5)
-    ts(R("NP"), j128, PX, -1.0, ALU.is_equal, ALU.mult)
-    act(R("Pm"), R("NP"), AF.Identity, 0.0, -1.0)
+    ts(R("maskM"), R("mrow"), RC, None, ALU.is_equal)
+    ts(R("blk8"), R("jrow", 0, 8), GC, None, ALU.is_equal)
+    ts(R("blkM"), R("grow"), GC, None, ALU.is_equal)
+    ts(R("Ib"), j128, PF, None, ALU.is_equal)
+    act(R("If"), R("Ib"), AF.Copy)
+    ts(R("I2"), j128, PF, 2.0, ALU.is_equal, ALU.mult)
+    for name, s in (("NIf", -1.0),) * (CFG["Q"] != "aa") + (("NIb", -1.0), ("Ih", 0.5), ("NIh", -0.5)):
+        act(R(name), R("Ib"), AF.Identity, 0.0, s)
+    ts(R("NP2"), j128, PX, -2.0, ALU.is_equal, ALU.mult)
+    act(R("PM2"), R("NP2"), AF.Identity, 0.0, -1.0)
+    tt(R("pw2", 32, 48), R("rown", 0, 16), R("maskM", 0, 16), ALU.mult)
+    red(CN, R("pw2", 32, 48))
+    tt(R("pw2", 16, 32), R("pw2", 0, 16), R("maskM", 0, 16), ALU.mult)
+    red(CP2, R("pw2", 16, 32))
+    ts(CNM, RC, 12.0, CN, ALU.is_lt, ALU.mult)
+    ts(CPM, RC, 12.0, CP2, ALU.is_lt, ALU.mult)
     ts(R("W19"), R("blk8"), UNIT, None, ALU.mult)
-    ts(R("W18"), R("blk8"), UNIT / 2, None, ALU.mult)
-    act(R("Ip"), R("If"), AF.Identity, 0.0, 0.5)
+    ts(R("pickw"), R("blk8"), CPM, None, ALU.mult)
     ts(R("pickb"), R("jrow", 0, 128, 16), PF, -2 * BIG, ALU.is_equal, ALU.mult)
-    scan(R("pw2"), R("hf16"), R("zr16"), float(2 ** 17), ALU.mult, ALU.add)
-    tt(R("pt16"), R("pw2"), R("maskM", 0, 16), ALU.mult)
-    red(col("cols", 7), R("pt16"))
-    ts(P2, col("cols", 7), 0.5, None, ALU.mult)
-    ts(R("Boff"), R("grow"), GC_, 65536.0, ALU.is_equal, ALU.mult)
-    ts(R("Bdia"), R("grow"), GC_, P2, ALU.is_equal, ALU.mult)
-    ts(R("rr16"), R("zr16"), RC_, None, ALU.add)
-    cp(R("thrc"), IND(R("pw2"), R("rr16")))
-    ms(R("pw3", 16, 32), 2.0)
-    scan(R("pw3", 0, 16), R("pw3", 16, 32), R("zr16"), 0.5, ALU.mult, ALU.add)
-    tt(R("pw3", 0, 16), R("pw3", 0, 16), R("maskM", 0, 16), ALU.mult)
-    red(col("cols", 8), R("pw3", 0, 16))
-    ts(col("cols", 9), RC_, 12.0, col("cols", 8), ALU.is_lt, ALU.mult)
-    ts(R("pickw"), R("blk8"), col("cols", 9), None, ALU.mult)
-    ts(col("cols", 10), RC_, 12.0, P2, ALU.is_lt, ALU.mult)
-    ts(R("D11"), R("If"), col("cols", 10), 1.0 / 16, ALU.mult, ALU.mult)
-    act(R("D11b"), R("D11"), AF.Copy)
-    iota(R("jb"), [[1, 256]], 0, 0)
-    iota(R("on2"), [[0, 256]], 1, 0)
-    for t in range(1, RO):
-        act(HB("Dt", t), R("D11"), AF.Identity, 0.0, 256.0 * t)
-    ts(R("Tr1"), R("mrow", 0, 128), RC_, col("cols", 8), ALU.is_gt, ALU.mult)
-    ts(R("Tr2"), R("mrow", 0, 128), 12.0, -1.0 / 32 / 65536, ALU.is_lt, ALU.mult)
-    tt(R("Tr1"), R("Tr1"), R("Tr2"), ALU.mult)
-    tt(R("Tr2"), R("thrc", 0, 128), R("Boff"), ALU.mult)
-    tt(R("Tri"), R("Tr1"), R("Tr2"), ALU.mult)
+    ts(R("t1"), j128, PF, CP2, ALU.is_gt, ALU.mult)
+    ts(R("t2"), m128, 12.0, 2.0, ALU.is_lt, ALU.mult)
+    tt(R("tu"), R("rown", 0, 128), R("t2"), ALU.mult)
+    tt(R("t3"), R("blkM"), R("tu"), ALU.mult)
+    tt(R("TriN"), R("t1"), R("t3"), ALU.mult)
+    tt(R("TriP"), R("I2"), R("TriN"), ALU.subtract)
+    act(tmp(6), RC, AF.Sigmoid, -256 * 11.5, 256.0, more=1300.0)
+    ts(U12, tmp(6), -1.0, 1.0, ALU.mult, ALU.add)
+    ts(tmp(6), RC, 12.0, None, ALU.is_equal)
+    ts(tmp(7), RC, 13.0, -EPS, ALU.is_equal, ALU.mult)
+    tt(tmp(1), tmp(6), tmp(7), ALU.add)
+    ts(CA, tmp(6), 0.5, tmp(1), ALU.mult, ALU.subtract)
+    ts(R("C30"), R("blkM"), tmp(1), None, ALU.mult)
+    ts(R("C80"), R("blkM"), CA, None, ALU.mult)
 
-    def code(bank, a, x, num):
-        n = x[4]
-        if isinstance(num, tuple):
-            mm(R(bank, a, a + n), R("D11"), num, True, False)
-        else:
-            mm(R(bank, a, a + n), R("D11b"), R("jb"), True, False)
-            if num:
-                mm(R(bank, a, a + n), HB("Dt", num), R("on2"), False, False)
-        for j in range(0, n, 256):
-            mm(R(bank, a + j, a + j + 256), R("NP"), R("mh"), False, False)
-        mm(R(bank, a, a + n), R("Tri"), x, False, True)
+    def code(bank, a, x, prow, nrow, c3, c8, whole=False):
+        o = R(bank, a, a + x[4])
+        for tri, d, c in (("TriN", "D", c3), ("TriP", "ND", c8)):
+            mm(o, R(tri), x, tri == "TriN")
+            if prow:
+                mm(o, R(d), prow)
+            mm(o, R(c), nrow or R("on5", 0, x[4]), False, tri == "TriP" and not whole)
+            if tri == "TriN":
+                const(o, "p24")
+                const(o, "m24")
+        if whole:
+            const(o, "p23")
+            const(o, "m2o", False, True)
+        return o
 
-    act(R("x2"), R("xs"), AF.Identity, 0.0, 2.0)
     for q in range(2):
-        bk, H = ("S0", "KA")[q], lambda nm: R(nm, 512 * q, 512 * q + 512)
-        code(bk, 0, H("x2"), H("vr"))
-        act(H("R00"), R(bk), AF.Identity, M35)
-        act(H("R0"), H("R00"), AF.Identity, -M35)
-        tt(H("b0"), R(bk), H("R0"), ALU.is_lt)
-        mm(R(bk), R("Ib"), H("x2"), True, False)
-        mm(R(bk), R("Ib"), H("b0"), False, True)
-        act(H("P"), R(bk), AF.Copy)
-    ts(WH, col("wts", 0), -0.5 / 256, None, ALU.mult)
-    for gg in range(8):
-        ts(R("Sel", 16 * gg, 2048, 129), R("onb", 0, 16), col("blk8", gg), -256.0, ALU.mult, ALU.mult)
-    ts(R("Wm"), R("Sel"), WH, None, ALU.mult)
-    ts(R("pt16"), R("jrow", 0, 16), 128.0, float(V0), ALU.mult, ALU.add)
-    ts(R("ncol"), R("pt16"), PF, None, ALU.add)
-    ts(R("pt16"), R("jrow", 0, 16), 16.0, float(W), ALU.mult, ALU.add)
-    ts(R("dmw"), R("pt16"), RC_, None, ALU.add)
-    for v in range(4):
-        iota(R("ki", 512 * v, 512 * v + 512, p=(0, 64)), [[-112, 2], [0, 16], [-256, 16]], 31 * 128, 0)
-    for v in range(2):
-        for ch in range(2):
-            for s in range(2):
-                for h in range(2):
-                    b = 1024 * v + 512 * ch + 256 * s + 128 * h
-                    on = [(ch, s, h, kq) in CFG["scalar"][v] for kq in range(4)]
-                    if all(on) or not any(on):
-                        iota(R("ki", b, b + 128, p=(64, 128)), [[0, 128]], (-7 if on[0] else -23) * 4096, 0)
-                    else:
-                        for kq in range(4):
-                            iota(R("ki", b + kq, b + 128, 4, p=(64, 128)), [[0, 32]], (-7 if on[kq] else -23) * 4096, 0)
-    act(R("Z0"), R("zis"), AF.Identity, 0.0, 2.0)
-    act(R("KK", 1024, 2048, 2), R("KK", 1, 1024, 2), AF.Copy)
-    act(R("KK", 1025, 2048, 2), R("KK", 0, 1024, 2), AF.Copy)
-    cp(R("L", 0, 1024), R("nbs"))
-
-    def wrap(src):
-        tt(R("bm"), IND(src, R("cidx")), R("maskM"), ALU.mult)
-        for h in range(2):
-            mm(R("TC0", 256 + 8 * h, 264 + 8 * h), HB("bm", h), R("blk8"))
+        o = code(("KE", "K0")[q], 0, R("xs", 512 * q, 512 * q + 512), None, None, "C30", "C80")
+        ts(R("P", 512 * q, 512 * q + 512), o, M23, -M23, ALU.add, ALU.add)
+    ts(R("D"), R("Ib"), CNM, None, ALU.mult)
+    act(R("ND"), R("D"), AF.Identity, 0.0, -1.0)
+    ms(R("t4"), 0.0)
+    ms(R("t4", 10, 128, 16), 1.0)
+    ms(R("t4", 11, 128, 16), 0.5)
+    ts(R("t1"), R("blkM"), tmp(6), None, ALU.mult)
+    tt(R("t2"), R("t1"), R("t4"), ALU.mult)
+    tt(R("C3"), R("C30"), R("t2"), ALU.subtract)
+    tt(R("C8"), R("C80"), R("t2"), ALU.add)
+    tt(R("N3"), R("C3"), R("D"), ALU.subtract)
+    tt(R("N8"), R("C8"), R("D"), ALU.add)
+    ts(R("pw2", 16, 24), R("jrow", 0, 8), 256.0, -1.0, ALU.mult, ALU.add)
+    ts(R("nbias"), R("pw2", 16, 24), U12, 1.0, ALU.mult, ALU.add)
+    ts(tmp(2), RC, 15.0, CN, ALU.is_lt, ALU.mult)
+    ts(R("Boff"), R("blkM"), 2.0 ** 26, None, ALU.mult)
+    ts(R("Bdia"), R("Boff"), tmp(2), None, ALU.mult)
+    ms(R3("mk", 0, 16, 16), 0.0)
+    ts(R3("mk", 0, 16, 0, 16), R("mrow"), RC, -2.0 ** 34, ALU.not_equal, ALU.mult)
+    act(R("NblkM"), R("blkM"), AF.Identity, 0.0, -1.0)
+    for j in range(2):
+        ms(R3("pr%d" % j, 0, 16, 16), -2000.0)
+    ms(R3("th2", 0, 16, 16), 0.0)
+    ts(R3("th2", 0, 16, 0, 16, p=(0, 64)), R("rown", p=(0, 64)), -2.0 ** 21, None, ALU.mult)
+    ms(R3("th2", 0, 16, 0, 16, p=(64, 128)), 32.0)
+    iota(R("d0"), [[0, 272]], 4096, 0)
+    ms(R("d0", 0, 272, 17), -4096.0)
+    ts(R("pw2", 32, 48), R("jrow", 0, 16), 16.0, float(W - V0), ALU.mult, ALU.add)
+    ts(R("d0", 16, 272, 17), R("pw2", 32, 48), RC, None, ALU.add)
+    ts(R("ncol"), R("jrow", 0, 16), 128.0, PF, ALU.mult, ALU.add)
+    ts(G15, GC, 16.0, 15.0, ALU.mult, ALU.add)
+    cp(WF, col("wts", 0))
+    ts(R("Wz"), R("jrow", 0, 144), G15, WF, ALU.is_equal, ALU.mult)
+    ts(col("tmi", 3), col("pci", 0), 2, 3, ALU.arith_shift_right, ALU.bitwise_and)
+    ts(tmp(3), col("tmi", 3), -4.0, PF, ALU.mult, ALU.add)
+    ts(tmp(4), tmp(3), 12.0, None, ALU.add)
+    cp(tmp(5), col("tmi", 3))
+    ts(R("cols", 24, 28), R("jrow", 0, 4), tmp(5), None, ALU.is_equal)
+    for q in range(4):
+        ts(R("Zq", 144 * q, 144 * q + 144), R("jrow", 0, 144), tmp(4), col("cols", 24 + q), ALU.is_equal, ALU.mult)
+    ms(R("Zb"), 0.0)
+    act(R("I4"), R("Ib"), AF.Copy)
+    iota(R("ki", p=(0, 64)), [[-128, 2], [0, 16], [-256, 16]], 31 * 128, 0)
+    iota(R("ki", p=(64, 128)), [[0, 512]], -23 * 4096, 0)
+    act(R("N13"), R("Ib"), AF.Identity, 0.0, -8192.0)
+    act(R("P13"), R("Ib"), AF.Identity, 0.0, 8192.0)
+    if CFG["fuse"]:
+        act(R("K32", 0, 1024), R("KK", 0, 1024), AF.Identity, OFF)
+        for j in range(2):
+            act(R("K32", 1024 + j, 2048, 2), R("KK", 1 - j, 1024, 2), AF.Identity, OFF)
+    else:
+        for j in range(2):
+            act(R("KK", 1024 + j, 2048, 2), R("KK", 1 - j, 1024, 2), AF.Copy)
+    ts(tmp(3), col("wts", 0), -0.5, None, ALU.mult)
+    ts(R("t3"), R("blkM"), tmp(3), None, ALU.mult)
+    mm(col("X2", 20), R("t3"), R("on5", 0, 1), True, True)
+    cp(WS, col("X2", 20))
 
     def cut_numbers(t, Z):
+        U = R("X2", 32, 48)
         for r in range(16):
-            mm(R("S1", 384, 400), HB("Wm", r), R(Z[0], Z[2] + r, Z[3], 16), r == 0, r == 15)
+            mm(U, R("Wz", 15 - r, 143 - r), R(Z[0], Z[2] + r, Z[3], 16), r == 0, r == 15)
         if t == 0:
-            cp(R("ui"), R("S1", 384, 400))
+            cp(R("ui"), U)
         else:
-            ts(R("ui"), R("S1", 384, 400), col("cols", 12), None, ALU.add)
+            ts(R("ui"), U, AT, None, ALU.add)
         ts(R("um"), R("ui"), V0 - 1, None, ALU.bitwise_and)
-        cp(R("u16", 0, 16), R("um"))
-        for j in range(2):
-            act(R("KU", 256 * j, 256 * j + 256), IND(R("KK", 1024 * j, 1024 * j + 1024), R("u16", 0, 16)), AF.Identity, 0.0, 2.0)
+        cp(R("u16"), R("um"))
+        for j in range(0 if CFG["fuse"] else 2):
+            act(R("KU", 256 * j, 256 * j + 256), IND(R("KK", 1024 * j, 1024 * j + 1024), R("u16")), AF.Identity, OFF)
 
-    wrap(R("pss"))
-    cp(R("pT0"), R("TC0", 256, 272))
-    cut_numbers(0, R("Z0"))
+    tt(R("bm"), IND(R("pss"), R("cidx")), R("maskM"), ALU.mult)
+    for h in range(2):
+        mm(R("K1", 8 * h, 8 * h + 8), HB("bm", h), R("blk8"), True, True)
+    ts(R("pT0"), R("K1", 0, 16), -float(V0), None, ALU.add)
+    cut_numbers(0, R("zis"))
     slot = {"v": 0, "a": 0, "s": 0}
+    DD = R("X1", 0, 272)
+    S16 = lambda nm, a=0, b=16: R3(nm, a, b, 0, 16)
 
     for t in range(RO):
         last = t == RO - 1
         SC = CFG["scalar"][1 if last else 0]
         pT = R("pT0") if t == 0 else R("lp", 16 * (t - 1), 16 * t)
-        Z = R("Z0") if t == 0 else R("lz", 256 * (t - 1), 256 * t)
-        bc, ac, CE, so, nf = "bc%d" % (t % 2), "act%d" % (t % 2), "CE%d" % (t % 2), ("so0", "soo")[t % 2], "nfr%d" % (t % 2)
+        Z = R("zis") if t == 0 else R("lz", 256 * (t - 1), 256 * t)
+        bc, pr, ac, CE, so = [n + str(t % 2) for n in ("bc", "pr", "act", "CE", "so")]
         n0 = V0 + M * t
+        nrow = R("nrow", M * t, M * t + M)
+        at(t, "pre")
+        act(nrow, R("jrow"), AF.Identity, col("nbias", t), U12)
+        gd = ("d", t)
+        mm(DD, R("Ib"), R("mk"), True, grp=gd)
+        mm(DD, ONB, R("th2"), grp=gd)
         at(t, "in")
-        wrap(pT)
+        tt(R("bm"), IND(pT, R("cidx")), R("maskM"), ALU.mult)
         act(R(bc), IND(pT, R("cidx")), AF.Copy)
         for h in range(2):
-            mm(HB("TC0", h), HB(bc, h), R("If"))
-        cp(R("pw16"), R("TC0", 256, 272))
-        cp(R("pwf"), R("TC0", 256, 272))
-        cp(R("pr16"), R("TC0", 0, 256))
-        mm(R("TC1", 0, 256), R("zb"), R("mh"), True, False, grp=("d", t))
+            mm(R("X0", 256 + 8 * h, 264 + 8 * h), HB("bm", h), R("blk8"), True, True)
+        for h in range(2):
+            mm(HB("X0" if CFG["pr"] == "v" else "X2", h), HB(bc, h), R("Ib"), True, True)
+        ts(R("pw16"), R("X0", 256, 272), float(V0), None, ALU.add)
+        cp(R("pwf"), R("X0", 256, 272))
+        cp(S16(pr), R("X0", 0, 256)) if CFG["pr"] == "v" else act(S16(pr), R("X2", 0, 256), AF.Copy)
+        for h in range(2):
+            mm(R("X1", 136 * h + 16, 136 * h + 136, 17), HB("bm", h), R("blk8"), grp=gd)
+        at(t, "eq")
         for c in range(16):
-            ts(EQ(c, 0, 256 - 16 * c), R("pr16", 16 * c, 256), col("pwf", c), None, ALU.is_equal)
+            ts(EQ(c, 0, 272 - 17 * c), R(pr, 17 * c, 272), col("pwf", c), None, ALU.is_equal)
             if c < 15:
-                mm(R("TC1", 16 * c + 16, 256), R("Boff"), EQ(c, 16, 256 - 16 * c), False, False, grp=("d", t))
-        mm(R("TC1", 0, 256), R("Bdia"), R3("eq", 0, 16, 0, 16), False, False, grp=("d", t))
-        tt(R(ac), R("TC1", 0, 256), R("thrc"), ALU.is_lt)
-        act(R("xg"), IND(R("P", 0, n0), R("pw16")), AF.Identity, -0.5)
-        act(R("xh"), R("xg"), AF.Identity, M24)
-        act(R("xp"), R("xh"), AF.Identity, -M24)
-        tt(R(CE, 0, 256), R("xp"), R("KU", 0, 256), ALU.min)
-        tt(R(CE, 256, 512), R("xp"), R("KU", 256, 512), ALU.min)
-        code("S1", 0, R(CE, 0, 256), t)
-        if CFG["RU"] == "a":
-            act(R("xh"), R("S1", 0, 256), AF.Identity, M35)
-            act(R("Ru", 0, 256), R("xh"), AF.Identity, -M35)
+                mm(R("X1", 17 * c + 17, 272), R("Boff"), EQ(c, 17, 272 - 17 * c), grp=gd)
+        mm(DD, R("Bdia"), R3("eq", 0, 16, 0, 17), grp=gd)
+        scan(R("sc"), R("d0"), DD, 0.0, ALU.min, ALU.max)
+        ts(R(so), R("sc", 16, 272, 17), float(V0), None, ALU.add)
+        act(R("idle"), DD, AF.Sigmoid)
+        AP = R("X1", 0, 256)
+        mm(AP, R("Ib"), R("on5", 0, 256), True)
+        mm(AP, R("NblkM"), S16("idle"), False, True)
+        at(t, "cd")
+        act(R("xp"), IND(R("P", 0, n0), R("pw16")), AF.Identity, OFF - 0.25, 0.5)
+        for ch in range(2):
+            k = IND(R("K32", 1024 * ch, 1024 * ch + 1024), R("u16")) if CFG["fuse"] else R("KU", 256 * ch, 256 * ch + 256)
+            tt(R(CE, 256 * ch, 256 * ch + 256), k, R("xp"), ALU.min)
+        o = code("X2", 0, R(CE, 0, 256), S16(pr), nrow, "N3", "N8", CFG["Cb"] == "a")
+        if CFG["Cb"] == "a":
+            act(R("Cb", 0, 256), o, AF.Copy)
         else:
-            ts(R("Ru", 0, 256), R("S1", 0, 256), M35, -M35, ALU.add, ALU.add)
-        tt(R("bit", 0, 256), R("S1", 0, 256), R("Ru", 0, 256), ALU.is_lt)
-        aw = R3("TC0", 0, 16, 0)
-        mm(aw, R("If"), R("dmw"), True, False)
-        for r in range(16):
-            mm(aw, HB("Sel", r), R(ac, r, 256, 16), False, r == 15)
-        if not last:
-            for h in range(2):
-                mm(R3("TC0", 8 * h, 8 * h + 8, 1), HB(ac, h), R("pickb"))
-        tt(R("Em"), R(CE, 256, 512), R(ac), ALU.mult)
-        code("TC1", 256, R("Em"), t)
-        ts(R("Ru", 256, 512), R("TC1", 256, 512), M35, -M35, ALU.add, ALU.add)
-        tt(R("bit", 256, 512), R("TC1", 256, 512), R("Ru", 256, 512), ALU.is_lt)
-        tt(R("so1"), aw, R("pwf"), ALU.max)
-        cp(R(so), R("so1"))
-        tt(IND(R("P"), R(so)), R(CE, 0, 256), R("bit", 0, 256), ALU.add)
-        tt(R("P", n0, n0 + M), R("Em"), R("bit", 256, 512), ALU.add)
+            ts(R("Cb", 0, 256), o, M23, -M23 - 2 * OFF, ALU.add, ALU.add)
+        cp(IND(R("P"), R(so)), R("Cb", 0, 256))
+        at(t, "ce")
+        o = code("X2", 256, R(CE, 256, 512), None, None, "C3", "C8", CFG["Eb"] == "p")
+        if CFG["Eb"] == "p":
+            act(R(ac), AP, AF.Copy, acc=None if last else AC)
+            tt(R("P", n0, n0 + M), o, R(ac), ALU.mult)
+        else:
+            ts(R("Cb", 256, 512), o, M23, -M23 - 2 * OFF, ALU.add, ALU.add)
+            tt(R("P", n0, n0 + M), R("Cb", 256, 512), AP, ALU.mult)
+            act(R(ac), AP, AF.Copy, acc=None if last else AC)
+
+        def thresholds(ch):
+            at(t, ("tb", "te")[ch])
+            S, x = ("K0", "KE")[ch], R("thr", 512 * ch, 512 * ch + 512)
+            for j in range(2):
+                mm(RS(S, 0, 128, 1, j, 4, 2), R("NP2"), R(CE, 256 * ch, 256 * ch + 256), True, True)
+            shift(CFG["TB"][ch], x, R(S), 2 * OFF)
+            for j in range(2):
+                o = R3(("TBC", "TBE")[ch], 0, 256, 2 * j, 2 * j + 2)
+                cp(o, x) if CFG["TB"][2 + ch] == "v" else act(o, x, AF.Copy)
+
+        thresholds(0)
+        thresholds(1)
         at(t, "a")
-        cp(R("a16"), IND(R("L", 0, n0) if t else R("nbs"), R("pw16")))
-        act(R("aF"), IND(R("L", 0, n0), R("pw16")), AF.Copy)
+        if t == 0:
+            ts(R("aF"), IND(R("nbs"), R("pw16")), -float(V0), None, ALU.add)
+        else:
+            act(R("aF"), IND(R("L", 0, n0), R("pw16")), AF.Identity, -float(V0))
+        for q in range(4):
+            for j in range(4):
+                x = 144 * q + 12 - 4 * j
+                mm(R("K1", 64 * q, 64 * q + 64), R("Zq", x, x + 128), R("aF", j, 256, 4), j == 0, j == 3)
+            if q in CFG["acut"]:
+                x = 64 * (max([-1] + [y for y in CFG["acut"] if y < q]) + 1)
+                shift(CFG["o16"][0], R("a16", x, 64 * q + 64), R("K1", x, 64 * q + 64), float(V0))
         at(t, "key")
         if not last:
-            red(col("cols", 11), aw)
-            ts(R("al1"), pT, 1.0 + BIG, None, ALU.add)
+            ts(R("al1"), pT, V0 + 1.0 + BIG, None, ALU.add)
             ts(R("al2"), R("al1"), int(BIG) + V0 - 1, None, ALU.bitwise_and)
-            tt(R("kyo"), R3("TC0", 0, 16, 1), R("al2"), ALU.add)
-        KB = (("KA", "KC"), ("KE", "KE"))
-        held = {}
-
-        def thresholds(ch, s, h):
-            if PB:
-                if held.get(("TB", h)) != ch:
-                    held[("TB", h)] = ch
-                    for kk in range(4):
-                        o, x = R3("TB", 128 * h, 128 * h + 128, kk), HB("NT", h, 256 * ch)
-                        add("p", "tr", (o, x, R("Ib")), [o], [x, R("Ib")], 128 * C["pcyc"] + C["p"], grp=None)
-                return R3("TB", 128 * h, 128 * h + 128, 0, 4)
-            bk = "TC1" if ch and not last else ("TC0", "TC1")[h]
-            if held.get(bk) != (ch, h):
-                held[bk] = (ch, h)
-                for kk in range(4):
-                    mm(R3(bk, 0, 128, kk), R("NP"), HB(CE, h, 256 * ch))
-            return R(bk)
-
-        if PB:
-            for j in range(4):
-                mm(HB("S1", j), HB(CE, j), R("NP"))
-            act(R("NT"), R("S1"), AF.Copy)
-            thresholds(0, 1, 0)
-            thresholds(0, 1, 1)
-        for ch in range(2):
-            b = 1024 * last + 512 * ch
-            if ch:
-                mm(R("KE"), R("onb"), R("ki", b, b + 512), True, False, grp=("KE", t))
-            else:
-                mm(R("KA", 0, 256), R("onb"), R("ki", b, b + 256), True, False, grp=("KA", t))
-                mm(R("KC", 256, 512), R("onb"), R("ki", b + 256, b + 512), True, False, grp=("KC", t))
+            const(R("X2", 0, 16), "mk", True)
             for h in range(2):
-                mm(HB(KB[ch][0], h), HB("aF", h), R("If"), False, False, grp=(KB[ch][0], t))
+                mm(R("X2", 8 * h, 8 * h + 8), HB(ac, h), R("pickb"), False, h == 1)
+            mm(col("X2", 16), R("onf"), AC, True, True)
+            tt(R("kyo"), R("X2", 0, 16), R("al2"), ALU.add)
+            ts(AT, col("X2", 16), WS, None, ALU.add)
+        KEY = lambda ch, s, h: HB("K%d" % h, s) if ch == 0 else HB("KE", 2 * s + h)
+        GRP = lambda ch, h: ("K%d" % h if ch == 0 else "KE", t)
+        for h in range(2):
+            mm(R("K%d" % h, 0, 256), ONB, R3("ki", 0, 2, 0, 128), True, grp=GRP(0, h))
+            mm(KEY(0, 0, h), HB("aF", h), R("Ib"), grp=GRP(0, h))
+        at(t, "ke")
+        mm(R("KE"), ONB, R("ki"), True, grp=GRP(1, 0))
+        for s in range(2):
+            if CFG["relu"]:
+                mm(R("KE", 256 * s, 256 * s + 256), R("NIb"), R(bc), grp=GRP(1, 0))
+            mm(KEY(1, 0, s), HB("aF", s), R("Ib"), grp=GRP(1, 0))
         at(t, "x" if last else "z")
         if not last:
-            mm(col("S1", 400), R("onf"), col("cols", 11))
-            ts(col("cols", 12), col("S1", 400), -1.0 / 4096, 8 * (M * W + M * (M - 1) // 2) / 4096.0, ALU.mult, ALU.add)
-            mm(R("S1", 0, 256), R("Ip"), R(CE, 0, 256), True, False)
-            mm(R("S1", 0, 256), R("Ih"), Z, False, True)
-            tt(R("dm"), R("S1", 0, 256), R(ac), ALU.mult)
-            mm(R("S1", 0, 256), R("Ib"), Z, True, False)
-            mm(R("S1", 0, 256), R("Ib"), R("mh"), False, False)
-            mm(R("S1", 0, 256), R("Ib"), R("dm"), False, True)
-            ts(R("sz", 256 * t, 256 * t + 256), R("S1", 0, 256), M24, -M24, ALU.add, ALU.add)
-            send("z", t, R("sz", 256 * t, 256 * t + 256), R("lz", 256 * t, 256 * t + 256), 2 * t)
+            o, dm = R("X2", 256, 512), R("dm", 256 * t, 256 * t + 256)
+            mm(o, R("Ih"), R(CE, 0, 256), True)
+            mm(o, R("NIh"), Z)
+            if t == 0:
+                const(o, "q")
+            const(o, "p23")
+            const(o, "m23", False, True)
+            tt(dm, o, R(ac), ALU.mult)
+            send("z", t, [Z, dm] + [R("half")] * (t == 0), R("lz", 256 * t, 256 * t + 256), 2 * t)
         else:
             for q, (a, b) in enumerate(((0, 1024), (1024, W))):
                 for a1 in range(a, b, 512):
-                    mm(R("S1"), R("Ip"), R("P", a1, a1 + 512), True, False)
-                    for j in range(2):
-                        mm(R("S1", 256 * j, 256 * j + 256), R("Ip"), R("mh"), False, j == 1)
-                    if a1 // 512 < CFG["xa"]:
-                        act(R("R00", 0, 512), R("S1"), AF.Identity, M23)
-                        act(R("Xo", a1, a1 + 512), R("R00", 0, 512), AF.Identity, -M23)
-                    else:
-                        ts(R("Xo", a1, a1 + 512), R("S1"), M23, -M23, ALU.add, ALU.add)
+                    shift(CFG["xo"][0], R("X16", a1, a1 + 512), R("P", a1, a1 + 512), OFF - 0.25, 0.5)
+                    shift(CFG["xo"][1], R("Xo", a1, a1 + 512), R("X16", a1, a1 + 512), -OFF)
                 dma("s", "stx%d" % q, ext("yx", a, b), R("Xo", a, b), 128 * 2 * (b - a))
+        if t == 0:
+            at(t, "key")
+            for q in range(2):
+                cp(R("L", 512 * q, 512 * q + 512), R("nbs", 512 * q, 512 * q + 512))
 
-        def gather(s, h):
+        def gather(s):
             at(t, "g")
-            for s1, i0, i1, q in CFG["gather"]:
-                if s1 == s and i0 // 128 == h:
+            for s1, i0, i1, q in CFG["gather"][1 if last else 0]:
+                if s1 == s:
                     o = R(("Ga", "Gb")[s], 16 * i0, 16 * i1)
-                    src = IND(R("P", 0, n0 + M), R(("a16", "b16")[s], i0, i1))
-                    if q == "v":
-                        cp(o, src)
-                    else:
-                        act(o, src, AF.Copy)
+                    src = IND(R("P", 0, n0 + M * s), R(("a16", "b16")[s], i0, i1))
+                    cp(o, src) if q == "v" else act(o, src, AF.Copy)
 
-        def siblings(h):
+        FOUR = lambda key, q, *kk: RS(key[0], key[2] // 4 + q, key[3] // 4, 4, *kk)
+
+        def siblings(qs, X):
             at(t, "sib")
-            S = ("S0", "S0" if PB else "S2")[h]
-            for k in range(16):
-                mm(R(S, k, 128, 16), R("Ga", 2048 * h + k, 2048 * h + 2048, 16), R("pickw"))
-            ts(HB("Rb", h), HB(S, 0), M35, -M35, ALU.add, ALU.add)
-            tt(HB("bT", h), HB(S, 0), HB("Rb", h), ALU.subtract)
-            mm(HB(S, 1), HB("bT", h), R("If"))
-            ts(HB("b16", h), HB(S, 1), float(V0), None, ALU.add)
-            for ch in range(2):
-                mm(HB(KB[ch][1], h, 256), R("If"), HB("bT", h), False, False, grp=(KB[ch][1], t))
+            q0, n = qs[0], 64 * len(qs)
+            S, B, Rb = R(X, 0, n), R(X, 256, 256 + n), R("Rb", 64 * q0, 64 * q0 + n)
+            for q in qs:
+                for h in range(2):
+                    y = 64 * (q - q0) + 32 * h
+                    mm(R(X, y, y + 32), HB("aF", h), RS("I4", q, 32, 4, 0, 4), True)
+                    for kk in range(4):
+                        x = 1024 * q + 512 * h
+                        mm(R(X, y + kk, y + 32, 4), R("Ga", x + kk, x + 512, 4), R("pickw"), False, kk == 3)
+            ts(Rb, S, M35, -M35, ALU.add, ALU.add)
+            tt(RS("Zb", 64 * q0 + 3, 64 * q0 + 3 + n, 4, 0, 4), S, Rb, ALU.subtract)
+            for y in range(0, n, 32):
+                for j in range(4):
+                    x = 64 * q0 + 3 + y - j
+                    mm(R(X, 256 + y, 288 + y), R("Zb", 4 * x, 4 * x + 128), R("Ib", j, 128, 4), j == 0, j == 3)
+            shift(CFG["o16"][1], R("b16", 64 * q0, 64 * q0 + n), B, float(V0))
+            for q in qs:
+                z = 64 * q + 3
+                at(t, "c")
+                for h in range(2):
+                    mm(FOUR(KEY(0, 1, h), q, 0, 4), R("Ib"), RS("Zb", z + 32 * h, z + 32 * h + 32, 4, 0, 4), grp=GRP(0, h))
+                at(t, "ke")
+                mm(FOUR(R("KE", 256, 512), q, 0, 4), R("Ib"), RS("Zb", z, z + 64, 4, 0, 4), grp=GRP(1, 0))
 
-        def tiles(ch, s, h):
-            G = ("Ga", "Gb")[s]
-            for kq in range(4):
-                at(t, ("c", "e" if (ch, s, h, kq) in SC else "ev")[ch])
-                b = 256 * s + 128 * h
-                x4 = R(G, 2048 * h + kq, 2048 * h + 2048, 4)
-                key = lambda kk: R(KB[ch][s], b + kq + 4 * kk, b + 128, 16)
-                grp = (KB[ch][s], t)
-                if (ch, s, h, kq) in SC:
-                    S = (S2, "S0", "KA")[slot["s"] % 3] if ch else (S2, "S0")[slot["s"] % 2]
+        def tiles(ch, s, q, hs):
+            G, TB = ("Ga", "Gb")[s], ("TBC", "TBE")[ch]
+            mine = [h for h in hs if not (ch and (s, h, q) in SC)]
+            for h in hs:
+                if h not in mine:
+                    at(t, "e")
+                    S = ("X0", "X2")[slot["s"] % 2]
                     slot["s"] += 1
                     j = 512 * (slot["a"] % NA)
                     slot["a"] += 1
-                    mm(R(S), R("Ib"), x4, True, False)
+                    mm(R(S), R("Ib"), R(G, 1024 * q + 512 * h, 1024 * q + 512 * h + 512), True)
                     for kk in range(4):
-                        mm(R(S, kk, 512, 4), R("Pm"), HB(CE, h, 256 * ch), False, kk == 3)
-                    act(R("ia", j, j + 512), R(S), AF.Sign, 0.5)
+                        mm(R(S, kk, 512, 4), R("PM2"), HB(CE, h, 256 * ch), False, kk == 3)
+                    act(R("ia", j, j + 512), R(S), AF.Sigmoid, 256 * (0.5 - 2 * OFF), 256.0)
                     for kk in range(4):
-                        mm(key(kk), R("ia", j + kk, j + 512, 4), R("W18"), False, False, grp=grp)
-                else:
-                    j = 128 * (slot["v"] % NV)
-                    slot["v"] += 1
-                    tt(R3("iv", j, j + 128, 0, 4), x4, thresholds(ch, s, h), ALU.is_ge)
+                        mm(FOUR(KEY(ch, s, h), q, kk), R("ia", j + kk, j + 512, 4), R("W19"), grp=GRP(ch, h))
+            if mine:
+                at(t, ("c", "ev")[ch])
+                slot["v"] += slot["v"] % len(mine)
+                j, n = 128 * (slot["v"] % NV), 128 * len(mine)
+                slot["v"] += len(mine)
+                x = 1024 * q + 512 * mine[0]
+                tt(R3("iv", j, j + n, 0, 4), R(G, x, x + 4 * n), R3(TB, 128 * mine[0], 128 * mine[0] + n, 0, 4), ALU.is_ge)
+                for x, h in enumerate(mine):
                     for kk in range(4):
-                        mm(key(kk), R3("iv", j, j + 128, kk), R("W19"), False, False, grp=grp)
+                        mm(FOUR(KEY(ch, s, h), q, kk), R3("iv", j + 128 * x, j + 128 * x + 128, kk), R("W19"), grp=GRP(ch, h))
 
-        def lists(ch):
-            c = "CE"[ch]
-            if ch == 1:
-                tt(R("m1E"), R("KE", 0, 256), R(bc), ALU.max)
-            tt(R("m2" + c), R(KB[ch][1], 256, 512), R("m1" + c), ALU.max)
-            if ch == 0:
-                for h in range(2):
-                    mm(HB("KC", h), HB("m2C", h), R("If"))
-                cp(R("RC"), R("KC", 0, 256))
-                ts(R("entC"), R("RC"), 8191, None, ALU.bitwise_and)
-                return
-            if ch == 1 and CFG["RE"] == "a":
-                act(R("R1"), R("m2E"), AF.Identity, M36)
-                act(R("RE"), R("R1"), AF.Identity, -M36)
+        def all_tiles(ch, s):
+            for q in range(4):
+                for hs in ([(0,), (1,)] if (ch, s, q) in CFG["split"] else [(0, 1)]):
+                    tiles(ch, s, q, hs)
+
+        def back(o, m, more, q=None):
+            if q:
+                mm(o, q, R("N13"), True)
             else:
-                ts(R("R" + c), R("m2" + c), M36, -M36, ALU.add, ALU.add)
-            for h in range(2):
-                mm(HB(KB[ch][1], h), HB("m2" + c, h), R("If"), True, False)
-                mm(HB(KB[ch][1], h), HB("R" + c, h), R("NIf"), False, True)
+                mm(o, m, R("NIf"), True)
+                const(o, "p36")
+                const(o, "m36")
+            mm(o, m, R("If"), False, not more)
+            for x, (l, r) in enumerate(more):
+                mm(o, l, r, False, x == len(more) - 1)
 
-        gather(0, 0)
-        gather(0, 1)
-        siblings(0)
-        tiles(0, 0, 0)
-        siblings(1)
-        tiles(0, 0, 1)
-        gather(1, 0)
-        gather(1, 1)
-        at(t, "c")
-        for h in range(2):
-            ts(HB("m1C", h), HB("KA", h), col("ncol", 2 * t + h), None, ALU.max)
-        if not last:
-            scan(R("wsc", 0, 256), R("rst", 0, 256), R("m1C"), 0.0, ALU.add, ALU.max)
-            tt(R("px1"), R("wsc", 15, 256, 16), R("kyo"), ALU.max)
-        at(t, "u")
-        if not last:
-            cut_numbers(t + 1, R("lz", 256 * t, 256 * t + 256))
-        tiles(0, 1, 0)
-        tiles(0, 1, 1)
+        gather(0)
+        for x, qs in enumerate(CFG["sibs"]):
+            siblings(qs, "X%d" % (x % 2))
+        all_tiles(0, 0)
+        gather(1)
+        all_tiles(0, 1)
         at(t, "out")
+        for h in range(2):
+            ts(HB("m1C", h), KEY(0, 0, h), col("ncol", 2 * t + h), None, ALU.max)
+            tt(HB("m2C", h), KEY(0, 1, h), HB("m1C", h), ALU.max)
+            if not last:
+                scan(HB("wsc", h), R("rst"), HB("m2C", h), 0.0, ALU.add, ALU.max)
         if not last:
-            scan(R("wsc", 256, 512), R("rst", 0, 256), R("KC", 256, 512), 0.0, ALU.add, ALU.max)
-            tt(R("px2"), R("px1"), R("wsc", 271, 512, 16), ALU.max)
-            ts(R("px3"), R("px2"), M36, -M36, ALU.add, ALU.add)
-            tt(R("sp", 16 * t, 16 * t + 16), R("px2"), R("px3"), ALU.subtract)
-            send("p", t, R("sp", 16 * t, 16 * t + 16), R("lp", 16 * t, 16 * t + 16), 2 * t + 1)
+            tt(R("px"), R("wsc", 15, 256, 16), R("kyo"), ALU.max)
+            ts(R("pq"), R("px"), M36, -M36, ALU.add, ALU.add)
+            tt(R("sp", 16 * t, 16 * t + 16), R("px"), R("pq"), ALU.subtract)
+            send("p", t, [R("sp", 16 * t, 16 * t + 16)], R("lp", 16 * t, 16 * t + 16), 2 * t + 1)
+            at(t, "u")
+            cut_numbers(t + 1, R("lz", 256 * t, 256 * t + 256))
         at(t, "lc")
-        lists(0)
+        for h in range(2):
+            q = CFG["Q"][0] == "a"
+            if q:
+                act(HB("QC", h), HB("m2C", h), AF.Identity, 1024.0, 1.0 / 8192)
+            back(HB("K%d" % h, 2), HB("m2C", h), [], q and HB("QC", h))
+            act(HB("entC", h), HB("K%d" % h, 2), AF.Identity, V0 + q * 2.0 ** 23)
         cp(IND(R("L"), R(so)), R("entC"))
         if last:
             dma("s", "stn0", ext("yn", 0, 1152), R("L", 0, 1152), 128 * 4 * 1152)
-            dma("s", "stn1", ext("yn", 1152, n0), R("L", 1152, n0), 128 * 4 * 1152)
-        for s, h in CFG["eorder"]:
-            tiles(1, s, h)
+            dma("a", "stn1", ext("yn", 1152, n0), R("L", 1152, n0), 128 * 4 * 1152)
+        all_tiles(1, 0)
+        all_tiles(1, 1)
         at(t, "le")
-        lists(1)
-        tt(R("L", n0, n0 + M), R("KE", 0, 256), R(ac), ALU.mult)
+        act(R("m1E"), R("KE", 0, 256), AF.Relu) if CFG["relu"] else tt(R("m1E"), R("KE", 0, 256), R(bc), ALU.max)
+        tt(R("m2E"), R("KE", 256, 512), R("m1E"), ALU.max)
+        q = CFG["Q"][1] == "a"
+        if q:
+            act(R("QE"), R("m2E"), AF.Identity, 1024.0, 1.0 / 8192)
+        for h in range(2):
+            j = 128 * CW.index("pq" if q else "pk")
+            back(HB("KE", h), HB("m2E", h), [(R("Ib"), S16(pr, 8 * h, 8 * h + 8))] * CFG["relu"] + [(R("cw", j, j + 128), R("on5", 0, 128))]
+                 + [(R("P13"), HB(ac, h))] * (CFG["Lw"] == "a"), q and HB("QE", h))
+        if CFG["Lw"] == "a":
+            act(R("L", n0, n0 + M), R("KE", 0, 256), AF.Relu, -8192.0)
+        else:
+            tt(R("L", n0, n0 + M), R("KE", 0, 256), R(ac), ALU.mult)
         if last:
             dma("s", "stn2", ext("yn", n0, W), R("L", n0, W), 128 * 4 * M)
     return ops
@@ -566,11 +684,12 @@ def depend(ops):
                     if o["eng"] == "p":
                         for m in b["cur"]:
                             q = ops[m]
-                            if o["grp"] is None or q["grp"] != o["grp"] or q["args"][3]:
+                            if o["grp"] is None or q["grp"] != o["grp"] or q["start"]:
                                 follow.add(m)
                     if o["n"] not in b["cur"]:
                         b["cur"].append(o["n"])
-                    continue
+                    if o["eng"] == "p":
+                        continue
                 keep = []
                 full = wr and r[5] is None and r[4] == r[3] - r[2] and r[1][0] == slice(None)
                 for (lo, hi, w, m) in acc.get(r[0], []):
@@ -585,76 +704,27 @@ def depend(ops):
         o["dep"], o["follow"] = dep, follow - dep
 
 
-def schedule(ops):
-    n = len(ops)
-    hop = C["hop"]
-    succ = [[] for _ in ops]
-    for o in ops:
-        for m in o["dep"] | o["follow"]:
-            succ[m].append(o["n"])
-    rank = [0.0] * n
-    for o in reversed(ops):
-        i = o["n"]
-        rank[i] = o["cost"] + o.get("lat", 0.0) + max([rank[m] + hop for m in succ[i]] + [0.0]) \
-            + CFG["boost"].get(o["w"][0][0] if o["w"] else "", 0.0)
-    left = [len(o["dep"] | o["follow"]) for o in ops]
-    ready_at = [0.0] * n
-    free = {e: 0.0 for e in "vapgsx"}
-    pool = {e: [] for e in "vapgsx"}
-    for o in ops:
-        if left[o["n"]] == 0:
-            pool[o["eng"]].append(o["n"])
-    order = []
-    end = 0.0
-    while len(order) < n:
-        best = None
-        for e, pl in pool.items():
-            if pl:
-                t0 = max(free[e], min(ready_at[i] for i in pl))
-                if best is None or t0 < best[0]:
-                    best = (t0, e)
-        t0, e = best
-        i = max((i for i in pool[e] if ready_at[i] <= t0 + 1e-6), key=lambda i: (rank[i], -i))
-        j = max((j for j in pool[e] if ready_at[j] <= t0 + CFG["look"]), key=lambda j: (rank[j], -j))
-        if j != i and ready_at[j] - t0 < CFG["frac"] * ops[i]["cost"]:
-            i, t0 = j, ready_at[j]
-        pool[e].remove(i)
-        o = ops[i]
-        o["t0"] = t0
-        if e != "x":
-            free[e] = t0 + o["cost"]
-        done = t0 + o["cost"] + o.get("lat", 0.0)
-        end = max(end, done)
-        order.append(i)
-        for m in succ[i]:
-            same = i in ops[m]["follow"] and ops[m]["eng"] == e
-            ready_at[m] = max(ready_at[m], t0 if same else done + hop)
-            left[m] -= 1
-            if left[m] == 0:
-                pool[ops[m]["eng"]].append(m)
-    return order, end
-
-
 def place(ops, seq, before):
     start = [0.0] * len(ops)
     line = {e: ([], []) for e in "vapgs"}
     for i in seq:
-        o = ops[i]
-        t = max([start[m] + d for m, d in before[i]] + [0.0])
-        if o["eng"] != "x":
-            a, b = line[o["eng"]]
-            lo, hi = 0, len(b)
-            while lo < hi:
-                mid = (lo + hi) // 2
-                if b[mid] <= t:
-                    lo = mid + 1
-                else:
-                    hi = mid
-            while lo < len(a) and a[lo] < t + o["cost"] - 1e-6:
-                t = max(t, b[lo])
+        e, c = ops[i]
+        t = 0.0
+        for m, d in before[i]:
+            d += start[m]
+            if d > t:
+                t = d
+        if e != "x":
+            a, b = line[e]
+            lo = n = len(b)
+            while lo and b[lo - 1] > t:
+                lo -= 1
+            while lo < n and a[lo] < t + c - 1e-6:
+                if b[lo] > t:
+                    t = b[lo]
                 lo += 1
             a.insert(lo, t)
-            b.insert(lo, t + o["cost"])
+            b.insert(lo, t + c)
         start[i] = t
     return start
 
@@ -682,40 +752,87 @@ def improve(ops):
             left[m] -= 1
             if not left[m]:
                 pool.append(m)
-    start = place(ops, seq, fwd)
-    best = (max(start[i] + ops[i]["cost"] + ops[i].get("lat", 0.0) for i in range(n)), start)
+    if CFG.get("path"):
+        way = [0.0] * n
+        for i in reversed(range(n)):
+            way[i] = max([way[m] + d - ops[m]["cost"] + ops[i]["cost"] for m, d in bwd[i]] + [ops[i]["cost"] + ops[i].get("lat", 0.0)])
+        seq = sorted(range(n), key=lambda i: (-way[i], i))
+    ec = [(o["eng"], o["cost"]) for o in ops]
+    ends = [(o["n"], o["cost"] + o.get("lat", 0.0)) for o in ops if o["kind"] == "dma"]
+    start = place(ec, seq, fwd)
+    finish = lambda st: max(st[i] + d for i, d in ends)
+    best = (finish(start), start)
     for o in ops:
         bwd[o["n"]].append((tail, o.get("lat", 0.0)))
-    ext = ops + [dict(eng="x", cost=0.0)]
-    finish = lambda st: max(st[i] + ops[i]["cost"] + ops[i].get("lat", 0.0) for i in range(n))
+    ext = ec + [("x", 0.0)]
 
     def there_and_back(st):
-        rev = place(ext, [tail] + sorted(range(n), key=lambda i: (-(st[i] + ops[i]["cost"]), -i)), bwd + [[]])
-        return place(ops, sorted(range(n), key=lambda i: (-(rev[i] + ops[i]["cost"]), i)), fwd)
+        rev = place(ext, [tail] + sorted(range(n), key=lambda i: (-(st[i] + ec[i][1]), -i)), bwd + [[]])
+        return place(ec, sorted(range(n), key=lambda i: (-(rev[i] + ec[i][1]), i)), fwd)
 
     for _ in range(CFG["passes"]):
         start = there_and_back(start)
         if finish(start) < best[0]:
             best = (finish(start), start)
-    kinds = {}
+    seen, like, kinds = {}, [], {}
     for o in ops:
-        kinds.setdefault((o["lvl"] % 100, o["eng"], o["w"][0][0][:2] if o["w"] else ""), []).append(o["n"])
-    names = sorted(kinds)
+        t, name = o["at"]
+        k = (name, o["eng"], o["w"][0][0].rstrip("01") if o["w"] else o["kind"])
+        seen[t, k] = seen.get((t, k), 0) + 1
+        like.append(k + (seen[t, k],))
+        if like[-1] not in kinds.setdefault(k, []):
+            kinds[k].append(like[-1])
+    arr = [i for i in range(n) if ops[i]["kind"] == "arr" and ops[i]["sem"][:2] == "ap"]
+    span = best[1][arr[2]] - best[1][arr[1]]
+    off = {}
+    for t in (2, 0, RO - 1):
+        zero = best[1][arr[t - 1]] if t else best[1][arr[0]] - span
+        for i in range(n):
+            if ops[i]["at"][0] == t and like[i] not in off:
+                off[like[i]] = best[1][i] - zero
+    if CFG["when"]:
+        span = CFG["span"]
+        for k, (a, step) in CFG["when"].items():
+            for x in kinds.get(k, []):
+                off[x] = a + step * (x[3] - 1)
+        for i in range(n):
+            if ops[i]["at"][1] == "start":
+                off[like[i]] = best[1][i] - CFG["lead"]
+    pre = [[m for m, d in f] for f in fwd]
+
+    def lay(off):
+        key = [ops[i]["at"][0] * span + off[like[i]] for i in range(n)]
+        for i in range(n):
+            for m in pre[i]:
+                if key[m] >= key[i]:
+                    key[i] = key[m] + 1e-3
+        st = place(ec, sorted(range(n), key=lambda i: key[i]), fwd)
+        return finish(st), st
+
+    names, each = sorted(kinds), sorted(off)
+    now = lay(off)
+    if CFG["when"]:
+        best = now
     x = CFG["seed"]
     for it in range(CFG["tries"]):
         x = (x * 1103515245 + 12345) % 2 ** 31
-        key = list(best[1])
-        shift = (-4000.0, -2000.0, -900.0, -400.0, 400.0, 900.0, 2000.0, 4000.0)[(x >> 8) % 8]
+        shift = (150.0, 400.0, 900.0, 2000.0, 4000.0)[(x >> 8) % 5] * (1 - 2 * ((x >> 20) % 2))
         members = kinds[names[(x >> 12) % len(names)]]
-        for i in members[(x >> 24) % 2::1 + (x >> 25) % 2]:
-            key[i] += shift
-        for i in range(n):
-            for m, d in fwd[i]:
-                if key[m] >= key[i]:
-                    key[i] = key[m] + 1e-3
-        start = place(ops, sorted(range(n), key=lambda i: key[i]), fwd)
-        if (x >> 20) % 4 == 0:
-            start = there_and_back(start)
+        x = (x * 1103515245 + 12345) % 2 ** 31
+        a = (x >> 10) % len(members)
+        members = (members, members[a:], members[:a + 1], members[a:a + 1])[(x >> 20) % 4]
+        for k in members:
+            off[k] += shift
+        new = lay(off)
+        if new[0] <= now[0] + CFG["slack"] * (1 - it / CFG["tries"]) * ((x >> 5) % 32) / 32:
+            now = new
+            if new[0] < best[0]:
+                best = new
+        else:
+            for k in members:
+                off[k] -= shift
+    for _ in range(2):
+        start = there_and_back(best[1])
         if finish(start) < best[0]:
             best = (finish(start), start)
     end, start = best
@@ -732,8 +849,8 @@ def plan():
     for i in order:
         if ops[i].get("grp") is not None:
             lastg[ops[i]["grp"]] = i
-    for i in lastg.values():
-        ops[i]["args"] = ops[i]["args"][:4] + (True,)
+    for gr, i in lastg.items():
+        ops[i]["args"][-1] = ops[i]["args"][-1][:4] + (True,)
     pos, cnt, known = {}, {}, {e: {} for e in "vapgsx"}
     for i in order:
         o = ops[i]
@@ -797,7 +914,7 @@ def rank_program(g, core, T, topo):
         q = Q[o["eng"]]
         for m in o["waits"]:
             q.wait_ge(T.sem[ops[m]["src"]], count(ops[m]))
-        a = [ap(T, x) for x in o["args"]]
+        a = [ap(T, x) for x in o["args"]] if k != "mm" else None
         if k == "cp":
             ins = q.tensor_copy(a[0], a[1])
         elif k == "tt":
@@ -811,21 +928,26 @@ def rank_program(g, core, T, topo):
         elif k == "red":
             ins = q.tensor_reduce(a[0], a[1], AxisListType.X, ALU.add)
         elif k == "act":
-            ins = q.activation(a[0], a[1], a[2], bias=a[3], scale=a[4])
+            ins = q.activation(a[0], a[1], a[2], bias=a[3], scale=a[4], accum_out=a[5])
         elif k == "mm":
-            ins = q.matmul(*a)
-        elif k == "tr":
-            ins = q.transpose(*a)
+            for x in o["args"]:
+                ins = q.matmul(*[ap(T, y) for y in x])
         elif k == "iota":
             if DT[o["args"][0][0]] == I32:
                 ins = q.iota(*a)
             else:
                 ins = q.iota(a[0], a[1], a[2], a[3], allow_small_or_imprecise_dtypes=True)
         elif k == "dma":
-            q.dma_start(a[0], a[1], **a[2]).then_inc(T.sem[o["sem"]], 16)
+            q.dma_start(a[0], a[1]).then_inc(T.sem[o["sem"]], 16)
             continue
         else:
-            q.remote_dma(a[3], a[2], T.sem[("ap%d" if a[0] == "p" else "az%d") % a[1]], T.sem[o["sem"]], pid, rid, topo.mask(core, nxt))
+            there = T.sem[("ap%d" if a[0] == "p" else "az%d") % a[1]]
+            if len(a) == 4:
+                q.remote_dma(a[2], a[3], there, T.sem[o["sem"]], pid, rid, topo.mask(core, nxt))
+            else:
+                x = RemoteDMATransfer(dst_ids=[DstId(rid=rid, pnc=pid)], dma_engine_mask=topo.mask(core, nxt), remote_sem=there,
+                                      srcs=a[3:], dsts=[a[2]], alu_op=1)
+                q.remote_dma_fused([x], local_sem=T.sem[o["sem"]])
             continue
         if o.get("mark"):
             ins.then_inc(T.sem[o["src"]], 1)

@@ -15,13 +15,13 @@ NV, NA = 24, 8
 F32, BF, F16, I32, U16 = "float32", "bfloat16", "float16", "int32", "uint16"
 
 CFG = {
-    "scalar": [{(0, h, q) for h in range(2) for q in range(2)}, {(0, h, q) for h in range(2) for q in range(2)}],
+    "scalar": [set(), set()],
     "split": {(0, 1, 3)},
     "gather": [[(0, 0, 64, "a"), (0, 64, 128, "v"), (0, 128, 192, "a"), (0, 192, 256, "a"),
                 (1, 0, 64, "a"), (1, 64, 128, "a"), (1, 128, 192, "a"), (1, 192, 224, "a"), (1, 224, 256, "a")]] * 2,
-    "TB": "aavv", "acut": (0, 3), "o16": "av", "Lw": "a", "sibs": [(0,), (1,), (2, 3)], "fuse": 0, "pr": "a", "Cb": "a", "Eb": "p", "Q": "aa", "xo": "vv", "run": 330.0, "passes": 4, "tries": 5000, "seed": 7,
-    "relu": 1,
-    "slack": 300.0, "span": 19500.0, "lead": 12000.0,
+    "TB": "aavv", "acut": (0, 3), "o16": "av", "Lw": "a", "sibs": [(0,), (1,), (2, 3)], "fuse": 0, "pr": "a", "Cb": "a", "Eb": "p", "Q": "aa", "xo": "vv", "run": 420.0, "passes": 4, "tries": 10000, "seed": 7,
+    "relu": 1, "onA": ("I2", "C30", "C80", "D", "t5", "t7", "Boff", "Bdia"), "usc": 0,
+    "slack": 500.0, "again": 50, "aim": 2, "span": 19500.0, "lead": 12000.0,
     "when": {
         ('pre', 'a', 'nrow'): (-3000, 0), ('pre', 'p', 'X'): (-1500, 100),
         ('in', 'v', 'bm'): (0, 0), ('in', 'a', 'bc'): (0, 0), ('in', 'p', 'X'): (450, 300), ('in', 'p', 'X2'): (500, 0), ('in', 'v', 'pw16'): (600, 0),
@@ -49,7 +49,7 @@ CFG = {
     "lvl": {"pre": -60, "in": 8, "eq": 10, "cd": 9, "ce": 12, "tb": 14, "a": 13, "key": 24, "z": 22, "x": 60, "g": 20, "sib": 21, "c": 25, "u": 40,
             "out": 26, "lc": 110, "te": 14, "ke": 28, "e": 111, "ev": 111, "le": 112},
 }
-C = {"cyc": 0.83, "pcyc": 0.42, "g": 1.56, "s": 3.8, "v": 55.0, "a": 120.0, "p": 12.0, "hop": 90.0, "flight": 2200.0, "dma": 2200.0}
+C = {"cyc": 0.83, "pcyc": 0.42, "g": 1.56, "s": 3.8, "v": 55.0, "a": 120.0, "p": 18.0, "hop": 90.0, "flight": 2200.0, "dma": 2200.0}
 CW = ["p24", "m24", "p36", "m36", "p23", "m23", "q", "mk", "pk", "m2o", "pq"]
 
 SB = {
@@ -57,15 +57,15 @@ SB = {
     "P": (WD, BF), "L": (WD, F32), "Xo": (W, BF), "X16": (W, F16),
     "pci": (4, I32), "tmi": (4, I32), "cols": (32, F32), "ci": (16, I32), "cidx": (16, U16),
     "jrow": (256, BF), "grow": (128, BF), "mrow": (256, BF), "maskM": (256, BF), "nrow": (M * RO, F16),
-    "rown": (256, BF), "first": (256, BF), "half": (256, BF), "pw2": (48, F32), "I2": (128, BF), "t4": (128, BF),
+    "rown": (256, BF), "first": (256, BF), "half": (256, BF), "pw2": (48, F32), "I2": (128, BF), "t4": (128, BF), "t5": (128, BF), "t6": (128, BF), "t7": (128, BF),
     "If": (128, F32), "NIf": (128, F32), "Ib": (128, BF), "NIb": (128, BF), "Ih": (128, BF), "NIh": (128, BF),
     "NP2": (128, BF), "PM2": (128, BF), "blkM": (128, BF), "t1": (128, BF), "t2": (128, BF), "t3": (128, BF),
     "tu": (128, BF), "N3": (128, BF), "N8": (128, BF), "nbias": (8, F32), "K32": (2048, F32), "QC": (256, F16), "QE": (256, F16), "N13": (128, BF), "P13": (128, BF),
     "TriN": (128, BF), "TriP": (128, BF), "D": (128, BF), "ND": (128, BF), "C3": (128, BF), "C8": (128, BF), "C30": (128, BF), "C80": (128, BF),
     "blk8": (8, BF), "W19": (8, BF), "pickw": (8, BF), "pickb": (8, BF), "Boff": (128, BF), "Bdia": (128, BF),
     "Wz": (144, BF), "on5": (512, BF), "onf": (128, F32), "cw": (128 * len(CW), BF),
-    "rst": (128, BF), "ncol": (16, F32), "d0": (272, F32), "sc": (272, F32), "pT0": (16, F32),
-    "bm": (256, F16), "bc0": (256, F16), "bc1": (256, F16), "pwf": (16, F32), "pw16": (16, U16),
+    "rst": (256, BF), "ncol": (16, F32), "d0": (272, F32), "sc": (272, F32), "pT0": (16, F32),
+    "bm": (256, F16), "bc0": (256, F16), "bc1": (256, F16), "pwf": (16, F32), "pwh": (16, F16), "pw16": (16, U16),
     "xp": (256, F16), "KU": (512, F16), "CE0": (512, F16), "CE1": (512, F16), "Cb": (512, BF),
     "so0": (16, U16), "so1": (16, U16), "thr": (1024, BF), "act0": (256, BF), "act1": (256, BF), "NblkM": (128, BF),
     "a16": (256, U16), "aF": (256, F16), "b16": (256, U16), "Rb": (256, F32), "Zq": (4 * 144, BF), "Ga": (4096, BF), "Gb": (4096, BF),
@@ -205,6 +205,13 @@ def build():
             return act(out, a, AF.Identity, bias, scale)
         return ts(out, a, bias, None, ALU.add) if scale == 1.0 else ts(out, a, scale, bias, ALU.mult, ALU.add)
 
+    def times(out, a, s):
+        if out[0] + str(out[2]) in onA or "all" in onA:
+            return act(out, a, AF.Identity, 0.0, s)
+        return ts(out, a, s, None, ALU.mult)
+
+    onA = [R(x)[0] + str(R(x)[2]) for x in CFG["onA"]]
+
     def mm(out, l, r, start=False, stop=False, grp=None):
         c = max(min(64, l[4]), r[4]) * C["pcyc"] * (4 if DT[l[0]] == F32 else 1) + C["p"]
         o = ops[-1]
@@ -256,7 +263,8 @@ def build():
     ms(R("on5"), 1.0)
     for name, val in (("p24", M24), ("m24", -M24), ("q", -0.25)) + (("p36", M36), ("m36", -M36), ("pk", 1024.0)) * (CFG["Q"] != "aa"):
         ms(HB("cw", CW.index(name)), val / 128)
-    for name, a, b in (("p23", M23 / 2, M23 / 2), ("mk", -512, -512), ("m2o", -M23, -2 * OFF), ("m23", -M23, -OFF / 2), ("pq", 2.0 ** 23, 1024.0)):
+    for name, a, b in (("p23", M23 / 2, M23 / 2), ("mk", -512, -512), ("m2o", -M23, -2 * OFF), ("m23", -M23, -OFF / 2)) \
+            + (("pq", 2.0 ** 23, 1024.0),) * (CFG["Lw"] != "a"):
         j = 128 * CW.index(name)
         if a == b:
             iota(R("cw", j, j + 128), [[0, 128]], int(a / 64), 0)
@@ -265,7 +273,7 @@ def build():
             iota(R("cw", j, j + 128, p=(64, 128)), [[0, 128]], int(b / 64), 0)
     act(R("onf"), R("on5", 0, 128), AF.Identity, 0.0, 1.0 / 16)
     ms(R("rst"), 0.0)
-    ms(R("rst", 0, 128, 16), -float(2 ** 25))
+    ms(R("rst", 0, 256, 16), -float(2 ** 25))
     ms(R("half"), 0.5)
     ms(R("first"), 0.0)
     ms(R("first", 0, 256, 16), 1.0)
@@ -286,19 +294,20 @@ def build():
     ts(R("blkM"), R("grow"), GC, None, ALU.is_equal)
     ts(R("Ib"), j128, PF, None, ALU.is_equal)
     act(R("If"), R("Ib"), AF.Copy)
-    ts(R("I2"), j128, PF, 2.0, ALU.is_equal, ALU.mult)
+    times(R("I2"), R("Ib"), 2.0)
     for name, s in (("NIf", -1.0),) * (CFG["Q"] != "aa") + (("NIb", -1.0), ("Ih", 0.5), ("NIh", -0.5)):
         act(R(name), R("Ib"), AF.Identity, 0.0, s)
     ts(R("NP2"), j128, PX, -2.0, ALU.is_equal, ALU.mult)
-    act(R("PM2"), R("NP2"), AF.Identity, 0.0, -1.0)
+    if any(CFG["scalar"]):
+        act(R("PM2"), R("NP2"), AF.Identity, 0.0, -1.0)
     tt(R("pw2", 32, 48), R("rown", 0, 16), R("maskM", 0, 16), ALU.mult)
     red(CN, R("pw2", 32, 48))
     tt(R("pw2", 16, 32), R("pw2", 0, 16), R("maskM", 0, 16), ALU.mult)
     red(CP2, R("pw2", 16, 32))
     ts(CNM, RC, 12.0, CN, ALU.is_lt, ALU.mult)
     ts(CPM, RC, 12.0, CP2, ALU.is_lt, ALU.mult)
-    ts(R("W19"), R("blk8"), UNIT, None, ALU.mult)
-    ts(R("pickw"), R("blk8"), CPM, None, ALU.mult)
+    times(R("W19"), R("blk8"), UNIT)
+    times(R("pickw"), R("blk8"), CPM)
     ts(R("pickb"), R("jrow", 0, 128, 16), PF, -2 * BIG, ALU.is_equal, ALU.mult)
     ts(R("t1"), j128, PF, CP2, ALU.is_gt, ALU.mult)
     ts(R("t2"), m128, 12.0, 2.0, ALU.is_lt, ALU.mult)
@@ -306,14 +315,14 @@ def build():
     tt(R("t3"), R("blkM"), R("tu"), ALU.mult)
     tt(R("TriN"), R("t1"), R("t3"), ALU.mult)
     tt(R("TriP"), R("I2"), R("TriN"), ALU.subtract)
-    act(tmp(6), RC, AF.Sigmoid, -256 * 11.5, 256.0, more=1300.0)
-    ts(U12, tmp(6), -1.0, 1.0, ALU.mult, ALU.add)
+    act(tmp(12), RC, AF.Sigmoid, 256 * 11.5, -256.0, more=1300.0)
+    ts(U12, tmp(12), 0.5, None, ALU.is_gt)
     ts(tmp(6), RC, 12.0, None, ALU.is_equal)
     ts(tmp(7), RC, 13.0, -EPS, ALU.is_equal, ALU.mult)
     tt(tmp(1), tmp(6), tmp(7), ALU.add)
     ts(CA, tmp(6), 0.5, tmp(1), ALU.mult, ALU.subtract)
-    ts(R("C30"), R("blkM"), tmp(1), None, ALU.mult)
-    ts(R("C80"), R("blkM"), CA, None, ALU.mult)
+    times(R("C30"), R("blkM"), tmp(1))
+    times(R("C80"), R("blkM"), CA)
 
     def code(bank, a, x, prow, nrow, c3, c8, whole=False):
         o = R(bank, a, a + x[4])
@@ -333,22 +342,22 @@ def build():
     for q in range(2):
         o = code(("KE", "K0")[q], 0, R("xs", 512 * q, 512 * q + 512), None, None, "C30", "C80")
         ts(R("P", 512 * q, 512 * q + 512), o, M23, -M23, ALU.add, ALU.add)
-    ts(R("D"), R("Ib"), CNM, None, ALU.mult)
+    times(R("D"), R("Ib"), CNM)
     act(R("ND"), R("D"), AF.Identity, 0.0, -1.0)
     ms(R("t4"), 0.0)
     ms(R("t4", 10, 128, 16), 1.0)
     ms(R("t4", 11, 128, 16), 0.5)
-    ts(R("t1"), R("blkM"), tmp(6), None, ALU.mult)
-    tt(R("t2"), R("t1"), R("t4"), ALU.mult)
-    tt(R("C3"), R("C30"), R("t2"), ALU.subtract)
-    tt(R("C8"), R("C80"), R("t2"), ALU.add)
+    times(R("t5"), R("blkM"), tmp(6))
+    tt(R("t6"), R("t5"), R("t4"), ALU.mult)
+    tt(R("C3"), R("C30"), R("t6"), ALU.subtract)
+    tt(R("C8"), R("C80"), R("t6"), ALU.add)
     tt(R("N3"), R("C3"), R("D"), ALU.subtract)
     tt(R("N8"), R("C8"), R("D"), ALU.add)
     ts(R("pw2", 16, 24), R("jrow", 0, 8), 256.0, -1.0, ALU.mult, ALU.add)
     ts(R("nbias"), R("pw2", 16, 24), U12, 1.0, ALU.mult, ALU.add)
     ts(tmp(2), RC, 15.0, CN, ALU.is_lt, ALU.mult)
-    ts(R("Boff"), R("blkM"), 2.0 ** 26, None, ALU.mult)
-    ts(R("Bdia"), R("Boff"), tmp(2), None, ALU.mult)
+    times(R("Boff"), R("blkM"), 2.0 ** 26)
+    times(R("Bdia"), R("Boff"), tmp(2))
     ms(R3("mk", 0, 16, 16), 0.0)
     ts(R3("mk", 0, 16, 0, 16), R("mrow"), RC, -2.0 ** 34, ALU.not_equal, ALU.mult)
     act(R("NblkM"), R("blkM"), AF.Identity, 0.0, -1.0)
@@ -364,7 +373,10 @@ def build():
     ts(R("ncol"), R("jrow", 0, 16), 128.0, PF, ALU.mult, ALU.add)
     ts(G15, GC, 16.0, 15.0, ALU.mult, ALU.add)
     cp(WF, col("wts", 0))
-    ts(R("Wz"), R("jrow", 0, 144), G15, WF, ALU.is_equal, ALU.mult)
+    if CFG["usc"]:
+        ts(R("Wz", 0, 128), R("blkM"), WF, None, ALU.mult)
+    else:
+        ts(R("Wz"), R("jrow", 0, 144), G15, WF, ALU.is_equal, ALU.mult)
     ts(col("tmi", 3), col("pci", 0), 2, 3, ALU.arith_shift_right, ALU.bitwise_and)
     ts(tmp(3), col("tmi", 3), -4.0, PF, ALU.mult, ALU.add)
     ts(tmp(4), tmp(3), 12.0, None, ALU.add)
@@ -385,14 +397,19 @@ def build():
     else:
         for j in range(2):
             act(R("KK", 1024 + j, 2048, 2), R("KK", 1 - j, 1024, 2), AF.Copy)
-    ts(tmp(3), col("wts", 0), -0.5, None, ALU.mult)
-    ts(R("t3"), R("blkM"), tmp(3), None, ALU.mult)
-    mm(col("X2", 20), R("t3"), R("on5", 0, 1), True, True)
+    ts(tmp(13), col("wts", 0), -0.5, None, ALU.mult)
+    times(R("t7"), R("blkM"), tmp(13))
+    mm(col("X2", 20), R("t7"), R("on5", 0, 1), True, True)
     cp(WS, col("X2", 20))
 
     def cut_numbers(t, Z):
         U = R("X2", 32, 48)
-        for r in range(16):
+        if CFG["usc"]:
+            mm(R("X2", 0, 256), R("Wz", 0, 128), Z, True)
+            mm(R("X2", 0, 256), R("Ib"), R3("mk", 0, 16, 0, 16), False, True)
+            scan(R("sc", 0, 256), R("rst"), R("X2", 0, 256), 0.0, ALU.add, ALU.max)
+            U = R("sc", 15, 256, 16)
+        for r in range(0 if CFG["usc"] else 16):
             mm(U, R("Wz", 15 - r, 143 - r), R(Z[0], Z[2] + r, Z[3], 16), r == 0, r == 15)
         if t == 0:
             cp(R("ui"), U)
@@ -426,17 +443,27 @@ def build():
         mm(DD, R("Ib"), R("mk"), True, grp=gd)
         mm(DD, ONB, R("th2"), grp=gd)
         at(t, "in")
-        tt(R("bm"), IND(pT, R("cidx")), R("maskM"), ALU.mult)
-        act(R(bc), IND(pT, R("cidx")), AF.Copy)
-        for h in range(2):
-            mm(R("X0", 256 + 8 * h, 264 + 8 * h), HB("bm", h), R("blk8"), True, True)
-        for h in range(2):
-            mm(HB("X0" if CFG["pr"] == "v" else "X2", h), HB(bc, h), R("Ib"), True, True)
-        ts(R("pw16"), R("X0", 256, 272), float(V0), None, ALU.add)
-        cp(R("pwf"), R("X0", 256, 272))
-        cp(S16(pr), R("X0", 0, 256)) if CFG["pr"] == "v" else act(S16(pr), R("X2", 0, 256), AF.Copy)
-        for h in range(2):
-            mm(R("X1", 136 * h + 16, 136 * h + 136, 17), HB("bm", h), R("blk8"), grp=gd)
+        if t == 0:
+            mm(R("X2", 0, 256), R("blkM"), R("bm"), True, True)
+            act(S16(pr), R("X2", 0, 256), AF.Identity, -float(V0))
+            cp(R("pw16"), R("pss"))
+            ts(R("pwf"), R("pss"), -float(V0), None, ALU.add)
+            ts(R("pwh"), R("pss"), -float(V0), None, ALU.add)
+            mm(R("X1", 16, 272, 17), R("Ib"), R("pwh"), grp=gd)
+            at(t, "key")
+            act(R(bc), IND(pT, R("cidx")), AF.Copy)
+        else:
+            tt(R("bm"), IND(pT, R("cidx")), R("maskM"), ALU.mult)
+            act(R(bc), IND(pT, R("cidx")), AF.Copy)
+            for h in range(2):
+                mm(R("X0", 256 + 8 * h, 264 + 8 * h), HB("bm", h), R("blk8"), True, True)
+            for h in range(2):
+                mm(HB("X2", h), HB(bc, h), R("Ib"), True, True)
+            ts(R("pw16"), R("X0", 256, 272), float(V0), None, ALU.add)
+            cp(R("pwf"), R("X0", 256, 272))
+            cp(S16(pr), R("X2", 0, 256)) if CFG["pr"] == "v" else act(S16(pr), R("X2", 0, 256), AF.Copy)
+            for h in range(2):
+                mm(R("X1", 136 * h + 16, 136 * h + 136, 17), HB("bm", h), R("blk8"), grp=gd)
         at(t, "eq")
         for c in range(16):
             ts(EQ(c, 0, 272 - 17 * c), R(pr, 17 * c, 272), col("pwf", c), None, ALU.is_equal)
@@ -627,7 +654,7 @@ def build():
             ts(HB("m1C", h), KEY(0, 0, h), col("ncol", 2 * t + h), None, ALU.max)
             tt(HB("m2C", h), KEY(0, 1, h), HB("m1C", h), ALU.max)
             if not last:
-                scan(HB("wsc", h), R("rst"), HB("m2C", h), 0.0, ALU.add, ALU.max)
+                scan(HB("wsc", h), R("rst", 0, 128), HB("m2C", h), 0.0, ALU.add, ALU.max)
         if not last:
             tt(R("px"), R("wsc", 15, 256, 16), R("kyo"), ALU.max)
             ts(R("pq"), R("px"), M36, -M36, ALU.add, ALU.add)
@@ -656,10 +683,10 @@ def build():
             act(R("QE"), R("m2E"), AF.Identity, 1024.0, 1.0 / 8192)
         for h in range(2):
             j = 128 * CW.index("pq" if q else "pk")
-            back(HB("KE", h), HB("m2E", h), [(R("Ib"), S16(pr, 8 * h, 8 * h + 8))] * CFG["relu"] + [(R("cw", j, j + 128), R("on5", 0, 128))]
-                 + [(R("P13"), HB(ac, h))] * (CFG["Lw"] == "a"), q and HB("QE", h))
+            back(HB("KE", h), HB("m2E", h), [(R("Ib"), S16(pr, 8 * h, 8 * h + 8))] * CFG["relu"]
+                 + [(R("P13"), HB(ac, h)) if CFG["Lw"] == "a" else (R("cw", j, j + 128), ONB)], q and HB("QE", h))
         if CFG["Lw"] == "a":
-            act(R("L", n0, n0 + M), R("KE", 0, 256), AF.Relu, -8192.0)
+            act(R("L", n0, n0 + M), R("KE", 0, 256), AF.Relu, V0 + q * 2.0 ** 23 - 8192.0)
         else:
             tt(R("L", n0, n0 + M), R("KE", 0, 256), R(ac), ALU.mult)
         if last:
@@ -799,9 +826,13 @@ def improve(ops):
             if ops[i]["at"][1] == "start":
                 off[like[i]] = best[1][i] - CFG["lead"]
     pre = [[m for m, d in f] for f in fwd]
+    wide, steps = [span], {}
+    for k in sorted(off):
+        steps.setdefault(k[0], []).append(k)
+        steps.setdefault(k[:2], []).append(k)
 
     def lay(off):
-        key = [ops[i]["at"][0] * span + off[like[i]] for i in range(n)]
+        key = [ops[i]["at"][0] * wide[0] + off[like[i]] for i in range(n)]
         for i in range(n):
             for m in pre[i]:
                 if key[m] >= key[i]:
@@ -809,7 +840,25 @@ def improve(ops):
         st = place(ec, sorted(range(n), key=lambda i: key[i]), fwd)
         return finish(st), st
 
-    names, each = sorted(kinds), sorted(off)
+    def blocked(st):
+        stop = {}
+        for i in range(n):
+            stop[ec[i][0], round(st[i] + ec[i][1])] = i
+        i = max(ends, key=lambda x: st[x[0]] + x[1])[0]
+        pairs = []
+        while st[i] > 1.0:
+            m, d = max(fwd[i] + [(i, -1e9)], key=lambda x: st[x[0]] + x[1])
+            if st[m] + d < st[i] - 1.0:
+                m = stop.get((ec[i][0], round(st[i])))
+                if m is None:
+                    break
+                if like[m] != like[i]:
+                    pairs.append((m, i))
+            i = m
+        return pairs
+
+    held = [None, None]
+    names = sorted(kinds)
     now = lay(off)
     if CFG["when"]:
         best = now
@@ -820,7 +869,28 @@ def improve(ops):
         members = kinds[names[(x >> 12) % len(names)]]
         x = (x * 1103515245 + 12345) % 2 ** 31
         a = (x >> 10) % len(members)
-        members = (members, members[a:], members[:a + 1], members[a:a + 1])[(x >> 20) % 4]
+        members = (members, members[a:], members[:a + 1], members[a:a + 1], steps[members[0][0]], steps[members[0][:2]])[(x >> 20) % 6]
+        if (x >> 24) % 4 < CFG["aim"]:
+            if held[0] is not now:
+                held[:] = [now, blocked(now[1])]
+            if held[1]:
+                m, i = held[1][(x >> 9) % len(held[1])]
+                gap = ops[i]["at"][0] * wide[0] + off[like[i]] - ops[m]["at"][0] * wide[0] - off[like[m]]
+                members, shift = (([like[i]], -gap - 1.0), ([like[m]], gap + 1.0))[(x >> 7) % 2]
+                if (x >> 6) % 2:
+                    members = [k for k in kinds[members[0][:3]] if (k[3] - members[0][3]) * shift >= 0]
+        if it % CFG["again"] == CFG["again"] - 1:
+            old, zero = dict(off), now[1][arr[1]]
+            for i in range(n):
+                if ops[i]["at"][0] == 2:
+                    off[like[i]] = now[1][i] - zero
+            wide[0], was = now[1][arr[2]] - zero, wide[0]
+            new = lay(off)
+            if new[0] <= now[0] + CFG["slack"]:
+                now = new
+            else:
+                off.update(old)
+                wide[0] = was
         for k in members:
             off[k] += shift
         new = lay(off)

from concourse.bass import DstId, RemoteDMATransfer
from concourse.mybir import AluOpType, AxisListType, ActivationFunctionType

ALU = AluOpType
AF = ActivationFunctionType
V0, M, RO, STEP, NR = 1024, 256, 6, 3, 8
W = V0 + M * RO
WD = W + M
UNIT = float(2 ** 19)
BIG = float(2 ** 22)
M23, M24, M35, M36 = 1.5 * 2 ** 23, 1.5 * 2 ** 24, 1.5 * 2 ** 35, 1.5 * 2 ** 36
OFF = 1536.0
EPS = 2.0 ** -12
NV, NA = 24, 8
F32, BF, F16, I32, U16 = "float32", "bfloat16", "float16", "int32", "uint16"

CFG = {
    "scalar": [set(), set()],
    "split": {(0, 1, 3)},
    "gather": [[(0, 0, 64, "a"), (0, 64, 128, "v"), (0, 128, 192, "a"), (0, 192, 256, "a"),
                (1, 0, 64, "a"), (1, 64, 128, "a"), (1, 128, 192, "a"), (1, 192, 224, "a"), (1, 224, 256, "a")]] * 2,
    "TB": "aavv", "acut": (0, 3), "o16": "av", "Lw": "a", "sibs": [(0,), (1,), (2, 3)], "fuse": 0, "pr": "a", "Cb": "a", "Eb": "p", "Q": "aa", "xo": "vv", "run": 420.0, "passes": 4, "tries": 10000, "seed": 7,
    "relu": 1, "onA": ("I2", "C30", "C80", "D", "t5", "t7", "Boff", "Bdia"), "usc": 0,
    "slack": 500.0, "again": 50, "aim": 2, "span": 19500.0, "lead": 12000.0,
    "when": {
        ('pre', 'a', 'nrow'): (-3000, 0), ('pre', 'p', 'X'): (-1500, 100),
        ('in', 'v', 'bm'): (0, 0), ('in', 'a', 'bc'): (0, 0), ('in', 'p', 'X'): (450, 300), ('in', 'p', 'X2'): (500, 0), ('in', 'v', 'pw16'): (600, 0),
        ('in', 'v', 'pwf'): (650, 0), ('in', 'a', 'pr'): (640, 0),
        ('eq', 'v', 'eq'): (1050, 120), ('eq', 'p', 'X'): (1900, 90), ('eq', 'v', 'sc'): (3450, 0), ('eq', 'v', 'so'): (3800, 0), ('eq', 'a', 'idle'): (4900, 0),
        ('cd', 'a', 'xp'): (960, 0), ('cd', 'v', 'CE'): (1000, 2200), ('cd', 'p', 'X2'): (1800, 250), ('cd', 'a', 'Cb'): (3400, 0), ('cd', 'v', 'P'): (3950, 0),
        ('ce', 'p', 'X2'): (4300, 240), ('ce', 'a', 'act'): (6300, 0), ('ce', 'v', 'P'): (6900, 0),
        ('tb', 'p', 'K'): (3900, 0), ('tb', 'a', 'thr'): (4250, 0), ('tb', 'v', 'TBC'): (6300, 270),
        ('te', 'p', 'KE'): (5500, 0), ('te', 'a', 'thr'): (9400, 0), ('te', 'v', 'TBE'): (12500, 270),
        ('a', 'a', 'aF'): (1400, 0), ('a', 'v', 'aF'): (1400, 0), ('a', 'p', 'K'): (3350, 200), ('a', 'a', 'a16'): (3800, 300),
        ('key', 'v', 'al'): (7200, 0), ('key', 'v', 'al2'): (7300, 0), ('key', 'p', 'X2'): (7000, 0), ('key', 'v', 'kyo'): (7400, 0),
        ('key', 'v', 'cols'): (7500, 0), ('key', 'p', 'K'): (6000, 100), ('key', 'v', 'L'): (12000, 500),
        ('ke', 'p', 'KE'): (10000, 200), ('z', 'p', 'X2'): (7600, 240), ('z', 'v', 'dm'): (8200, 0), ('z', 'g', 'send'): (8500, 0), ('z', 'x', 'lz'): (8800, 0),
        ('g', 'a', 'Ga'): (4900, 1400), ('g', 'v', 'Ga'): (4900, 1400), ('g', 'a', 'Gb'): (9500, 1400), ('g', 'v', 'Gb'): (9000, 1400),
        ('sib', 'p', 'X'): (6400, 350), ('sib', 'v', 'Rb'): (6800, 1400), ('sib', 'v', 'Zb'): (6900, 1400), ('sib', 'v', 'b16'): (7300, 1400),
        ('c', 'p', 'K'): (7500, 330), ('c', 'v', 'iv'): (7600, 900),
        ('out', 'v', 'm1C'): (14000, 500), ('out', 'v', 'm2C'): (14200, 500), ('out', 'v', 'wsc'): (14400, 500), ('out', 'v', 'px'): (15200, 0),
        ('out', 'v', 'pq'): (15300, 0), ('out', 'v', 'sp'): (15400, 0), ('out', 'g', 'send'): (15500, 0), ('out', 'x', 'lp'): (15800, 0),
        ('u', 'p', 'X2'): (12000, 320), ('u', 'v', 'ui'): (12800, 0), ('u', 'v', 'um'): (12900, 0), ('u', 'v', 'u16'): (13000, 0), ('u', 'a', 'KU'): (16500, 400),
        ('lc', 'a', 'QC'): (15500, 300), ('lc', 'p', 'K'): (15800, 300), ('lc', 'a', 'entC'): (16100, 300), ('lc', 'v', 'L'): (17500, 0),
        ('ev', 'v', 'iv'): (15600, 480), ('ev', 'p', 'KE'): (16000, 480), ('e', 'p', 'X'): (14500, 500), ('e', 'p', 'X2'): (14800, 500),
        ('e', 'a', 'ia'): (15000, 550), ('e', 'p', 'KE'): (15600, 550),
        ('le', 'a', 'm1E'): (18800, 0), ('le', 'v', 'm2E'): (19200, 0), ('le', 'a', 'QE'): (19500, 0), ('le', 'p', 'KE'): (19800, 250), ('le', 'a', 'L'): (20800, 0),
    },
    "lvl": {"pre": -60, "in": 8, "eq": 10, "cd": 9, "ce": 12, "tb": 14, "a": 13, "key": 24, "z": 22, "x": 60, "g": 20, "sib": 21, "c": 25, "u": 40,
            "out": 26, "lc": 110, "te": 14, "ke": 28, "e": 111, "ev": 111, "le": 112},
}
C = {"cyc": 0.83, "pcyc": 0.42, "g": 1.56, "s": 3.8, "v": 55.0, "a": 120.0, "p": 18.0, "hop": 90.0, "flight": 2200.0, "dma": 2200.0}
CW = ["p24", "m24", "p36", "m36", "p23", "m23", "q", "mk", "pk", "m2o", "pq"]

SB = {
    "nbs": (1024, I32), "KK": (2048, BF), "zis": (256, BF), "pss": (16, I32), "wts": (4, I32), "xs": (1024, BF),
    "P": (WD, BF), "L": (WD, F32), "Xo": (W, BF), "X16": (W, F16),
    "pci": (4, I32), "tmi": (4, I32), "cols": (32, F32), "ci": (16, I32), "cidx": (16, U16),
    "jrow": (256, BF), "grow": (128, BF), "mrow": (256, BF), "maskM": (256, BF), "nrow": (M * RO, F16),
    "rown": (256, BF), "first": (256, BF), "half": (256, BF), "pw2": (48, F32), "I2": (128, BF), "t4": (128, BF), "t5": (128, BF), "t6": (128, BF), "t7": (128, BF),
    "If": (128, F32), "NIf": (128, F32), "Ib": (128, BF), "NIb": (128, BF), "Ih": (128, BF), "NIh": (128, BF),
    "NP2": (128, BF), "PM2": (128, BF), "blkM": (128, BF), "t1": (128, BF), "t2": (128, BF), "t3": (128, BF),
    "tu": (128, BF), "N3": (128, BF), "N8": (128, BF), "nbias": (8, F32), "K32": (2048, F32), "QC": (256, F16), "QE": (256, F16), "N13": (128, BF), "P13": (128, BF),
    "TriN": (128, BF), "TriP": (128, BF), "D": (128, BF), "ND": (128, BF), "C3": (128, BF), "C8": (128, BF), "C30": (128, BF), "C80": (128, BF),
    "blk8": (8, BF), "W19": (8, BF), "pickw": (8, BF), "pickb": (8, BF), "Boff": (128, BF), "Bdia": (128, BF),
    "Wz": (144, BF), "on5": (512, BF), "onf": (128, F32), "cw": (128 * len(CW), BF),
    "rst": (256, BF), "ncol": (16, F32), "d0": (272, F32), "sc": (272, F32), "pT0": (16, F32),
    "bm": (256, F16), "bc0": (256, F16), "bc1": (256, F16), "pwf": (16, F32), "pwh": (16, F16), "pw16": (16, U16),
    "xp": (256, F16), "KU": (512, F16), "CE0": (512, F16), "CE1": (512, F16), "Cb": (512, BF),
    "so0": (16, U16), "so1": (16, U16), "thr": (1024, BF), "act0": (256, BF), "act1": (256, BF), "NblkM": (128, BF),
    "a16": (256, U16), "aF": (256, F16), "b16": (256, U16), "Rb": (256, F32), "Zq": (4 * 144, BF), "Ga": (4096, BF), "Gb": (4096, BF),
    "wsc": (256, F32), "px": (16, F32), "pq": (16, F32), "ia": (512 * NA, BF), "al1": (16, I32), "al2": (16, I32), "kyo": (16, F32),
    "ui": (16, I32), "um": (16, I32), "u16": (16, U16),
    "m1C": (256, F32), "m2C": (256, F32), "entC": (256, F32), "m1E": (256, F32), "m2E": (256, F32),
    "sp": (16 * (RO - 1), F32), "dm": (256 * (RO - 1), BF), "lp": (16 * (RO - 1), F32), "lz": (256 * (RO - 1), BF),
}
MATS = [n for n, x in SB.items() if x == (128, BF)]
for _n in MATS:
    del SB[_n]
SB["mat"] = (128 * len(MATS), BF)
SHAPES = {n: [128, c] for n, (c, d) in SB.items()}
SCRATCH = {n: ("sbuf", [128, c], d) for n, (c, d) in SB.items()}
for _n, _s in [("iv", [128, 128 * NV, 4]), ("eq", [128, 16, 272]), ("mk", [128, 16, 17]), ("th2", [128, 16, 17]), ("ki", [128, 2, 256]),
               ("idle", [128, 16, 17]), ("pr0", [128, 16, 17]), ("pr1", [128, 16, 17]),
               ("Zb", [128, 260, 4]), ("I4", [128, 32, 4])]:
    SHAPES[_n] = _s
    SCRATCH[_n] = ("sbuf", _s, F16 if _n[:2] in ("pr", "Zb") else BF)
PS = {"TBC": [128, 256, 4], "TBE": [128, 256, 4], "K0": [128, 128, 4], "K1": [128, 128, 4], "KE": [128, 128, 4],
      "X0": [128, 512], "X1": [128, 512], "X2": [128, 512]}
for _n, _s in PS.items():
    SHAPES[_n] = _s
    SCRATCH[_n] = ("psum", _s, BF if _n[:2] == "TB" else F32)
DT = {n: v[2] for n, v in SCRATCH.items()}
LOADS = ["ps", "zi", "wt", "kc", "nb", "xc"]
STORES = ["x0", "x1", "n0", "n1", "n2"]
SEMAPHORES = ["sv", "sa", "st", "sg"] + ["ld" + n for n in LOADS] + ["st" + n for n in STORES] \
    + ["ap%d" % t for t in range(RO - 1)] + ["az%d" % t for t in range(RO - 1)] + ["lo%d" % t for t in range(2 * RO - 2)]
ESEM = {"v": "sv", "a": "sa", "p": "st", "g": "sg"}


def R(name, a=None, b=None, step=1, p=None):
    if name in MATS:
        j = 128 * MATS.index(name)
        return R("mat", j + (a or 0), j + (b or 128), step, p)
    n = SHAPES[name][1] * (SHAPES[name][2] if len(SHAPES[name]) == 3 else 1)
    a = 0 if a is None else a
    b = n if b is None else b
    ps = slice(None) if p is None else slice(p[0], p[1])
    if len(SHAPES[name]) == 3:
        q = SHAPES[name][2]
        return (name, (ps, slice(a // q, b // q), slice(None)), a, b, b - a, None)
    return (name, (ps, slice(a, b, step)), a, b, len(range(a, b, step)), None)


def R3(name, i0, i1, k0, k1=None, p=None):
    q = SHAPES[name][2]
    kk = k0 if k1 is None else slice(k0, k1)
    ps = slice(None) if p is None else slice(p[0], p[1])
    return (name, (ps, slice(i0, i1), kk), i0 * q, i1 * q, (i1 - i0) * (1 if k1 is None else k1 - k0), None)


def RS(name, i0, i1, step, k0, k1=None, kstep=1):
    q = SHAPES[name][2]
    kk = k0 if k1 is None else slice(k0, k1, kstep)
    n = len(range(i0, i1, step)) * (1 if k1 is None else len(range(k0, k1, kstep)))
    return (name, (slice(None), slice(i0, i1, step), kk), i0 * q, i1 * q, n, None)


def EQ(c, a, b):
    return ("eq", (slice(None), c, slice(a, b)), 272 * c + a, 272 * c + b, b - a, None)


def IND(win, off):
    return (win[0], win[1], win[2], win[3], 16 * off[4], off)


def ap(T, r):
    if not isinstance(r, tuple):
        return r
    x = T[r[0]][r[1]]
    return x if r[5] is None else x.indirect(ap(T, r[5]))


def build():
    ops = []
    cyc = C["cyc"]
    lvl = [0, (0, "start")]

    def at(t, name):
        lvl[0] = 100 * t + CFG["lvl"][name]
        lvl[1] = (t, name)

    def add(eng, kind, args, outs, ins, cost, **kw):
        rd = []
        for r in ins:
            if isinstance(r, tuple):
                rd.append(r)
                if r[5] is not None:
                    rd.append(r[5])
        for r in outs:
            if r[5] is not None:
                rd.append(r[5])
        o = dict(eng=eng, kind=kind, args=args, w=list(outs), r=rd, cost=cost, n=len(ops), lvl=lvl[0], at=lvl[1], **kw)
        ops.append(o)
        return o

    def two(*rs):
        return all(DT[r[0]] in (BF, F16, U16) for r in rs)

    def vcost(out, ins, tt=False):
        n = ins[0][4]
        if out[5] is not None:
            return 50 + n * C["s"] * cyc
        if ins[0][5] is not None:
            return 50 + n * C["g"] * cyc
        c = 0.5 if two(out, *ins) else 1.0
        if tt and not any(r[0] in PS for r in ins):
            c *= 2
        return C["v"] + n * c * cyc

    def cp(out, a):
        return add("v", "cp", (out, a), [out], [a], vcost(out, [a]))

    def tt(out, a, b, op):
        return add("v", "tt", (out, a, b, op), [out], [a, b], vcost(out, [a, b], True))

    def ts(out, a, s1, s2, o0, o1=None):
        return add("v", "ts", (out, a, s1, s2, o0, o1), [out], [a, s1, s2], vcost(out, [a]))

    def ms(out, val):
        return add("v", "ms", (out, val), [out], [], C["v"] + out[4] * cyc * (0.5 if two(out) else 1))

    def scan(out, a, b, init, o0, o1):
        return add("v", "scan", (out, a, b, init, o0, o1), [out], [a, b], vcost(out, [a, b]))

    def red(out, a):
        return add("v", "red", (out, a), [out], [a], C["v"] + a[4] * cyc)

    def act(out, a, f, bias=0.0, scale=1.0, acc=None, more=0.0):
        c = 65 + a[4] * C["g"] * cyc if a[5] is not None else C["a"] + a[4] * cyc
        return add("a", "act", (out, a, f, bias, scale, acc), [out] + ([acc] if acc else []), [a, bias, scale], c + more + (20 if acc else 0))

    def shift(q, out, a, bias, scale=1.0):
        if q == "a":
            return act(out, a, AF.Identity, bias, scale)
        return ts(out, a, bias, None, ALU.add) if scale == 1.0 else ts(out, a, scale, bias, ALU.mult, ALU.add)

    def times(out, a, s):
        if out[0] + str(out[2]) in onA or "all" in onA:
            return act(out, a, AF.Identity, 0.0, s)
        return ts(out, a, s, None, ALU.mult)

    onA = [R(x)[0] + str(R(x)[2]) for x in CFG["onA"]]

    def mm(out, l, r, start=False, stop=False, grp=None):
        c = max(min(64, l[4]), r[4]) * C["pcyc"] * (4 if DT[l[0]] == F32 else 1) + C["p"]
        o = ops[-1]
        if o["kind"] == "mm" and o["w"][0][0] == out[0] and o["grp"] == grp and o["at"] == lvl[1] and o["cost"] + c < CFG["run"] \
                and not (grp and o["start"]):
            o["args"].append((out, l, r, start, stop))
            o["w"].append(out)
            o["r"] += [l, r]
            o["cost"] += c
            return o
        return add("p", "mm", [(out, l, r, start, stop)], [out], [l, r], c, grp=grp, start=start)

    def const(out, name, start=False, stop=False, grp=None):
        j = 128 * CW.index(name)
        return mm(out, R("cw", j, j + 128), R("on5", 0, out[4]), start, stop, grp)

    def iota(out, pat, base, cm):
        return add("g", "iota", (out, pat, base, cm), [out], [], 130 + 2 * out[4] * cyc)

    def dma(q, sem, out, src, nbytes):
        outs = [out] if out[0] in SHAPES else []
        ins = [src] if src[0] in SHAPES else []
        return add(q, "dma", (out, src), outs, ins, 100.0, sem=sem, lat=C["dma"] + nbytes / 200.0)

    def ext(name, a, b):
        return (name, (slice(None), slice(a, b)), a, b, b - a, None)

    def send(kind, t, srcs, dst, li):
        s = add("g", "send", (kind, t, dst) + tuple(srcs), [], srcs, 300.0, sem="lo%d" % li, lat=C["flight"])
        return add("x", "arr", (dst,) + tuple(srcs), [dst], [], 0.0, sem=("ap%d" if kind == "p" else "az%d") % t, lat=0.0, after=s)

    col = lambda name, j: R(name, j, j + 1)
    ONB = R("on5", 0, 128)
    HB = lambda nm, h, o=0: R(nm, o + 128 * h, o + 128 * h + 128)
    dma("s", "ldxc", R("xs"), ext("xc", 0, 1024), 262144)
    dma("a", "ldps", R("pss"), ext("ps", 0, 16), 8192)
    dma("s", "ldzi", R("zis"), ext("zi", 0, 256), 65536)
    dma("a", "ldwt", R("wts", 0, 1), ("wt", (slice(None), slice(None)), 0, 1, 1, None), 4096)
    dma("a", "ldkc", R("KK", 0, 1024), ext("kc", 0, 1024), 262144)
    dma("s", "ldnb", R("nbs"), ext("nb", 0, 1024), 524288)
    iota(R("pci", 0, 1), [[0, 1]], 0, 1)
    iota(R("jrow"), [[1, 256]], 0, 0)
    iota(R("mrow"), [[0, 16], [1, 16]], 0, 0)
    iota(R("grow"), [[1, 8], [0, 16]], 0, 0)
    iota(R("ci"), [[1, 16]], 0, 0)
    PF, RC, GC, PX, CN, CNM, CP2, CPM, CA, G15, WF, U12, AC, AT, WS = [col("cols", j) for j in range(15)]
    tmp = lambda j: col("cols", 16 + j)
    j128, m128 = R("jrow", 0, 128), R("mrow", 0, 128)
    ms(R("on5"), 1.0)
    for name, val in (("p24", M24), ("m24", -M24), ("q", -0.25)) + (("p36", M36), ("m36", -M36), ("pk", 1024.0)) * (CFG["Q"] != "aa"):
        ms(HB("cw", CW.index(name)), val / 128)
    for name, a, b in (("p23", M23 / 2, M23 / 2), ("mk", -512, -512), ("m2o", -M23, -2 * OFF), ("m23", -M23, -OFF / 2)) \
            + (("pq", 2.0 ** 23, 1024.0),) * (CFG["Lw"] != "a"):
        j = 128 * CW.index(name)
        if a == b:
            iota(R("cw", j, j + 128), [[0, 128]], int(a / 64), 0)
        else:
            iota(R("cw", j, j + 128, p=(0, 64)), [[0, 128]], int(a / 64), 0)
            iota(R("cw", j, j + 128, p=(64, 128)), [[0, 128]], int(b / 64), 0)
    act(R("onf"), R("on5", 0, 128), AF.Identity, 0.0, 1.0 / 16)
    ms(R("rst"), 0.0)
    ms(R("rst", 0, 256, 16), -float(2 ** 25))
    ms(R("half"), 0.5)
    ms(R("first"), 0.0)
    ms(R("first", 0, 256, 16), 1.0)
    scan(R("rown"), R("half"), R("first"), 0.0, ALU.mult, ALU.max)
    ms(R("pw2", 16, 32), 2.0)
    scan(R("pw2", 0, 16), R("pw2", 16, 32), R("first", 0, 16), 0.0, ALU.mult, ALU.max)
    cp(PF, col("pci", 0))
    ts(col("tmi", 0), col("pci", 0), 15, None, ALU.bitwise_and)
    ts(col("tmi", 1), col("pci", 0), 4, None, ALU.arith_shift_right)
    ts(col("tmi", 2), col("pci", 0), 1, None, ALU.bitwise_and)
    cp(RC, col("tmi", 0))
    cp(GC, col("tmi", 1))
    ts(tmp(0), col("tmi", 2), -2.0, 1.0, ALU.mult, ALU.add)
    tt(PX, tmp(0), PF, ALU.add)
    cp(R("cidx"), R("ci"))
    ts(R("maskM"), R("mrow"), RC, None, ALU.is_equal)
    ts(R("blk8"), R("jrow", 0, 8), GC, None, ALU.is_equal)
    ts(R("blkM"), R("grow"), GC, None, ALU.is_equal)
    ts(R("Ib"), j128, PF, None, ALU.is_equal)
    act(R("If"), R("Ib"), AF.Copy)
    times(R("I2"), R("Ib"), 2.0)
    for name, s in (("NIf", -1.0),) * (CFG["Q"] != "aa") + (("NIb", -1.0), ("Ih", 0.5), ("NIh", -0.5)):
        act(R(name), R("Ib"), AF.Identity, 0.0, s)
    ts(R("NP2"), j128, PX, -2.0, ALU.is_equal, ALU.mult)
    if any(CFG["scalar"]):
        act(R("PM2"), R("NP2"), AF.Identity, 0.0, -1.0)
    tt(R("pw2", 32, 48), R("rown", 0, 16), R("maskM", 0, 16), ALU.mult)
    red(CN, R("pw2", 32, 48))
    tt(R("pw2", 16, 32), R("pw2", 0, 16), R("maskM", 0, 16), ALU.mult)
    red(CP2, R("pw2", 16, 32))
    ts(CNM, RC, 12.0, CN, ALU.is_lt, ALU.mult)
    ts(CPM, RC, 12.0, CP2, ALU.is_lt, ALU.mult)
    times(R("W19"), R("blk8"), UNIT)
    times(R("pickw"), R("blk8"), CPM)
    ts(R("pickb"), R("jrow", 0, 128, 16), PF, -2 * BIG, ALU.is_equal, ALU.mult)
    ts(R("t1"), j128, PF, CP2, ALU.is_gt, ALU.mult)
    ts(R("t2"), m128, 12.0, 2.0, ALU.is_lt, ALU.mult)
    tt(R("tu"), R("rown", 0, 128), R("t2"), ALU.mult)
    tt(R("t3"), R("blkM"), R("tu"), ALU.mult)
    tt(R("TriN"), R("t1"), R("t3"), ALU.mult)
    tt(R("TriP"), R("I2"), R("TriN"), ALU.subtract)
    act(tmp(12), RC, AF.Sigmoid, 256 * 11.5, -256.0, more=1300.0)
    ts(U12, tmp(12), 0.5, None, ALU.is_gt)
    ts(tmp(6), RC, 12.0, None, ALU.is_equal)
    ts(tmp(7), RC, 13.0, -EPS, ALU.is_equal, ALU.mult)
    tt(tmp(1), tmp(6), tmp(7), ALU.add)
    ts(CA, tmp(6), 0.5, tmp(1), ALU.mult, ALU.subtract)
    times(R("C30"), R("blkM"), tmp(1))
    times(R("C80"), R("blkM"), CA)

    def code(bank, a, x, prow, nrow, c3, c8, whole=False):
        o = R(bank, a, a + x[4])
        for tri, d, c in (("TriN", "D", c3), ("TriP", "ND", c8)):
            mm(o, R(tri), x, tri == "TriN")
            if prow:
                mm(o, R(d), prow)
            mm(o, R(c), nrow or R("on5", 0, x[4]), False, tri == "TriP" and not whole)
            if tri == "TriN":
                const(o, "p24")
                const(o, "m24")
        if whole:
            const(o, "p23")
            const(o, "m2o", False, True)
        return o

    for q in range(2):
        o = code(("KE", "K0")[q], 0, R("xs", 512 * q, 512 * q + 512), None, None, "C30", "C80")
        ts(R("P", 512 * q, 512 * q + 512), o, M23, -M23, ALU.add, ALU.add)
    times(R("D"), R("Ib"), CNM)
    act(R("ND"), R("D"), AF.Identity, 0.0, -1.0)
    ms(R("t4"), 0.0)
    ms(R("t4", 10, 128, 16), 1.0)
    ms(R("t4", 11, 128, 16), 0.5)
    times(R("t5"), R("blkM"), tmp(6))
    tt(R("t6"), R("t5"), R("t4"), ALU.mult)
    tt(R("C3"), R("C30"), R("t6"), ALU.subtract)
    tt(R("C8"), R("C80"), R("t6"), ALU.add)
    tt(R("N3"), R("C3"), R("D"), ALU.subtract)
    tt(R("N8"), R("C8"), R("D"), ALU.add)
    ts(R("pw2", 16, 24), R("jrow", 0, 8), 256.0, -1.0, ALU.mult, ALU.add)
    ts(R("nbias"), R("pw2", 16, 24), U12, 1.0, ALU.mult, ALU.add)
    ts(tmp(2), RC, 15.0, CN, ALU.is_lt, ALU.mult)
    times(R("Boff"), R("blkM"), 2.0 ** 26)
    times(R("Bdia"), R("Boff"), tmp(2))
    ms(R3("mk", 0, 16, 16), 0.0)
    ts(R3("mk", 0, 16, 0, 16), R("mrow"), RC, -2.0 ** 34, ALU.not_equal, ALU.mult)
    act(R("NblkM"), R("blkM"), AF.Identity, 0.0, -1.0)
    for j in range(2):
        ms(R3("pr%d" % j, 0, 16, 16), -2000.0)
    ms(R3("th2", 0, 16, 16), 0.0)
    ts(R3("th2", 0, 16, 0, 16, p=(0, 64)), R("rown", p=(0, 64)), -2.0 ** 21, None, ALU.mult)
    ms(R3("th2", 0, 16, 0, 16, p=(64, 128)), 32.0)
    iota(R("d0"), [[0, 272]], 4096, 0)
    ms(R("d0", 0, 272, 17), -4096.0)
    ts(R("pw2", 32, 48), R("jrow", 0, 16), 16.0, float(W - V0), ALU.mult, ALU.add)
    ts(R("d0", 16, 272, 17), R("pw2", 32, 48), RC, None, ALU.add)
    ts(R("ncol"), R("jrow", 0, 16), 128.0, PF, ALU.mult, ALU.add)
    ts(G15, GC, 16.0, 15.0, ALU.mult, ALU.add)
    cp(WF, col("wts", 0))
    if CFG["usc"]:
        ts(R("Wz", 0, 128), R("blkM"), WF, None, ALU.mult)
    else:
        ts(R("Wz"), R("jrow", 0, 144), G15, WF, ALU.is_equal, ALU.mult)
    ts(col("tmi", 3), col("pci", 0), 2, 3, ALU.arith_shift_right, ALU.bitwise_and)
    ts(tmp(3), col("tmi", 3), -4.0, PF, ALU.mult, ALU.add)
    ts(tmp(4), tmp(3), 12.0, None, ALU.add)
    cp(tmp(5), col("tmi", 3))
    ts(R("cols", 24, 28), R("jrow", 0, 4), tmp(5), None, ALU.is_equal)
    for q in range(4):
        ts(R("Zq", 144 * q, 144 * q + 144), R("jrow", 0, 144), tmp(4), col("cols", 24 + q), ALU.is_equal, ALU.mult)
    ms(R("Zb"), 0.0)
    act(R("I4"), R("Ib"), AF.Copy)
    iota(R("ki", p=(0, 64)), [[-128, 2], [0, 16], [-256, 16]], 31 * 128, 0)
    iota(R("ki", p=(64, 128)), [[0, 512]], -23 * 4096, 0)
    act(R("N13"), R("Ib"), AF.Identity, 0.0, -8192.0)
    act(R("P13"), R("Ib"), AF.Identity, 0.0, 8192.0)
    if CFG["fuse"]:
        act(R("K32", 0, 1024), R("KK", 0, 1024), AF.Identity, OFF)
        for j in range(2):
            act(R("K32", 1024 + j, 2048, 2), R("KK", 1 - j, 1024, 2), AF.Identity, OFF)
    else:
        for j in range(2):
            act(R("KK", 1024 + j, 2048, 2), R("KK", 1 - j, 1024, 2), AF.Copy)
    ts(tmp(13), col("wts", 0), -0.5, None, ALU.mult)
    times(R("t7"), R("blkM"), tmp(13))
    mm(col("X2", 20), R("t7"), R("on5", 0, 1), True, True)
    cp(WS, col("X2", 20))

    def cut_numbers(t, Z):
        U = R("X2", 32, 48)
        if CFG["usc"]:
            mm(R("X2", 0, 256), R("Wz", 0, 128), Z, True)
            mm(R("X2", 0, 256), R("Ib"), R3("mk", 0, 16, 0, 16), False, True)
            scan(R("sc", 0, 256), R("rst"), R("X2", 0, 256), 0.0, ALU.add, ALU.max)
            U = R("sc", 15, 256, 16)
        for r in range(0 if CFG["usc"] else 16):
            mm(U, R("Wz", 15 - r, 143 - r), R(Z[0], Z[2] + r, Z[3], 16), r == 0, r == 15)
        if t == 0:
            cp(R("ui"), U)
        else:
            ts(R("ui"), U, AT, None, ALU.add)
        ts(R("um"), R("ui"), V0 - 1, None, ALU.bitwise_and)
        cp(R("u16"), R("um"))
        for j in range(0 if CFG["fuse"] else 2):
            act(R("KU", 256 * j, 256 * j + 256), IND(R("KK", 1024 * j, 1024 * j + 1024), R("u16")), AF.Identity, OFF)

    tt(R("bm"), IND(R("pss"), R("cidx")), R("maskM"), ALU.mult)
    for h in range(2):
        mm(R("K1", 8 * h, 8 * h + 8), HB("bm", h), R("blk8"), True, True)
    ts(R("pT0"), R("K1", 0, 16), -float(V0), None, ALU.add)
    cut_numbers(0, R("zis"))
    slot = {"v": 0, "a": 0, "s": 0}
    DD = R("X1", 0, 272)
    S16 = lambda nm, a=0, b=16: R3(nm, a, b, 0, 16)

    for t in range(RO):
        last = t == RO - 1
        SC = CFG["scalar"][1 if last else 0]
        pT = R("pT0") if t == 0 else R("lp", 16 * (t - 1), 16 * t)
        Z = R("zis") if t == 0 else R("lz", 256 * (t - 1), 256 * t)
        bc, pr, ac, CE, so = [n + str(t % 2) for n in ("bc", "pr", "act", "CE", "so")]
        n0 = V0 + M * t
        nrow = R("nrow", M * t, M * t + M)
        at(t, "pre")
        act(nrow, R("jrow"), AF.Identity, col("nbias", t), U12)
        gd = ("d", t)
        mm(DD, R("Ib"), R("mk"), True, grp=gd)
        mm(DD, ONB, R("th2"), grp=gd)
        at(t, "in")
        if t == 0:
            mm(R("X2", 0, 256), R("blkM"), R("bm"), True, True)
            act(S16(pr), R("X2", 0, 256), AF.Identity, -float(V0))
            cp(R("pw16"), R("pss"))
            ts(R("pwf"), R("pss"), -float(V0), None, ALU.add)
            ts(R("pwh"), R("pss"), -float(V0), None, ALU.add)
            mm(R("X1", 16, 272, 17), R("Ib"), R("pwh"), grp=gd)
            at(t, "key")
            act(R(bc), IND(pT, R("cidx")), AF.Copy)
        else:
            tt(R("bm"), IND(pT, R("cidx")), R("maskM"), ALU.mult)
            act(R(bc), IND(pT, R("cidx")), AF.Copy)
            for h in range(2):
                mm(R("X0", 256 + 8 * h, 264 + 8 * h), HB("bm", h), R("blk8"), True, True)
            for h in range(2):
                mm(HB("X2", h), HB(bc, h), R("Ib"), True, True)
            ts(R("pw16"), R("X0", 256, 272), float(V0), None, ALU.add)
            cp(R("pwf"), R("X0", 256, 272))
            cp(S16(pr), R("X2", 0, 256)) if CFG["pr"] == "v" else act(S16(pr), R("X2", 0, 256), AF.Copy)
            for h in range(2):
                mm(R("X1", 136 * h + 16, 136 * h + 136, 17), HB("bm", h), R("blk8"), grp=gd)
        at(t, "eq")
        for c in range(16):
            ts(EQ(c, 0, 272 - 17 * c), R(pr, 17 * c, 272), col("pwf", c), None, ALU.is_equal)
            if c < 15:
                mm(R("X1", 17 * c + 17, 272), R("Boff"), EQ(c, 17, 272 - 17 * c), grp=gd)
        mm(DD, R("Bdia"), R3("eq", 0, 16, 0, 17), grp=gd)
        scan(R("sc"), R("d0"), DD, 0.0, ALU.min, ALU.max)
        ts(R(so), R("sc", 16, 272, 17), float(V0), None, ALU.add)
        act(R("idle"), DD, AF.Sigmoid)
        AP = R("X1", 0, 256)
        mm(AP, R("Ib"), R("on5", 0, 256), True)
        mm(AP, R("NblkM"), S16("idle"), False, True)
        at(t, "cd")
        act(R("xp"), IND(R("P", 0, n0), R("pw16")), AF.Identity, OFF - 0.25, 0.5)
        for ch in range(2):
            k = IND(R("K32", 1024 * ch, 1024 * ch + 1024), R("u16")) if CFG["fuse"] else R("KU", 256 * ch, 256 * ch + 256)
            tt(R(CE, 256 * ch, 256 * ch + 256), k, R("xp"), ALU.min)
        o = code("X2", 0, R(CE, 0, 256), S16(pr), nrow, "N3", "N8", CFG["Cb"] == "a")
        if CFG["Cb"] == "a":
            act(R("Cb", 0, 256), o, AF.Copy)
        else:
            ts(R("Cb", 0, 256), o, M23, -M23 - 2 * OFF, ALU.add, ALU.add)
        cp(IND(R("P"), R(so)), R("Cb", 0, 256))
        at(t, "ce")
        o = code("X2", 256, R(CE, 256, 512), None, None, "C3", "C8", CFG["Eb"] == "p")
        if CFG["Eb"] == "p":
            act(R(ac), AP, AF.Copy, acc=None if last else AC)
            tt(R("P", n0, n0 + M), o, R(ac), ALU.mult)
        else:
            ts(R("Cb", 256, 512), o, M23, -M23 - 2 * OFF, ALU.add, ALU.add)
            tt(R("P", n0, n0 + M), R("Cb", 256, 512), AP, ALU.mult)
            act(R(ac), AP, AF.Copy, acc=None if last else AC)

        def thresholds(ch):
            at(t, ("tb", "te")[ch])
            S, x = ("K0", "KE")[ch], R("thr", 512 * ch, 512 * ch + 512)
            for j in range(2):
                mm(RS(S, 0, 128, 1, j, 4, 2), R("NP2"), R(CE, 256 * ch, 256 * ch + 256), True, True)
            shift(CFG["TB"][ch], x, R(S), 2 * OFF)
            for j in range(2):
                o = R3(("TBC", "TBE")[ch], 0, 256, 2 * j, 2 * j + 2)
                cp(o, x) if CFG["TB"][2 + ch] == "v" else act(o, x, AF.Copy)

        thresholds(0)
        thresholds(1)
        at(t, "a")
        if t == 0:
            ts(R("aF"), IND(R("nbs"), R("pw16")), -float(V0), None, ALU.add)
        else:
            act(R("aF"), IND(R("L", 0, n0), R("pw16")), AF.Identity, -float(V0))
        for q in range(4):
            for j in range(4):
                x = 144 * q + 12 - 4 * j
                mm(R("K1", 64 * q, 64 * q + 64), R("Zq", x, x + 128), R("aF", j, 256, 4), j == 0, j == 3)
            if q in CFG["acut"]:
                x = 64 * (max([-1] + [y for y in CFG["acut"] if y < q]) + 1)
                shift(CFG["o16"][0], R("a16", x, 64 * q + 64), R("K1", x, 64 * q + 64), float(V0))
        at(t, "key")
        if not last:
            ts(R("al1"), pT, V0 + 1.0 + BIG, None, ALU.add)
            ts(R("al2"), R("al1"), int(BIG) + V0 - 1, None, ALU.bitwise_and)
            const(R("X2", 0, 16), "mk", True)
            for h in range(2):
                mm(R("X2", 8 * h, 8 * h + 8), HB(ac, h), R("pickb"), False, h == 1)
            mm(col("X2", 16), R("onf"), AC, True, True)
            tt(R("kyo"), R("X2", 0, 16), R("al2"), ALU.add)
            ts(AT, col("X2", 16), WS, None, ALU.add)
        KEY = lambda ch, s, h: HB("K%d" % h, s) if ch == 0 else HB("KE", 2 * s + h)
        GRP = lambda ch, h: ("K%d" % h if ch == 0 else "KE", t)
        for h in range(2):
            mm(R("K%d" % h, 0, 256), ONB, R3("ki", 0, 2, 0, 128), True, grp=GRP(0, h))
            mm(KEY(0, 0, h), HB("aF", h), R("Ib"), grp=GRP(0, h))
        at(t, "ke")
        mm(R("KE"), ONB, R("ki"), True, grp=GRP(1, 0))
        for s in range(2):
            if CFG["relu"]:
                mm(R("KE", 256 * s, 256 * s + 256), R("NIb"), R(bc), grp=GRP(1, 0))
            mm(KEY(1, 0, s), HB("aF", s), R("Ib"), grp=GRP(1, 0))
        at(t, "x" if last else "z")
        if not last:
            o, dm = R("X2", 256, 512), R("dm", 256 * t, 256 * t + 256)
            mm(o, R("Ih"), R(CE, 0, 256), True)
            mm(o, R("NIh"), Z)
            if t == 0:
                const(o, "q")
            const(o, "p23")
            const(o, "m23", False, True)
            tt(dm, o, R(ac), ALU.mult)
            send("z", t, [Z, dm] + [R("half")] * (t == 0), R("lz", 256 * t, 256 * t + 256), 2 * t)
        else:
            for q, (a, b) in enumerate(((0, 1024), (1024, W))):
                for a1 in range(a, b, 512):
                    shift(CFG["xo"][0], R("X16", a1, a1 + 512), R("P", a1, a1 + 512), OFF - 0.25, 0.5)
                    shift(CFG["xo"][1], R("Xo", a1, a1 + 512), R("X16", a1, a1 + 512), -OFF)
                dma("s", "stx%d" % q, ext("yx", a, b), R("Xo", a, b), 128 * 2 * (b - a))
        if t == 0:
            at(t, "key")
            for q in range(2):
                cp(R("L", 512 * q, 512 * q + 512), R("nbs", 512 * q, 512 * q + 512))

        def gather(s):
            at(t, "g")
            for s1, i0, i1, q in CFG["gather"][1 if last else 0]:
                if s1 == s:
                    o = R(("Ga", "Gb")[s], 16 * i0, 16 * i1)
                    src = IND(R("P", 0, n0 + M * s), R(("a16", "b16")[s], i0, i1))
                    cp(o, src) if q == "v" else act(o, src, AF.Copy)

        FOUR = lambda key, q, *kk: RS(key[0], key[2] // 4 + q, key[3] // 4, 4, *kk)

        def siblings(qs, X):
            at(t, "sib")
            q0, n = qs[0], 64 * len(qs)
            S, B, Rb = R(X, 0, n), R(X, 256, 256 + n), R("Rb", 64 * q0, 64 * q0 + n)
            for q in qs:
                for h in range(2):
                    y = 64 * (q - q0) + 32 * h
                    mm(R(X, y, y + 32), HB("aF", h), RS("I4", q, 32, 4, 0, 4), True)
                    for kk in range(4):
                        x = 1024 * q + 512 * h
                        mm(R(X, y + kk, y + 32, 4), R("Ga", x + kk, x + 512, 4), R("pickw"), False, kk == 3)
            ts(Rb, S, M35, -M35, ALU.add, ALU.add)
            tt(RS("Zb", 64 * q0 + 3, 64 * q0 + 3 + n, 4, 0, 4), S, Rb, ALU.subtract)
            for y in range(0, n, 32):
                for j in range(4):
                    x = 64 * q0 + 3 + y - j
                    mm(R(X, 256 + y, 288 + y), R("Zb", 4 * x, 4 * x + 128), R("Ib", j, 128, 4), j == 0, j == 3)
            shift(CFG["o16"][1], R("b16", 64 * q0, 64 * q0 + n), B, float(V0))
            for q in qs:
                z = 64 * q + 3
                at(t, "c")
                for h in range(2):
                    mm(FOUR(KEY(0, 1, h), q, 0, 4), R("Ib"), RS("Zb", z + 32 * h, z + 32 * h + 32, 4, 0, 4), grp=GRP(0, h))
                at(t, "ke")
                mm(FOUR(R("KE", 256, 512), q, 0, 4), R("Ib"), RS("Zb", z, z + 64, 4, 0, 4), grp=GRP(1, 0))

        def tiles(ch, s, q, hs):
            G, TB = ("Ga", "Gb")[s], ("TBC", "TBE")[ch]
            mine = [h for h in hs if not (ch and (s, h, q) in SC)]
            for h in hs:
                if h not in mine:
                    at(t, "e")
                    S = ("X0", "X2")[slot["s"] % 2]
                    slot["s"] += 1
                    j = 512 * (slot["a"] % NA)
                    slot["a"] += 1
                    mm(R(S), R("Ib"), R(G, 1024 * q + 512 * h, 1024 * q + 512 * h + 512), True)
                    for kk in range(4):
                        mm(R(S, kk, 512, 4), R("PM2"), HB(CE, h, 256 * ch), False, kk == 3)
                    act(R("ia", j, j + 512), R(S), AF.Sigmoid, 256 * (0.5 - 2 * OFF), 256.0)
                    for kk in range(4):
                        mm(FOUR(KEY(ch, s, h), q, kk), R("ia", j + kk, j + 512, 4), R("W19"), grp=GRP(ch, h))
            if mine:
                at(t, ("c", "ev")[ch])
                slot["v"] += slot["v"] % len(mine)
                j, n = 128 * (slot["v"] % NV), 128 * len(mine)
                slot["v"] += len(mine)
                x = 1024 * q + 512 * mine[0]
                tt(R3("iv", j, j + n, 0, 4), R(G, x, x + 4 * n), R3(TB, 128 * mine[0], 128 * mine[0] + n, 0, 4), ALU.is_ge)
                for x, h in enumerate(mine):
                    for kk in range(4):
                        mm(FOUR(KEY(ch, s, h), q, kk), R3("iv", j + 128 * x, j + 128 * x + 128, kk), R("W19"), grp=GRP(ch, h))

        def all_tiles(ch, s):
            for q in range(4):
                for hs in ([(0,), (1,)] if (ch, s, q) in CFG["split"] else [(0, 1)]):
                    tiles(ch, s, q, hs)

        def back(o, m, more, q=None):
            if q:
                mm(o, q, R("N13"), True)
            else:
                mm(o, m, R("NIf"), True)
                const(o, "p36")
                const(o, "m36")
            mm(o, m, R("If"), False, not more)
            for x, (l, r) in enumerate(more):
                mm(o, l, r, False, x == len(more) - 1)

        gather(0)
        for x, qs in enumerate(CFG["sibs"]):
            siblings(qs, "X%d" % (x % 2))
        all_tiles(0, 0)
        gather(1)
        all_tiles(0, 1)
        at(t, "out")
        for h in range(2):
            ts(HB("m1C", h), KEY(0, 0, h), col("ncol", 2 * t + h), None, ALU.max)
            tt(HB("m2C", h), KEY(0, 1, h), HB("m1C", h), ALU.max)
            if not last:
                scan(HB("wsc", h), R("rst", 0, 128), HB("m2C", h), 0.0, ALU.add, ALU.max)
        if not last:
            tt(R("px"), R("wsc", 15, 256, 16), R("kyo"), ALU.max)
            ts(R("pq"), R("px"), M36, -M36, ALU.add, ALU.add)
            tt(R("sp", 16 * t, 16 * t + 16), R("px"), R("pq"), ALU.subtract)
            send("p", t, [R("sp", 16 * t, 16 * t + 16)], R("lp", 16 * t, 16 * t + 16), 2 * t + 1)
            at(t, "u")
            cut_numbers(t + 1, R("lz", 256 * t, 256 * t + 256))
        at(t, "lc")
        for h in range(2):
            q = CFG["Q"][0] == "a"
            if q:
                act(HB("QC", h), HB("m2C", h), AF.Identity, 1024.0, 1.0 / 8192)
            back(HB("K%d" % h, 2), HB("m2C", h), [], q and HB("QC", h))
            act(HB("entC", h), HB("K%d" % h, 2), AF.Identity, V0 + q * 2.0 ** 23)
        cp(IND(R("L"), R(so)), R("entC"))
        if last:
            dma("s", "stn0", ext("yn", 0, 1152), R("L", 0, 1152), 128 * 4 * 1152)
            dma("a", "stn1", ext("yn", 1152, n0), R("L", 1152, n0), 128 * 4 * 1152)
        all_tiles(1, 0)
        all_tiles(1, 1)
        at(t, "le")
        act(R("m1E"), R("KE", 0, 256), AF.Relu) if CFG["relu"] else tt(R("m1E"), R("KE", 0, 256), R(bc), ALU.max)
        tt(R("m2E"), R("KE", 256, 512), R("m1E"), ALU.max)
        q = CFG["Q"][1] == "a"
        if q:
            act(R("QE"), R("m2E"), AF.Identity, 1024.0, 1.0 / 8192)
        for h in range(2):
            j = 128 * CW.index("pq" if q else "pk")
            back(HB("KE", h), HB("m2E", h), [(R("Ib"), S16(pr, 8 * h, 8 * h + 8))] * CFG["relu"]
                 + [(R("P13"), HB(ac, h)) if CFG["Lw"] == "a" else (R("cw", j, j + 128), ONB)], q and HB("QE", h))
        if CFG["Lw"] == "a":
            act(R("L", n0, n0 + M), R("KE", 0, 256), AF.Relu, V0 + q * 2.0 ** 23 - 8192.0)
        else:
            tt(R("L", n0, n0 + M), R("KE", 0, 256), R(ac), ALU.mult)
        if last:
            dma("s", "stn2", ext("yn", n0, W), R("L", n0, W), 128 * 4 * M)
    return ops


def depend(ops):
    acc = {}
    bank = {}
    for o in ops:
        dep, follow = set(), set()
        if "after" in o:
            follow.add(o["after"]["n"])
        for rs, wr in ((o["r"], False), (o["w"], True)):
            for r in rs:
                if r[0] in PS:
                    b = bank.setdefault(r[0], {"eng": None, "cur": [], "prev": []})
                    if b["eng"] != o["eng"]:
                        b["eng"], b["prev"], b["cur"] = o["eng"], b["cur"], []
                    dep.update(b["prev"])
                    if o["eng"] == "p":
                        for m in b["cur"]:
                            q = ops[m]
                            if o["grp"] is None or q["grp"] != o["grp"] or q["start"]:
                                follow.add(m)
                    if o["n"] not in b["cur"]:
                        b["cur"].append(o["n"])
                    if o["eng"] == "p":
                        continue
                keep = []
                full = wr and r[5] is None and r[4] == r[3] - r[2] and r[1][0] == slice(None)
                for (lo, hi, w, m) in acc.get(r[0], []):
                    if lo < r[3] and r[2] < hi and (w or wr) and m != o["n"]:
                        dep.add(m)
                    if not (full and r[2] <= lo and hi <= r[3]):
                        keep.append((lo, hi, w, m))
                keep.append((r[2], r[3], wr, o["n"]))
                acc[r[0]] = keep
        dep.discard(o["n"])
        follow.discard(o["n"])
        o["dep"], o["follow"] = dep, follow - dep


def place(ops, seq, before):
    start = [0.0] * len(ops)
    line = {e: ([], []) for e in "vapgs"}
    for i in seq:
        e, c = ops[i]
        t = 0.0
        for m, d in before[i]:
            d += start[m]
            if d > t:
                t = d
        if e != "x":
            a, b = line[e]
            lo = n = len(b)
            while lo and b[lo - 1] > t:
                lo -= 1
            while lo < n and a[lo] < t + c - 1e-6:
                if b[lo] > t:
                    t = b[lo]
                lo += 1
            a.insert(lo, t)
            b.insert(lo, t + c)
        start[i] = t
    return start


def improve(ops):
    n = len(ops)
    fwd = [[] for _ in ops]
    bwd = [[] for _ in ops]
    for o in ops:
        i = o["n"]
        for m in o["dep"] | o["follow"]:
            q = ops[m]
            d = q["cost"] + (0.0 if m in o["follow"] and q["eng"] == o["eng"] else q.get("lat", 0.0) + C["hop"])
            fwd[i].append((m, d))
            bwd[m].append((i, o["cost"] - q["cost"] + d))
    tail = n
    left = [len(f) for f in fwd]
    pool = [i for i in range(n) if not left[i]]
    seq = []
    while pool:
        i = min(pool, key=lambda i: (ops[i]["lvl"], i))
        pool.remove(i)
        seq.append(i)
        for m, d in bwd[i]:
            left[m] -= 1
            if not left[m]:
                pool.append(m)
    if CFG.get("path"):
        way = [0.0] * n
        for i in reversed(range(n)):
            way[i] = max([way[m] + d - ops[m]["cost"] + ops[i]["cost"] for m, d in bwd[i]] + [ops[i]["cost"] + ops[i].get("lat", 0.0)])
        seq = sorted(range(n), key=lambda i: (-way[i], i))
    ec = [(o["eng"], o["cost"]) for o in ops]
    ends = [(o["n"], o["cost"] + o.get("lat", 0.0)) for o in ops if o["kind"] == "dma"]
    start = place(ec, seq, fwd)
    finish = lambda st: max(st[i] + d for i, d in ends)
    best = (finish(start), start)
    for o in ops:
        bwd[o["n"]].append((tail, o.get("lat", 0.0)))
    ext = ec + [("x", 0.0)]

    def there_and_back(st):
        rev = place(ext, [tail] + sorted(range(n), key=lambda i: (-(st[i] + ec[i][1]), -i)), bwd + [[]])
        return place(ec, sorted(range(n), key=lambda i: (-(rev[i] + ec[i][1]), i)), fwd)

    for _ in range(CFG["passes"]):
        start = there_and_back(start)
        if finish(start) < best[0]:
            best = (finish(start), start)
    seen, like, kinds = {}, [], {}
    for o in ops:
        t, name = o["at"]
        k = (name, o["eng"], o["w"][0][0].rstrip("01") if o["w"] else o["kind"])
        seen[t, k] = seen.get((t, k), 0) + 1
        like.append(k + (seen[t, k],))
        if like[-1] not in kinds.setdefault(k, []):
            kinds[k].append(like[-1])
    arr = [i for i in range(n) if ops[i]["kind"] == "arr" and ops[i]["sem"][:2] == "ap"]
    span = best[1][arr[2]] - best[1][arr[1]]
    off = {}
    for t in (2, 0, RO - 1):
        zero = best[1][arr[t - 1]] if t else best[1][arr[0]] - span
        for i in range(n):
            if ops[i]["at"][0] == t and like[i] not in off:
                off[like[i]] = best[1][i] - zero
    if CFG["when"]:
        span = CFG["span"]
        for k, (a, step) in CFG["when"].items():
            for x in kinds.get(k, []):
                off[x] = a + step * (x[3] - 1)
        for i in range(n):
            if ops[i]["at"][1] == "start":
                off[like[i]] = best[1][i] - CFG["lead"]
    pre = [[m for m, d in f] for f in fwd]
    wide, steps = [span], {}
    for k in sorted(off):
        steps.setdefault(k[0], []).append(k)
        steps.setdefault(k[:2], []).append(k)

    def lay(off):
        key = [ops[i]["at"][0] * wide[0] + off[like[i]] for i in range(n)]
        for i in range(n):
            for m in pre[i]:
                if key[m] >= key[i]:
                    key[i] = key[m] + 1e-3
        st = place(ec, sorted(range(n), key=lambda i: key[i]), fwd)
        return finish(st), st

    def blocked(st):
        stop = {}
        for i in range(n):
            stop[ec[i][0], round(st[i] + ec[i][1])] = i
        i = max(ends, key=lambda x: st[x[0]] + x[1])[0]
        pairs = []
        while st[i] > 1.0:
            m, d = max(fwd[i] + [(i, -1e9)], key=lambda x: st[x[0]] + x[1])
            if st[m] + d < st[i] - 1.0:
                m = stop.get((ec[i][0], round(st[i])))
                if m is None:
                    break
                if like[m] != like[i]:
                    pairs.append((m, i))
            i = m
        return pairs

    held = [None, None]
    names = sorted(kinds)
    now = lay(off)
    if CFG["when"]:
        best = now
    x = CFG["seed"]
    for it in range(CFG["tries"]):
        x = (x * 1103515245 + 12345) % 2 ** 31
        shift = (150.0, 400.0, 900.0, 2000.0, 4000.0)[(x >> 8) % 5] * (1 - 2 * ((x >> 20) % 2))
        members = kinds[names[(x >> 12) % len(names)]]
        x = (x * 1103515245 + 12345) % 2 ** 31
        a = (x >> 10) % len(members)
        members = (members, members[a:], members[:a + 1], members[a:a + 1], steps[members[0][0]], steps[members[0][:2]])[(x >> 20) % 6]
        if (x >> 24) % 4 < CFG["aim"]:
            if held[0] is not now:
                held[:] = [now, blocked(now[1])]
            if held[1]:
                m, i = held[1][(x >> 9) % len(held[1])]
                gap = ops[i]["at"][0] * wide[0] + off[like[i]] - ops[m]["at"][0] * wide[0] - off[like[m]]
                members, shift = (([like[i]], -gap - 1.0), ([like[m]], gap + 1.0))[(x >> 7) % 2]
                if (x >> 6) % 2:
                    members = [k for k in kinds[members[0][:3]] if (k[3] - members[0][3]) * shift >= 0]
        if it % CFG["again"] == CFG["again"] - 1:
            old, zero = dict(off), now[1][arr[1]]
            for i in range(n):
                if ops[i]["at"][0] == 2:
                    off[like[i]] = now[1][i] - zero
            wide[0], was = now[1][arr[2]] - zero, wide[0]
            new = lay(off)
            if new[0] <= now[0] + CFG["slack"]:
                now = new
            else:
                off.update(old)
                wide[0] = was
        for k in members:
            off[k] += shift
        new = lay(off)
        if new[0] <= now[0] + CFG["slack"] * (1 - it / CFG["tries"]) * ((x >> 5) % 32) / 32:
            now = new
            if new[0] < best[0]:
                best = new
        else:
            for k in members:
                off[k] -= shift
    for _ in range(2):
        start = there_and_back(best[1])
        if finish(start) < best[0]:
            best = (finish(start), start)
    end, start = best
    for o in ops:
        o["t0"] = start[o["n"]]
    return sorted(range(n), key=lambda i: (start[i], i)), end


def plan():
    ops = build()
    depend(ops)
    order, end = improve(ops)
    lastg = {}
    for i in order:
        if ops[i].get("grp") is not None:
            lastg[ops[i]["grp"]] = i
    for gr, i in lastg.items():
        ops[i]["args"][-1] = ops[i]["args"][-1][:4] + (True,)
    pos, cnt, known = {}, {}, {e: {} for e in "vapgsx"}
    for i in order:
        o = ops[i]
        e = o["eng"]
        kn = known[e]
        need = {}
        if o["kind"] == "iota":
            if lastg.get("g") is not None:
                o["dep"].add(lastg["g"])
            lastg["g"] = i
        for m in o["dep"]:
            src, p = pos[m]
            if kn.get(src, 0) < p and need.get(src, (0, 0))[0] < p:
                need[src] = (p, m)
        waits = []
        for src, (p, m) in sorted(need.items(), key=lambda kv: -ops[kv[1][1]]["t0"]):
            if kn.get(src, 0) >= p:
                continue
            waits.append(m)
            ops[m]["mark"] = True
            for s2, p2 in ops[m]["clock"].items():
                if kn.get(s2, 0) < p2:
                    kn[s2] = p2
        o["waits"] = waits[::-1]
        src = o.get("sem") or ESEM[e]
        cnt[src] = cnt.get(src, 0) + 1
        pos[i] = (src, cnt[src])
        o["src"] = src
        o["clock"] = dict(kn) if e != "x" else {}
        o["clock"][src] = cnt[src]
    val = {}
    for i in order:
        o = ops[i]
        if "sem" not in o and o.get("mark"):
            val[o["src"]] = val.get(o["src"], 0) + 1
            o["val"] = val[o["src"]]
    return ops, order, val, end


PLAN = []


def rank_program(g, core, T, topo):
    rank = T.rank_of(core)
    if rank is None:
        return
    if not PLAN:
        PLAN.append(plan())
    ops, order, val, _ = PLAN[0]
    nxt = T.cores[(rank + STEP) % NR]
    prv = T.cores[(rank - STEP) % NR]
    rid, pid, _ = topo.addr(nxt)
    n_out, n_in = len(topo.engines(core, nxt)), len(topo.engines(prv, core))
    Q = {"v": g.vector, "a": g.scalar, "p": g.tensor, "g": g, "s": g.sync}
    count = lambda o: {"dma": 16, "send": n_out, "arr": n_in}.get(o["kind"]) or o["val"]
    for i in order:
        o = ops[i]
        k = o["kind"]
        if k == "arr":
            continue
        q = Q[o["eng"]]
        for m in o["waits"]:
            q.wait_ge(T.sem[ops[m]["src"]], count(ops[m]))
        a = [ap(T, x) for x in o["args"]] if k != "mm" else None
        if k == "cp":
            ins = q.tensor_copy(a[0], a[1])
        elif k == "tt":
            ins = q.tensor_tensor(a[0], a[1], a[2], a[3])
        elif k == "ts":
            ins = q.tensor_scalar(a[0], a[1], a[2], None, a[4]) if a[5] is None else q.tensor_scalar(*a)
        elif k == "ms":
            ins = q.memset(a[0], a[1])
        elif k == "scan":
            ins = q.tensor_tensor_scan(*a)
        elif k == "red":
            ins = q.tensor_reduce(a[0], a[1], AxisListType.X, ALU.add)
        elif k == "act":
            ins = q.activation(a[0], a[1], a[2], bias=a[3], scale=a[4], accum_out=a[5])
        elif k == "mm":
            for x in o["args"]:
                ins = q.matmul(*[ap(T, y) for y in x])
        elif k == "iota":
            if DT[o["args"][0][0]] == I32:
                ins = q.iota(*a)
            else:
                ins = q.iota(a[0], a[1], a[2], a[3], allow_small_or_imprecise_dtypes=True)
        elif k == "dma":
            q.dma_start(a[0], a[1]).then_inc(T.sem[o["sem"]], 16)
            continue
        else:
            there = T.sem[("ap%d" if a[0] == "p" else "az%d") % a[1]]
            if len(a) == 4:
                q.remote_dma(a[2], a[3], there, T.sem[o["sem"]], pid, rid, topo.mask(core, nxt))
            else:
                x = RemoteDMATransfer(dst_ids=[DstId(rid=rid, pnc=pid)], dma_engine_mask=topo.mask(core, nxt), remote_sem=there,
                                      srcs=a[3:], dsts=[a[2]], alu_op=1)
                q.remote_dma_fused([x], local_sem=T.sem[o["sem"]])
            continue
        if o.get("mark"):
            ins.then_inc(T.sem[o["src"]], 1)
    for i in order:
        o = ops[i]
        if o["kind"] in ("dma", "send", "arr"):
            g.wait_ge(T.sem[o["sem"]], count(o))
    for s, c in val.items():
        g.wait_ge(T.sem[s], c)
